import numpy as np
import ml_dtypes


def mxq(x, axis, fmt="e4m3"):
    dtype, down = {"e4m3": (ml_dtypes.float8_e4m3fn, 7), "e5m2": (ml_dtypes.float8_e5m2, 14)}[fmt]
    v = np.moveaxis(np.asarray(x, np.float32).astype(ml_dtypes.bfloat16).astype(np.float64), axis, -1)
    blocks = v.reshape(v.shape[:-1] + (-1, 32))
    amax = np.abs(blocks).max(-1, keepdims=True)
    byte = np.maximum(np.where(amax > 0, np.frexp(amax)[1] - 1 + 127, 0) - down, 1)
    scale = np.exp2(byte - 127.0)
    codes = (blocks / scale).astype(np.float32).astype(dtype).astype(np.float64)
    return np.moveaxis((codes * scale).reshape(v.shape), -1, axis)


WIDE = False


def mx_kscale(k):
    if not WIDE:
        return np.ones(k)
    levels = np.array([10, -10, 5, -5, 0])
    if k % 512:
        return np.exp2(np.random.permutation(np.resize(levels, k // 32))).repeat(32)
    a = np.empty((k // 512, 16))
    for p in range(k // 512):
        a[p, :8] = np.random.permutation(np.resize(levels, 8))
        for g in range(8):
            far = levels[np.abs(levels - a[p, g]) >= 10]
            a[p, g + 8] = far[np.random.randint(len(far))]
    return np.exp2(a.ravel()).repeat(32)


def f64(x):
    return np.asarray(x).astype(np.float64)


def striped(idx):
    return np.tile(idx.reshape(-1, 16).T, (8, 1)).astype(np.uint16)


def unstriped(offs):
    return offs[:16].T.reshape(-1).astype(np.int64)


E2M1 = np.array([0.0, 0.5, 1.0, 1.5, 2.0, 3.0, 4.0, 6.0, -0.0, -0.5, -1.0, -1.5, -2.0, -3.0, -4.0, -6.0])


def pack_weight(w, fmt):
    k, n = w.shape
    w = f64(np.asarray(w, np.float32).astype(ml_dtypes.bfloat16)).reshape(k // 32, 32, n)
    amax = np.abs(w).max(1)
    if fmt == "e4m3":
        byte = np.frexp(amax)[1] - 1 + 127 - 7
    else:
        mant, ex = np.frexp(amax / 6.0)
        byte = np.where(mant > 0.5, ex, ex - 1) + 127
    byte = np.clip(np.where(amax > 0, byte, 1), 1, 254)
    scaled = (w * np.exp2(127.0 - byte)[:, None, :]).reshape(k, n).astype(np.float32)
    by_word = np.ascontiguousarray(scaled.reshape(k // 512, 128, 4, n).transpose(0, 1, 3, 2))
    if fmt == "e4m3":
        words = by_word.astype(ml_dtypes.float8_e4m3fn).view(np.uint8)
    else:
        c = by_word.astype(ml_dtypes.float4_e2m1fn).view(np.uint8) & 0xF
        words = (c[..., 0::2] | (c[..., 1::2] << 4)).reshape(k // 512, 128, 2 * n)
    return np.ascontiguousarray(words), np.ascontiguousarray(byte.astype(np.uint8).reshape(k // 512, 16, n))


def unpack_weight(words, scales, fmt):
    g, _, n = scales.shape
    words = np.ascontiguousarray(words).reshape(g, 128, n, -1)
    if fmt == "e4m3":
        vals = words.view(ml_dtypes.float8_e4m3fn).astype(np.float64)
    else:
        nib = np.empty((g, 128, n, 4), np.uint8)
        nib[..., 0::2] = words & 0xF
        nib[..., 1::2] = words >> 4
        vals = E2M1[nib]
    vals = vals * np.repeat(np.exp2(scales.astype(np.float64) - 127.0), 8, axis=1)[..., None]
    return vals.transpose(0, 1, 3, 2).reshape(g * 512, n)


def gelu(v):
    return 0.5 * v * (1.0 + np.tanh(np.sqrt(2.0 / np.pi) * (v + 0.044715 * v**3)))


K, KA, T, T2, S, S2, N = 1024, 512, 4096, 2048, 1024, 1024, 512

def setup_inputs():
    n = np.random.standard_normal
    s = mx_kscale(K)[:, None]
    u = mx_kscale(S)[:, None]
    tab_words, tab_scales = pack_weight(n((K, T)) * s / np.sqrt(KA), "e4m3")
    tab2_words, tab2_scales = pack_weight(n((K, T2)) / s, "e4m3")
    w4_words, w4_scales = pack_weight(n((S, N)) / np.sqrt(S) / u, "e2m1")
    return {
        "tab_words": tab_words, "tab_scales": tab_scales,
        "tab2_words": tab2_words, "tab2_scales": tab2_scales,
        "offs": striped(np.random.permutation(T)[:S]),
        "offs2": striped(np.random.permutation(T2)[:S2]),
        "margin": (np.exp(0.3 * n(S)) * u[:, 0]).astype(np.float32),
        "wc": (0.8 * n((S, N)) / np.sqrt(S) / u).astype(np.float32),
        "w4_words": w4_words, "w4_scales": w4_scales,
    }

def reference(tab_words, tab_scales, tab2_words, tab2_scales, offs, offs2, margin, wc, w4_words, w4_scales):
    v = unpack_weight(tab_words, tab_scales, "e4m3")[:, unstriped(offs)]
    v2 = unpack_weight(tab2_words, tab2_scales, "e4m3")[:, unstriped(offs2)]
    a = v[:KA].T @ v2[:KA]
    f = v[KA:].T @ v2[KA:]
    h = f64(margin)[:, None] * (a / (1.0 + f * f))
    hq = mxq(h, 0, "e4m3")
    wcq = mxq(f64(wc), 0, "e4m3")
    w4 = unpack_weight(w4_words, w4_scales, "e2m1")
    return w4.T @ hq + wcq.T @ hq

@@ -1,0 +1,306 @@
+from contextlib import ExitStack
+
+import concourse.mybir as mybir
+
+K, T, T2, S, S2, N = 1024, 4096, 2048, 1024, 1024, 512
+FLOPS = 2 * K * S * S2 + 2 * 2 * S * N * S2
+
+F32 = mybir.dt.float32
+BF16 = mybir.dt.bfloat16
+I32 = mybir.dt.int32
+U32 = mybir.dt.uint32
+U16 = mybir.dt.uint16
+U8 = mybir.dt.uint8
+FP8X4 = mybir.dt.float8_e4m3fn_x4
+FP4X4 = mybir.dt.float4_e2m1fn_x4
+ACT = mybir.ActivationFunctionType
+MULT = mybir.AluOpType.mult
+ADD = mybir.AluOpType.add
+
+P = 128
+PACK = 4
+HALF = 512
+AFF, FAT = 0, 1
+SHARED_UNITS = ((0, 1), (1, 0))
+
+
+def tile_list_fatigue_brand_affinity_kernel(
+    tc, tab_words, tab_scales, tab2_words, tab2_scales, offs, offs2, margin, wc, w4_words, w4_scales, out
+):
+    nc = tc.nc
+    with ExitStack() as ctx:
+        lists = ctx.enter_context(tc.tile_pool(name="lists", bufs=1))
+        keep = ctx.enter_context(tc.tile_pool(name="keep", bufs=1))
+        stage = ctx.enter_context(tc.tile_pool(name="stage", bufs=1))
+        ring = ctx.enter_context(tc.tile_pool(name="ring", bufs=3))
+        psum = ctx.enter_context(tc.psum_pool(name="psum", bufs=2))
+        psum_out = ctx.enter_context(tc.psum_pool(name="psum_out", bufs=1))
+
+        def kept(shape, dtype, name, tag=""):
+            return keep.tile(shape, dtype, name=name, tag=tag or name, align_bytes=64)
+
+        idx = lists.tile([P, S // 16], U16, name="idx")
+        idx2 = lists.tile([P, S2 // 16], U16, name="idx2")
+        prod_words = [kept([P, T], U32, f"prod_words{a}") for a in range(2)]
+        shop_words = [kept([P, T2], U32, f"shop_words{a}") for a in range(2)]
+        prod_scales = kept([P, T], U8, "prod_scales")
+        shop_scales = kept([P, T2], U8, "shop_scales")
+        margins = kept([P, 2, PACK], F32, "margins")
+        warm = kept([P, 2], F32, "warm")
+
+        def load_words(queue, tile, words):
+            queue.dma_start(out=tile[:].bitcast(I32), in_=words.rearrange("p t i -> p (t i)").bitcast(I32))
+
+        def load_scales(queue, tile, scales, first):
+            for q in range(4):
+                queue.dma_start(
+                    out=tile[32 * q + first : 32 * q + first + 8, :].bitcast(I32),
+                    in_=scales[:, 4 * q : 4 * q + 4, :].bitcast(I32),
+                )
+
+        nc.vector.memset(prod_scales[:].bitcast(I32), 0)
+        nc.vector.memset(shop_scales[:].bitcast(I32), 0)
+        nc.vector.memset(warm[:, 0:1], 1.0)
+        nc.scalar.activation(out=warm[:, 1:2], in_=warm[:, 0:1], func=ACT.Abs_reciprocal_sqrt)
+
+        nc.sync.dma_start(idx2[:], offs2)
+        load_words(nc.sync, shop_words[FAT], tab2_words[FAT])
+        nc.sync.dma_start(idx[:], offs)
+        load_scales(nc.sync, shop_scales, tab2_scales, 8)
+        load_scales(nc.gpsimd, prod_scales, tab_scales, 0)
+        load_words(nc.sync, prod_words[FAT], tab_words[FAT])
+        nc.sync.dma_start(out=margins[:], in_=margin.rearrange("(b p t) -> p b t", b=2, t=PACK))
+        load_words(nc.sync, shop_words[AFF], tab2_words[AFF])
+        load_words(nc.sync, prod_words[AFF], tab_words[AFF])
+
+        weights = {}
+
+        def load_wc():
+            weights["wc_raw"] = kept([P, 2, PACK, N], F32, "wc_raw", tag=f"prod_words{FAT}")
+            for b in range(2):
+                nc.sync.dma_start(
+                    out=weights["wc_raw"][:, b, :, :],
+                    in_=wc[b * HALF : (b + 1) * HALF, :].rearrange("(p t) n -> p t n", t=PACK),
+                )
+
+        def load_base_words():
+            weights["base_words"] = kept([P, 2, 2 * N], U8, "base_words", tag="prod_scales")
+            nc.sync.dma_start(
+                out=weights["base_words"][:].bitcast(I32), in_=w4_words.rearrange("b p x -> p b x").bitcast(I32)
+            )
+
+        def load_base_scales():
+            weights["base_scales"] = kept([P, 2, N], U8, "base_scales", tag="shop_scales")
+            nc.vector.memset(weights["base_scales"][:].rearrange("p b n -> p (b n)").bitcast(I32), 0)
+            for q in range(4):
+                nc.sync.dma_start(
+                    out=weights["base_scales"][32 * q : 32 * q + 4, :, :].bitcast(I32),
+                    in_=w4_scales[:, 4 * q : 4 * q + 4, :].rearrange("b r n -> r b n").bitcast(I32),
+                )
+
+        def staged_tile(cols, dtype, name, offset):
+            return stage.tile([P, cols], dtype, name=name, align_bytes=64, offset=offset)
+
+        def gather(picked, window, offsets, first, count):
+            nc.vector.tensor_copy(
+                out=picked, in_=window[:].indirect(offsets[:, first // 16 : (first + count) // 16])
+            )
+            return picked
+
+        def by_slot(picked, dtype, view, name):
+            ordered = kept([P, HALF], dtype, name)
+            nc.vector.tensor_copy(
+                out=ordered[:].bitcast(view).rearrange("p (t s) -> p s t", t=PACK),
+                in_=picked.bitcast(view).rearrange("p (s t) -> p s t", t=PACK),
+            )
+            return ordered
+
+        v_words, v_scales, v2_words, v2_scales = {}, {}, {}, {}
+
+        def pick_shop_fatigue(jh):
+            tile = kept([P, HALF], U32, "v2wf0") if jh == 0 else staged_tile(HALF, U32, "v2wf1", 2048)
+            v2_words[FAT, jh] = gather(tile[:], shop_words[FAT], idx2, jh * HALF, HALF)
+
+        def pick_shop_affinity():
+            tile = staged_tile(S2, U32, "v2wa", 4096)
+            gather(tile[:], shop_words[AFF], idx2, 0, S2)
+            for jh in range(2):
+                v2_words[AFF, jh] = tile[:, jh * HALF : (jh + 1) * HALF]
+
+        def pick_shop_scales(jh):
+            tile = kept([P, HALF], U8, "v2s0") if jh == 0 else staged_tile(HALF, U8, "v2s1", 8192)
+            v2_scales[jh] = gather(tile[:], shop_scales, idx2, jh * HALF, HALF)
+
+        def pick_prod_words(a, b):
+            tile = staged_tile(2176 if (a, b) == (FAT, 0) else HALF, U32, f"gw{a}{b}", 0)
+            picked = gather(tile[:, 0:HALF], prod_words[a], idx, b * HALF, HALF)
+            v_words[a, b] = by_slot(picked, U32, I32, f"vw{a}{b}")
+
+        def pick_prod_scales(b):
+            tile = staged_tile(HALF, U8, "gs0", 0) if b == 0 else kept([P, HALF], U8, "gs1")
+            v_scales[b] = by_slot(gather(tile[:], prod_scales, idx, b * HALF, HALF), U8, U8, f"vs{b}")
+
+        def table_product(dst, a, b, t, jh, cols):
+            slot = slice(t * P, (t + 1) * P)
+            nc.tensor.matmul_mx(
+                out=dst,
+                lhsT=v_words[a, b][:, slot].bitcast(FP8X4),
+                lhsT_scale=v_scales[b][4 * a :, slot],
+                rhs=v2_words[a, jh][:, cols].bitcast(FP8X4),
+                rhs_scale=v2_scales[jh][8 + 4 * a :, cols],
+                start=True,
+                stop=True,
+            )
+
+        damp = {}
+
+        def damping(jh, b):
+            damp[jh, b] = kept([P, PACK, HALF], F32, f"damp{jh}{b}")
+            for t in range(PACK):
+                f_bank = psum.tile([P, HALF], F32, name="f_bank")
+                table_product(f_bank[:], FAT, b, t, jh, slice(0, HALF))
+                squared = ring.tile([P, HALF], F32, name="squared")
+                nc.scalar.activation(out=squared[:], in_=f_bank[:], func=ACT.Square)
+                weight = damp[jh, b][:, t, :]
+                if (jh, b) in SHARED_UNITS:
+                    root = ring.tile([P, HALF], F32, name="root")
+                    nc.scalar.activation(out=root[:], in_=squared[:], func=ACT.Abs_reciprocal_sqrt, bias=1.0)
+                    nc.scalar.activation(out=weight, in_=root[:], func=ACT.Square)
+                    nc.gpsimd.tensor_scalar(
+                        out=weight, in0=weight, scalar1=margins[:, b, t : t + 1], scalar2=0.0, op0=MULT, op1=ADD
+                    )
+                else:
+                    nc.scalar.activation(out=weight, in_=squared[:], func=ACT.Abs_reciprocal_sqrt, bias=1.0)
+                    nc.vector.scalar_tensor_tensor(
+                        out=weight, in0=weight, scalar=margins[:, b, t : t + 1], in1=weight, op0=MULT, op1=MULT
+                    )
+
+        h_bf, h_words, h_scales = {}, {}, {}
+
+        def affinity(jh, b, c):
+            if c == 0:
+                h_bf[jh, b] = kept([P, HALF * PACK], BF16, f"h_bf{jh}{b}")
+                h_words[jh, b] = kept([P, HALF], U32, f"h_words{jh}{b}")
+                h_scales[jh, b] = kept([P, HALF], U8, f"h_scales{jh}{b}")
+            cols = slice(c * P, (c + 1) * P)
+            a_bank = psum.tile([P, PACK, P], F32, name="a_bank")
+            for t in range(PACK):
+                table_product(a_bank[:, t, :], AFF, b, t, jh, cols)
+            nc.vector.tensor_tensor(
+                out=h_bf[jh, b][:, c * HALF : (c + 1) * HALF].rearrange("p (k i t) -> p k t i", i=4, t=PACK),
+                in0=a_bank[:].rearrange("p t (k i) -> p k t i", i=4),
+                in1=damp[jh, b][:, :, cols].rearrange("p t (k i) -> p k t i", i=4),
+                op=MULT,
+            )
+
+        def quantise_h(jh, b, c0, c1):
+            nc.vector.quantize_mx(
+                out=h_words[jh, b][:, c0 * P : c1 * P].bitcast(FP8X4),
+                scales=h_scales[jh, b][:, c0 * P : c1 * P],
+                in_=h_bf[jh, b][:, c0 * HALF : c1 * HALF],
+            )
+
+        wc_words, wc_scales = {}, {}
+
+        def quantise_wc(b):
+            wc_bf = kept([P, N, PACK], BF16, f"wc_bf{b}")
+            nc.scalar.copy(
+                out=wc_bf[:].rearrange("p (k i) t -> p k t i", i=4),
+                in_=weights["wc_raw"][:, b, :, :].rearrange("p t (k i) -> p k t i", i=4),
+            )
+            wc_words[b] = kept([P, N], U32, f"wc_words{b}")
+            wc_scales[b] = kept([P, N], U8, f"wc_scales{b}")
+            nc.vector.quantize_mx(
+                out=wc_words[b][:].bitcast(FP8X4), scales=wc_scales[b][:], in_=wc_bf[:].rearrange("p n t -> p (n t)")
+            )
+
+        acc = {}
+
+        def brand_pair(dst, jh, b, nt, cols, start, stop):
+            brands = slice(nt * P, (nt + 1) * P)
+            nc.tensor.matmul_mx(
+                out=dst,
+                lhsT=weights["base_words"][:, b, 2 * nt * P : 2 * (nt + 1) * P].bitcast(FP4X4),
+                lhsT_scale=weights["base_scales"][:, b, brands],
+                rhs=h_words[jh, b][:, cols].bitcast(FP8X4),
+                rhs_scale=h_scales[jh, b][:, cols],
+                start=start,
+                stop=False,
+            )
+            nc.tensor.matmul_mx(
+                out=dst,
+                lhsT=wc_words[b][:, brands].bitcast(FP8X4),
+                lhsT_scale=wc_scales[b][:, brands],
+                rhs=h_words[jh, b][:, cols].bitcast(FP8X4),
+                rhs_scale=h_scales[jh, b][:, cols],
+                start=False,
+                stop=stop,
+            )
+
+        def brands_wide(b):
+            for nt in range(4):
+                if b == 0:
+                    acc[0, nt] = psum_out.tile([P, HALF], F32, name=f"acc{nt}")
+                brand_pair(acc[0, nt][:], 0, b, nt, slice(0, HALF), b == 0, b == 1)
+
+        def brands_narrow(b, c):
+            if b == 0:
+                acc[1, c] = psum_out.tile([P, 4, P], F32, name=f"acc{c}")
+            for nt in range(4):
+                brand_pair(
+                    acc[1, c][:, nt, :], 1, b, nt, slice(c * P, (c + 1) * P), b == 0 and nt == 0, b == 1 and nt == 3
+                )
+
+        def store_wide(nt):
+            staged = ring.tile([P, HALF], F32, name="staged", bufs=4)
+            nc.scalar.copy(out=staged[:], in_=acc[0, nt][:])
+            nc.sync.dma_start(out=out[nt * P : (nt + 1) * P, 0:HALF], in_=staged[:])
+
+        def store_narrow(c):
+            staged = ring.tile([P, 4, P], F32, name="staged_narrow", bufs=4)
+            nc.scalar.copy(out=staged[:], in_=acc[1, c][:])
+            nc.sync.dma_start(
+                out=out[:, HALF + c * P : HALF + (c + 1) * P].rearrange("(nt p) j -> p nt j", p=P), in_=staged[:]
+            )
+
+        pick_shop_fatigue(0)
+        pick_shop_scales(0)
+        pick_prod_scales(0)
+        pick_prod_scales(1)
+        load_base_words()
+        pick_prod_words(FAT, 0)
+        pick_prod_words(FAT, 1)
+        load_wc()
+        damping(0, 0)
+        pick_shop_fatigue(1)
+        pick_shop_scales(1)
+        load_base_scales()
+        pick_shop_affinity()
+        damping(0, 1)
+        pick_prod_words(AFF, 0)
+        pick_prod_words(AFF, 1)
+        for c in range(4):
+            affinity(0, 0, c)
+        damping(1, 0)
+        quantise_wc(0)
+        quantise_h(0, 0, 0, 4)
+        brands_wide(0)
+        for c in range(4):
+            affinity(0, 1, c)
+        quantise_wc(1)
+        damping(1, 1)
+        quantise_h(0, 1, 0, 4)
+        brands_wide(1)
+        for c in range(4):
+            affinity(1, 0, c)
+        affinity(1, 1, 0)
+        quantise_h(1, 0, 0, 4)
+        for c in range(4):
+            store_wide(c)
+            brands_narrow(0, c)
+        for c in range(4):
+            if c < 3:
+                affinity(1, 1, c + 1)
+            quantise_h(1, 1, c, c + 1)
+            brands_narrow(1, c)
+            store_narrow(c)

@@ -58,8 +58,8 @@ def tile_list_fatigue_brand_affinity_kernel(
                     in_=scales[:, 4 * q : 4 * q + 4, :].bitcast(I32),
                 )
 
-        nc.vector.memset(prod_scales[:].bitcast(I32), 0)
         nc.vector.memset(shop_scales[:].bitcast(I32), 0)
+        nc.vector.memset(prod_scales[:].bitcast(I32), 0)
         nc.vector.memset(warm[:, 0:1], 1.0)
         nc.scalar.activation(out=warm[:, 1:2], in_=warm[:, 0:1], func=ACT.Abs_reciprocal_sqrt)
 
@@ -67,7 +67,7 @@ def tile_list_fatigue_brand_affinity_kernel(
         load_words(nc.sync, shop_words[FAT], tab2_words[FAT])
         nc.sync.dma_start(idx[:], offs)
         load_scales(nc.sync, shop_scales, tab2_scales, 8)
-        load_scales(nc.gpsimd, prod_scales, tab_scales, 0)
+        load_scales(nc.sync, prod_scales, tab_scales, 0)
         load_words(nc.sync, prod_words[FAT], tab_words[FAT])
         nc.sync.dma_start(out=margins[:], in_=margin.rearrange("(b p t) -> p b t", b=2, t=PACK))
         load_words(nc.sync, shop_words[AFF], tab2_words[AFF])
@@ -107,18 +107,18 @@ def tile_list_fatigue_brand_affinity_kernel(
             )
             return picked
 
-        def by_slot(picked, dtype, view, name):
+        def by_slot(picked, dtype, view, name, run):
             ordered = kept([P, HALF], dtype, name)
             nc.vector.tensor_copy(
-                out=ordered[:].bitcast(view).rearrange("p (t s) -> p s t", t=PACK),
-                in_=picked.bitcast(view).rearrange("p (s t) -> p s t", t=PACK),
+                out=ordered[:].bitcast(view).rearrange("p (t c i) -> p c t i", t=PACK, i=run),
+                in_=picked.bitcast(view).rearrange("p (c i t) -> p c t i", t=PACK, i=run),
             )
             return ordered
 
         v_words, v_scales, v2_words, v2_scales = {}, {}, {}, {}
 
         def pick_shop_fatigue(jh):
-            tile = kept([P, HALF], U32, "v2wf0") if jh == 0 else staged_tile(HALF, U32, "v2wf1", 2048)
+            tile = kept([P, HALF], U32, f"v2wf{jh}")
             v2_words[FAT, jh] = gather(tile[:], shop_words[FAT], idx2, jh * HALF, HALF)
 
         def pick_shop_affinity():
@@ -134,11 +134,11 @@ def tile_list_fatigue_brand_affinity_kernel(
         def pick_prod_words(a, b):
             tile = staged_tile(2176 if (a, b) == (FAT, 0) else HALF, U32, f"gw{a}{b}", 0)
             picked = gather(tile[:, 0:HALF], prod_words[a], idx, b * HALF, HALF)
-            v_words[a, b] = by_slot(picked, U32, I32, f"vw{a}{b}")
+            v_words[a, b] = by_slot(picked, U32, I32, f"vw{a}{b}", 4)
 
         def pick_prod_scales(b):
             tile = staged_tile(HALF, U8, "gs0", 0) if b == 0 else kept([P, HALF], U8, "gs1")
-            v_scales[b] = by_slot(gather(tile[:], prod_scales, idx, b * HALF, HALF), U8, U8, f"vs{b}")
+            v_scales[b] = by_slot(gather(tile[:], prod_scales, idx, b * HALF, HALF), U8, U8, f"vs{b}", 16)
 
         def table_product(dst, a, b, t, jh, cols):
             slot = slice(t * P, (t + 1) * P)
@@ -187,9 +187,9 @@ def tile_list_fatigue_brand_affinity_kernel(
             for t in range(PACK):
                 table_product(a_bank[:, t, :], AFF, b, t, jh, cols)
             nc.vector.tensor_tensor(
-                out=h_bf[jh, b][:, c * HALF : (c + 1) * HALF].rearrange("p (k i t) -> p k t i", i=4, t=PACK),
-                in0=a_bank[:].rearrange("p t (k i) -> p k t i", i=4),
-                in1=damp[jh, b][:, :, cols].rearrange("p t (k i) -> p k t i", i=4),
+                out=h_bf[jh, b][:, c * HALF : (c + 1) * HALF].rearrange("p (k i t) -> p k t i", i=2, t=PACK),
+                in0=a_bank[:].rearrange("p t (k i) -> p k t i", i=2),
+                in1=damp[jh, b][:, :, cols].rearrange("p t (k i) -> p k t i", i=2),
                 op=MULT,
             )
 
@@ -204,7 +204,7 @@ def tile_list_fatigue_brand_affinity_kernel(
 
         def quantise_wc(b):
             wc_bf = kept([P, N, PACK], BF16, f"wc_bf{b}")
-            nc.scalar.copy(
+            (nc.vector.tensor_copy if b == 0 else nc.scalar.copy)(
                 out=wc_bf[:].rearrange("p (k i) t -> p k t i", i=4),
                 in_=weights["wc_raw"][:, b, :, :].rearrange("p t (k i) -> p k t i", i=4),
             )
@@ -268,11 +268,11 @@ def tile_list_fatigue_brand_affinity_kernel(
         pick_prod_scales(0)
         pick_prod_scales(1)
         load_base_words()
+        pick_shop_fatigue(1)
         pick_prod_words(FAT, 0)
         pick_prod_words(FAT, 1)
         load_wc()
         damping(0, 0)
-        pick_shop_fatigue(1)
         pick_shop_scales(1)
         load_base_scales()
         pick_shop_affinity()

@@ -21,7 +21,7 @@ P = 128
 PACK = 4
 HALF = 512
 AFF, FAT = 0, 1
-SHARED_UNITS = ((0, 1), (1, 0))
+SHARED_FIRST, SHARED_END = 4, 12
 
 
 def tile_list_fatigue_brand_affinity_kernel(
@@ -91,7 +91,7 @@ def tile_list_fatigue_brand_affinity_kernel(
 
         def load_base_scales():
             weights["base_scales"] = kept([P, 2, N], U8, "base_scales", tag="shop_scales")
-            nc.vector.memset(weights["base_scales"][:].rearrange("p b n -> p (b n)").bitcast(I32), 0)
+            nc.gpsimd.memset(weights["base_scales"][:].rearrange("p b n -> p (b n)").bitcast(I32), 0)
             for q in range(4):
                 nc.sync.dma_start(
                     out=weights["base_scales"][32 * q : 32 * q + 4, :, :].bitcast(I32),
@@ -157,12 +157,15 @@ def tile_list_fatigue_brand_affinity_kernel(
         def damping(jh, b):
             damp[jh, b] = kept([P, PACK, HALF], F32, f"damp{jh}{b}")
             for t in range(PACK):
-                f_bank = psum.tile([P, HALF], F32, name="f_bank")
+                if (jh, b) == (1, 1):
+                    f_bank = psum_out.tile([P, HALF], F32, name=f"acc{t}")
+                else:
+                    f_bank = psum.tile([P, HALF], F32, name="f_bank")
                 table_product(f_bank[:], FAT, b, t, jh, slice(0, HALF))
                 squared = ring.tile([P, HALF], F32, name="squared")
                 nc.scalar.activation(out=squared[:], in_=f_bank[:], func=ACT.Square)
                 weight = damp[jh, b][:, t, :]
-                if (jh, b) in SHARED_UNITS:
+                if SHARED_FIRST <= 8 * jh + 4 * b + t < SHARED_END:
                     root = ring.tile([P, HALF], F32, name="root")
                     nc.scalar.activation(out=root[:], in_=squared[:], func=ACT.Abs_reciprocal_sqrt, bias=1.0)
                     nc.scalar.activation(out=weight, in_=root[:], func=ACT.Square)
@@ -183,7 +186,7 @@ def tile_list_fatigue_brand_affinity_kernel(
                 h_words[jh, b] = kept([P, HALF], U32, f"h_words{jh}{b}")
                 h_scales[jh, b] = kept([P, HALF], U8, f"h_scales{jh}{b}")
             cols = slice(c * P, (c + 1) * P)
-            a_bank = psum.tile([P, PACK, P], F32, name="a_bank")
+            a_bank = psum.tile([P, PACK, P], F32, name="f_bank" if jh == 1 and c % 2 == 1 else "a_bank")
             for t in range(PACK):
                 table_product(a_bank[:, t, :], AFF, b, t, jh, cols)
             nc.vector.tensor_tensor(
@@ -204,7 +207,7 @@ def tile_list_fatigue_brand_affinity_kernel(
 
         def quantise_wc(b):
             wc_bf = kept([P, N, PACK], BF16, f"wc_bf{b}")
-            (nc.vector.tensor_copy if b == 0 else nc.scalar.copy)(
+            nc.vector.tensor_copy(
                 out=wc_bf[:].rearrange("p (k i) t -> p k t i", i=4),
                 in_=weights["wc_raw"][:, b, :, :].rearrange("p t (k i) -> p k t i", i=4),
             )
@@ -237,19 +240,25 @@ def tile_list_fatigue_brand_affinity_kernel(
                 stop=stop,
             )
 
-        def brands_wide(b):
-            for nt in range(4):
-                if b == 0:
-                    acc[0, nt] = psum_out.tile([P, HALF], F32, name=f"acc{nt}")
+        def brands_wide(nt):
+            acc[0, nt] = psum_out.tile([P, HALF], F32, name=f"acc{nt}")
+            for b in range(2):
                 brand_pair(acc[0, nt][:], 0, b, nt, slice(0, HALF), b == 0, b == 1)
 
+        def narrow_parts(c):
+            return ((0, 4),) if c < 3 else ((0, 2), (2, 4))
+
         def brands_narrow(b, c):
-            if b == 0:
-                acc[1, c] = psum_out.tile([P, 4, P], F32, name=f"acc{c}")
-            for nt in range(4):
-                brand_pair(
-                    acc[1, c][:, nt, :], 1, b, nt, slice(c * P, (c + 1) * P), b == 0 and nt == 0, b == 1 and nt == 3
-                )
+            for lo, hi in narrow_parts(c):
+                if b == 0 and lo == 0:
+                    acc[1, c, lo] = psum_out.tile([P, hi - lo, P], F32, name=f"acc{c}")
+                elif b == 0:
+                    acc[1, c, lo] = psum.tile([P, hi - lo, P], F32, name="a_bank")
+                for nt in range(lo, hi):
+                    brand_pair(
+                        acc[1, c, lo][:, nt - lo, :], 1, b, nt, slice(c * P, (c + 1) * P),
+                        b == 0 and nt == lo, b == 1 and nt == hi - 1,
+                    )
 
         def store_wide(nt):
             staged = ring.tile([P, HALF], F32, name="staged", bufs=4)
@@ -257,11 +266,13 @@ def tile_list_fatigue_brand_affinity_kernel(
             nc.sync.dma_start(out=out[nt * P : (nt + 1) * P, 0:HALF], in_=staged[:])
 
         def store_narrow(c):
-            staged = ring.tile([P, 4, P], F32, name="staged_narrow", bufs=4)
-            nc.scalar.copy(out=staged[:], in_=acc[1, c][:])
-            nc.sync.dma_start(
-                out=out[:, HALF + c * P : HALF + (c + 1) * P].rearrange("(nt p) j -> p nt j", p=P), in_=staged[:]
-            )
+            for lo, hi in narrow_parts(c):
+                staged = kept([P, hi - lo, P], F32, f"staged{c}{lo}")
+                (nc.scalar.copy if lo == 0 else nc.vector.tensor_copy)(out=staged[:], in_=acc[1, c, lo][:])
+                nc.sync.dma_start(
+                    out=out[lo * P : hi * P, HALF + c * P : HALF + (c + 1) * P].rearrange("(nt p) j -> p nt j", p=P),
+                    in_=staged[:],
+                )
 
         pick_shop_fatigue(0)
         pick_shop_scales(0)
@@ -284,15 +295,14 @@ def tile_list_fatigue_brand_affinity_kernel(
         damping(1, 0)
         quantise_wc(0)
         quantise_h(0, 0, 0, 4)
-        brands_wide(0)
         for c in range(4):
             affinity(0, 1, c)
         quantise_wc(1)
         damping(1, 1)
         quantise_h(0, 1, 0, 4)
-        brands_wide(1)
         for c in range(4):
             affinity(1, 0, c)
+            brands_wide(c)
         affinity(1, 1, 0)
         quantise_h(1, 0, 0, 4)
         for c in range(4):

@@ -15,13 +15,11 @@ FP8X4 = mybir.dt.float8_e4m3fn_x4
 FP4X4 = mybir.dt.float4_e2m1fn_x4
 ACT = mybir.ActivationFunctionType
 MULT = mybir.AluOpType.mult
-ADD = mybir.AluOpType.add
 
 P = 128
 PACK = 4
 HALF = 512
 AFF, FAT = 0, 1
-SHARED_FIRST, SHARED_END = 4, 12
 
 
 def tile_list_fatigue_brand_affinity_kernel(
@@ -46,7 +44,6 @@ def tile_list_fatigue_brand_affinity_kernel(
         prod_scales = kept([P, T], U8, "prod_scales")
         shop_scales = kept([P, T2], U8, "shop_scales")
         margins = kept([P, 2, PACK], F32, "margins")
-        warm = kept([P, 2], F32, "warm")
 
         def load_words(queue, tile, words):
             queue.dma_start(out=tile[:].bitcast(I32), in_=words.rearrange("p t i -> p (t i)").bitcast(I32))
@@ -60,8 +57,6 @@ def tile_list_fatigue_brand_affinity_kernel(
 
         nc.vector.memset(shop_scales[:].bitcast(I32), 0)
         nc.vector.memset(prod_scales[:].bitcast(I32), 0)
-        nc.vector.memset(warm[:, 0:1], 1.0)
-        nc.scalar.activation(out=warm[:, 1:2], in_=warm[:, 0:1], func=ACT.Abs_reciprocal_sqrt)
 
         nc.sync.dma_start(idx2[:], offs2)
         load_words(nc.sync, shop_words[FAT], tab2_words[FAT])
@@ -91,7 +86,7 @@ def tile_list_fatigue_brand_affinity_kernel(
 
         def load_base_scales():
             weights["base_scales"] = kept([P, 2, N], U8, "base_scales", tag="shop_scales")
-            nc.gpsimd.memset(weights["base_scales"][:].rearrange("p b n -> p (b n)").bitcast(I32), 0)
+            nc.vector.memset(weights["base_scales"][:].rearrange("p b n -> p (b n)").bitcast(I32), 0)
             for q in range(4):
                 nc.sync.dma_start(
                     out=weights["base_scales"][32 * q : 32 * q + 4, :, :].bitcast(I32),
@@ -165,18 +160,10 @@ def tile_list_fatigue_brand_affinity_kernel(
                 squared = ring.tile([P, HALF], F32, name="squared")
                 nc.scalar.activation(out=squared[:], in_=f_bank[:], func=ACT.Square)
                 weight = damp[jh, b][:, t, :]
-                if SHARED_FIRST <= 8 * jh + 4 * b + t < SHARED_END:
-                    root = ring.tile([P, HALF], F32, name="root")
-                    nc.scalar.activation(out=root[:], in_=squared[:], func=ACT.Abs_reciprocal_sqrt, bias=1.0)
-                    nc.scalar.activation(out=weight, in_=root[:], func=ACT.Square)
-                    nc.gpsimd.tensor_scalar(
-                        out=weight, in0=weight, scalar1=margins[:, b, t : t + 1], scalar2=0.0, op0=MULT, op1=ADD
-                    )
-                else:
-                    nc.scalar.activation(out=weight, in_=squared[:], func=ACT.Abs_reciprocal_sqrt, bias=1.0)
-                    nc.vector.scalar_tensor_tensor(
-                        out=weight, in0=weight, scalar=margins[:, b, t : t + 1], in1=weight, op0=MULT, op1=MULT
-                    )
+                nc.scalar.activation(out=weight, in_=squared[:], func=ACT.Abs_reciprocal_sqrt, bias=1.0)
+                nc.vector.scalar_tensor_tensor(
+                    out=weight, in0=weight, scalar=margins[:, b, t : t + 1], in1=weight, op0=MULT, op1=MULT
+                )
 
         h_bf, h_words, h_scales = {}, {}, {}
 
@@ -207,7 +194,7 @@ def tile_list_fatigue_brand_affinity_kernel(
 
         def quantise_wc(b):
             wc_bf = kept([P, N, PACK], BF16, f"wc_bf{b}")
-            nc.vector.tensor_copy(
+            nc.scalar.copy(
                 out=wc_bf[:].rearrange("p (k i) t -> p k t i", i=4),
                 in_=weights["wc_raw"][:, b, :, :].rearrange("p t (k i) -> p k t i", i=4),
             )

@@ -15,11 +15,14 @@ FP8X4 = mybir.dt.float8_e4m3fn_x4
 FP4X4 = mybir.dt.float4_e2m1fn_x4
 ACT = mybir.ActivationFunctionType
 MULT = mybir.AluOpType.mult
+MAX = mybir.AluOpType.max
+IS_GE = mybir.AluOpType.is_ge
 
 P = 128
 PACK = 4
 HALF = 512
 AFF, FAT = 0, 1
+SMALLEST_MARGIN = 1e-30
 
 
 def tile_list_fatigue_brand_affinity_kernel(
@@ -29,7 +32,7 @@ def tile_list_fatigue_brand_affinity_kernel(
     with ExitStack() as ctx:
         lists = ctx.enter_context(tc.tile_pool(name="lists", bufs=1))
         keep = ctx.enter_context(tc.tile_pool(name="keep", bufs=1))
-        stage = ctx.enter_context(tc.tile_pool(name="stage", bufs=1))
+        reuse = ctx.enter_context(tc.tile_pool(name="reuse", bufs=1))
         ring = ctx.enter_context(tc.tile_pool(name="ring", bufs=3))
         psum = ctx.enter_context(tc.psum_pool(name="psum", bufs=2))
         psum_out = ctx.enter_context(tc.psum_pool(name="psum_out", bufs=1))
@@ -39,14 +42,15 @@ def tile_list_fatigue_brand_affinity_kernel(
 
         idx = lists.tile([P, S // 16], U16, name="idx")
         idx2 = lists.tile([P, S2 // 16], U16, name="idx2")
-        prod_words = [kept([P, T], U32, f"prod_words{a}") for a in range(2)]
-        shop_words = [kept([P, T2], U32, f"shop_words{a}") for a in range(2)]
+        prod_fatigue = reuse.tile([P, T + HALF // 4], U32, name="prod_fatigue", align_bytes=64, offset=0)
+        prod_words = {AFF: kept([P, T], U32, "prod_affinity")[:], FAT: prod_fatigue[:, 0:T]}
+        shop_words = [kept([P, T2], U32, f"shop_words{a}")[:] for a in range(2)]
         prod_scales = kept([P, T], U8, "prod_scales")
         shop_scales = kept([P, T2], U8, "shop_scales")
         margins = kept([P, 2, PACK], F32, "margins")
 
         def load_words(queue, tile, words):
-            queue.dma_start(out=tile[:].bitcast(I32), in_=words.rearrange("p t i -> p (t i)").bitcast(I32))
+            queue.dma_start(out=tile.bitcast(I32), in_=words.rearrange("p t i -> p (t i)").bitcast(I32))
 
         def load_scales(queue, tile, scales, first):
             for q in range(4):
@@ -58,20 +62,20 @@ def tile_list_fatigue_brand_affinity_kernel(
         nc.vector.memset(shop_scales[:].bitcast(I32), 0)
         nc.vector.memset(prod_scales[:].bitcast(I32), 0)
 
+        nc.scalar.dma_start(out=margins[:], in_=margin.rearrange("(b p t) -> p b t", b=2, t=PACK))
         nc.sync.dma_start(idx2[:], offs2)
         load_words(nc.sync, shop_words[FAT], tab2_words[FAT])
         nc.sync.dma_start(idx[:], offs)
         load_scales(nc.sync, shop_scales, tab2_scales, 8)
         load_scales(nc.sync, prod_scales, tab_scales, 0)
         load_words(nc.sync, prod_words[FAT], tab_words[FAT])
-        nc.sync.dma_start(out=margins[:], in_=margin.rearrange("(b p t) -> p b t", b=2, t=PACK))
         load_words(nc.sync, shop_words[AFF], tab2_words[AFF])
         load_words(nc.sync, prod_words[AFF], tab_words[AFF])
 
         weights = {}
 
         def load_wc():
-            weights["wc_raw"] = kept([P, 2, PACK, N], F32, "wc_raw", tag=f"prod_words{FAT}")
+            weights["wc_raw"] = reuse.tile([P, 2, PACK, N], F32, name="wc_raw", align_bytes=64, offset=0)
             for b in range(2):
                 nc.sync.dma_start(
                     out=weights["wc_raw"][:, b, :, :],
@@ -93,59 +97,66 @@ def tile_list_fatigue_brand_affinity_kernel(
                     in_=w4_scales[:, 4 * q : 4 * q + 4, :].rearrange("b r n -> r b n").bitcast(I32),
                 )
 
-        def staged_tile(cols, dtype, name, offset):
-            return stage.tile([P, cols], dtype, name=name, align_bytes=64, offset=offset)
+        def gather(picked, window, offsets):
+            nc.vector.tensor_copy(out=picked, in_=window.indirect(offsets))
 
-        def gather(picked, window, offsets, first, count):
-            nc.vector.tensor_copy(
-                out=picked, in_=window[:].indirect(offsets[:, first // 16 : (first + count) // 16])
-            )
-            return picked
-
-        def by_slot(picked, dtype, view, name, run):
-            ordered = kept([P, HALF], dtype, name)
-            nc.vector.tensor_copy(
-                out=ordered[:].bitcast(view).rearrange("p (t c i) -> p c t i", t=PACK, i=run),
-                in_=picked.bitcast(view).rearrange("p (c i t) -> p c t i", t=PACK, i=run),
-            )
-            return ordered
-
-        v_words, v_scales, v2_words, v2_scales = {}, {}, {}, {}
-
-        def pick_shop_fatigue(jh):
-            tile = kept([P, HALF], U32, f"v2wf{jh}")
-            v2_words[FAT, jh] = gather(tile[:], shop_words[FAT], idx2, jh * HALF, HALF)
-
-        def pick_shop_affinity():
-            tile = staged_tile(S2, U32, "v2wa", 4096)
-            gather(tile[:], shop_words[AFF], idx2, 0, S2)
-            for jh in range(2):
-                v2_words[AFF, jh] = tile[:, jh * HALF : (jh + 1) * HALF]
-
-        def pick_shop_scales(jh):
-            tile = kept([P, HALF], U8, "v2s0") if jh == 0 else staged_tile(HALF, U8, "v2s1", 8192)
-            v2_scales[jh] = gather(tile[:], shop_scales, idx2, jh * HALF, HALF)
+        v2_words = [kept([P, S2], U32, f"v2_words{a}") for a in range(2)]
+        v2_scales = {}
+        v_words = {(a, b): kept([P, HALF], U32, f"v_words{a}{b}") for a in range(2) for b in range(2)}
+        listed_scales = kept([P, S], U8, "listed_scales")
+        v_scales = kept([P, S], U8, "v_scales")
 
         def pick_prod_words(a, b):
-            tile = staged_tile(2176 if (a, b) == (FAT, 0) else HALF, U32, f"gw{a}{b}", 0)
-            picked = gather(tile[:, 0:HALF], prod_words[a], idx, b * HALF, HALF)
-            v_words[a, b] = by_slot(picked, U32, I32, f"vw{a}{b}", 4)
+            gather(
+                v_words[a, b][:].rearrange("p (t s) -> p s t", t=PACK),
+                prod_words[a],
+                idx[:, b * HALF // 16 : (b + 1) * HALF // 16],
+            )
 
-        def pick_prod_scales(b):
-            tile = staged_tile(HALF, U8, "gs0", 0) if b == 0 else kept([P, HALF], U8, "gs1")
-            v_scales[b] = by_slot(gather(tile[:], prod_scales, idx, b * HALF, HALF), U8, U8, f"vs{b}", 16)
+        def pick_prod_scales():
+            gather(listed_scales[:], prod_scales[:], idx[:])
+
+        def pick_shop_scales(jh):
+            if jh == 0:
+                v2_scales[jh] = kept([P, HALF], U8, "v2_scales0")
+            else:
+                v2_scales[jh] = reuse.tile([P, HALF], U8, name="v2_scales1", align_bytes=64, offset=4 * T)
+            gather(v2_scales[jh][:], shop_scales[:], idx2[:, jh * HALF // 16 : (jh + 1) * HALF // 16])
+
+        def order_prod_scales():
+            nc.vector.tensor_copy(
+                out=v_scales[:].rearrange("p (b t c i) -> p b c t i", b=2, t=PACK, i=16),
+                in_=listed_scales[:].rearrange("p (b c i t) -> p b c t i", b=2, t=PACK, i=16),
+            )
 
         def table_product(dst, a, b, t, jh, cols):
             slot = slice(t * P, (t + 1) * P)
+            shoppers = slice(jh * HALF + cols.start, jh * HALF + cols.stop)
             nc.tensor.matmul_mx(
                 out=dst,
                 lhsT=v_words[a, b][:, slot].bitcast(FP8X4),
-                lhsT_scale=v_scales[b][4 * a :, slot],
-                rhs=v2_words[a, jh][:, cols].bitcast(FP8X4),
+                lhsT_scale=v_scales[4 * a :, b * HALF + t * P : b * HALF + (t + 1) * P],
+                rhs=v2_words[a][:, shoppers].bitcast(FP8X4),
                 rhs_scale=v2_scales[jh][8 + 4 * a :, cols],
                 start=True,
                 stop=True,
             )
+
+        size_roots = kept([P, PACK], F32, "size_roots")
+        signs = kept([P, 1, PACK], BF16, "signs")
+
+        def split_margins():
+            first = margins[:, 0, :]
+            sizes = kept([P, PACK], F32, "sizes")
+            clamped = kept([P, PACK], F32, "clamped")
+            inverse_roots = kept([P, PACK], F32, "inverse_roots")
+            doubled = kept([P, PACK], F32, "doubled")
+            nc.vector.scalar_tensor_tensor(out=sizes[:], in0=first, scalar=-1.0, in1=first, op0=MULT, op1=MAX)
+            nc.vector.tensor_scalar(out=doubled[:], in0=first, scalar1=0.0, scalar2=2.0, op0=IS_GE, op1=MULT)
+            nc.vector.tensor_scalar_max(out=clamped[:], in0=sizes[:], scalar1=SMALLEST_MARGIN)
+            nc.vector.tensor_scalar_add(out=signs[:, 0, :], in0=doubled[:], scalar1=-1.0)
+            nc.scalar.activation(out=inverse_roots[:], in_=clamped[:], func=ACT.Abs_reciprocal_sqrt)
+            nc.vector.tensor_tensor(out=size_roots[:], in0=clamped[:], in1=inverse_roots[:], op=MULT)
 
         damp = {}
 
@@ -160,10 +171,15 @@ def tile_list_fatigue_brand_affinity_kernel(
                 squared = ring.tile([P, HALF], F32, name="squared")
                 nc.scalar.activation(out=squared[:], in_=f_bank[:], func=ACT.Square)
                 weight = damp[jh, b][:, t, :]
-                nc.scalar.activation(out=weight, in_=squared[:], func=ACT.Abs_reciprocal_sqrt, bias=1.0)
-                nc.vector.scalar_tensor_tensor(
-                    out=weight, in0=weight, scalar=margins[:, b, t : t + 1], in1=weight, op0=MULT, op1=MULT
-                )
+                if (jh, b) == (0, 0):
+                    root = ring.tile([P, HALF], F32, name="root")
+                    nc.scalar.activation(out=root[:], in_=squared[:], func=ACT.Abs_reciprocal_sqrt, bias=1.0)
+                    nc.scalar.activation(out=weight, in_=root[:], func=ACT.Square, scale=size_roots[:, t : t + 1])
+                else:
+                    nc.scalar.activation(out=weight, in_=squared[:], func=ACT.Abs_reciprocal_sqrt, bias=1.0)
+                    nc.vector.scalar_tensor_tensor(
+                        out=weight, in0=weight, scalar=margins[:, b, t : t + 1], in1=weight, op0=MULT, op1=MULT
+                    )
 
         h_bf, h_words, h_scales = {}, {}, {}
 
@@ -182,6 +198,10 @@ def tile_list_fatigue_brand_affinity_kernel(
                 in1=damp[jh, b][:, :, cols].rearrange("p t (k i) -> p k t i", i=2),
                 op=MULT,
             )
+
+        def apply_signs():
+            h_view = h_bf[0, 0][:].rearrange("p (j t) -> p j t", t=PACK)
+            nc.vector.tensor_tensor(out=h_view, in0=h_view, in1=signs[:].to_broadcast([P, HALF, PACK]), op=MULT)
 
         def quantise_h(jh, b, c0, c1):
             nc.vector.quantize_mx(
@@ -261,25 +281,26 @@ def tile_list_fatigue_brand_affinity_kernel(
                     in_=staged[:],
                 )
 
-        pick_shop_fatigue(0)
+        gather(v2_words[FAT][:], shop_words[FAT], idx2[:])
         pick_shop_scales(0)
-        pick_prod_scales(0)
-        pick_prod_scales(1)
+        pick_prod_scales()
         load_base_words()
-        pick_shop_fatigue(1)
+        order_prod_scales()
+        split_margins()
         pick_prod_words(FAT, 0)
         pick_prod_words(FAT, 1)
         load_wc()
-        damping(0, 0)
         pick_shop_scales(1)
         load_base_scales()
-        pick_shop_affinity()
+        damping(0, 0)
+        gather(v2_words[AFF][:], shop_words[AFF], idx2[:])
         damping(0, 1)
         pick_prod_words(AFF, 0)
         pick_prod_words(AFF, 1)
         for c in range(4):
             affinity(0, 0, c)
         damping(1, 0)
+        apply_signs()
         quantise_wc(0)
         quantise_h(0, 0, 0, 4)
         for c in range(4):

@@ -15,14 +15,11 @@ FP8X4 = mybir.dt.float8_e4m3fn_x4
 FP4X4 = mybir.dt.float4_e2m1fn_x4
 ACT = mybir.ActivationFunctionType
 MULT = mybir.AluOpType.mult
-MAX = mybir.AluOpType.max
-IS_GE = mybir.AluOpType.is_ge
 
 P = 128
 PACK = 4
 HALF = 512
 AFF, FAT = 0, 1
-SMALLEST_MARGIN = 1e-30
 
 
 def tile_list_fatigue_brand_affinity_kernel(
@@ -62,13 +59,17 @@ def tile_list_fatigue_brand_affinity_kernel(
         nc.vector.memset(shop_scales[:].bitcast(I32), 0)
         nc.vector.memset(prod_scales[:].bitcast(I32), 0)
 
-        nc.scalar.dma_start(out=margins[:], in_=margin.rearrange("(b p t) -> p b t", b=2, t=PACK))
+        warm = kept([P, 2], F32, "warm")
+        nc.gpsimd.memset(warm[:, 0:1], 1.0)
+        nc.scalar.activation(out=warm[:, 1:2], in_=warm[:, 0:1], func=ACT.Abs_reciprocal_sqrt)
+
         nc.sync.dma_start(idx2[:], offs2)
         load_words(nc.sync, shop_words[FAT], tab2_words[FAT])
         nc.sync.dma_start(idx[:], offs)
         load_scales(nc.sync, shop_scales, tab2_scales, 8)
         load_scales(nc.sync, prod_scales, tab_scales, 0)
         load_words(nc.sync, prod_words[FAT], tab_words[FAT])
+        nc.sync.dma_start(out=margins[:], in_=margin.rearrange("(b p t) -> p b t", b=2, t=PACK))
         load_words(nc.sync, shop_words[AFF], tab2_words[AFF])
         load_words(nc.sync, prod_words[AFF], tab_words[AFF])
 
@@ -142,44 +143,33 @@ def tile_list_fatigue_brand_affinity_kernel(
                 stop=True,
             )
 
-        size_roots = kept([P, PACK], F32, "size_roots")
-        signs = kept([P, 1, PACK], BF16, "signs")
+        quarters = [(jh, b) for jh in range(2) for b in range(2)]
+        damp = {q: kept([P, PACK, HALF], F32, f"damp{q[0]}{q[1]}") for q in quarters}
+        squared = {}
 
-        def split_margins():
-            first = margins[:, 0, :]
-            sizes = kept([P, PACK], F32, "sizes")
-            clamped = kept([P, PACK], F32, "clamped")
-            inverse_roots = kept([P, PACK], F32, "inverse_roots")
-            doubled = kept([P, PACK], F32, "doubled")
-            nc.vector.scalar_tensor_tensor(out=sizes[:], in0=first, scalar=-1.0, in1=first, op0=MULT, op1=MAX)
-            nc.vector.tensor_scalar(out=doubled[:], in0=first, scalar1=0.0, scalar2=2.0, op0=IS_GE, op1=MULT)
-            nc.vector.tensor_scalar_max(out=clamped[:], in0=sizes[:], scalar1=SMALLEST_MARGIN)
-            nc.vector.tensor_scalar_add(out=signs[:, 0, :], in0=doubled[:], scalar1=-1.0)
-            nc.scalar.activation(out=inverse_roots[:], in_=clamped[:], func=ACT.Abs_reciprocal_sqrt)
-            nc.vector.tensor_tensor(out=size_roots[:], in0=clamped[:], in1=inverse_roots[:], op=MULT)
+        def square(k):
+            (jh, b), t = quarters[k // PACK], k % PACK
+            f_bank = psum.tile([P, HALF], F32, name="f_bank")
+            table_product(f_bank[:], FAT, b, t, jh, slice(0, HALF))
+            squared[k] = ring.tile([P, HALF], F32, name="squared")
+            nc.scalar.activation(out=squared[k][:], in_=f_bank[:], func=ACT.Square)
 
-        damp = {}
+        def root(k):
+            weight = damp[quarters[k // PACK]][:, k % PACK, :]
+            nc.scalar.activation(out=weight, in_=squared[k][:], func=ACT.Abs_reciprocal_sqrt, bias=1.0)
 
-        def damping(jh, b):
-            damp[jh, b] = kept([P, PACK, HALF], F32, f"damp{jh}{b}")
-            for t in range(PACK):
-                if (jh, b) == (1, 1):
-                    f_bank = psum_out.tile([P, HALF], F32, name=f"acc{t}")
-                else:
-                    f_bank = psum.tile([P, HALF], F32, name="f_bank")
-                table_product(f_bank[:], FAT, b, t, jh, slice(0, HALF))
-                squared = ring.tile([P, HALF], F32, name="squared")
-                nc.scalar.activation(out=squared[:], in_=f_bank[:], func=ACT.Square)
-                weight = damp[jh, b][:, t, :]
-                if (jh, b) == (0, 0):
-                    root = ring.tile([P, HALF], F32, name="root")
-                    nc.scalar.activation(out=root[:], in_=squared[:], func=ACT.Abs_reciprocal_sqrt, bias=1.0)
-                    nc.scalar.activation(out=weight, in_=root[:], func=ACT.Square, scale=size_roots[:, t : t + 1])
-                else:
-                    nc.scalar.activation(out=weight, in_=squared[:], func=ACT.Abs_reciprocal_sqrt, bias=1.0)
-                    nc.vector.scalar_tensor_tensor(
-                        out=weight, in0=weight, scalar=margins[:, b, t : t + 1], in1=weight, op0=MULT, op1=MULT
-                    )
+        def weigh(k):
+            (jh, b), t = quarters[k // PACK], k % PACK
+            weight = damp[jh, b][:, t, :]
+            nc.vector.scalar_tensor_tensor(
+                out=weight, in0=weight, scalar=margins[:, b, t : t + 1], in1=weight, op0=MULT, op1=MULT
+            )
+
+        def roots(k0, k1):
+            for k in range(k0, k1):
+                if k + 1 < 4 * PACK:
+                    square(k + 1)
+                root(k)
 
         h_bf, h_words, h_scales = {}, {}, {}
 
@@ -189,7 +179,7 @@ def tile_list_fatigue_brand_affinity_kernel(
                 h_words[jh, b] = kept([P, HALF], U32, f"h_words{jh}{b}")
                 h_scales[jh, b] = kept([P, HALF], U8, f"h_scales{jh}{b}")
             cols = slice(c * P, (c + 1) * P)
-            a_bank = psum.tile([P, PACK, P], F32, name="f_bank" if jh == 1 and c % 2 == 1 else "a_bank")
+            a_bank = psum.tile([P, PACK, P], F32, name="f_bank" if (jh, b) == (1, 1) and c % 2 == 1 else "a_bank")
             for t in range(PACK):
                 table_product(a_bank[:, t, :], AFF, b, t, jh, cols)
             nc.vector.tensor_tensor(
@@ -198,10 +188,6 @@ def tile_list_fatigue_brand_affinity_kernel(
                 in1=damp[jh, b][:, :, cols].rearrange("p t (k i) -> p k t i", i=2),
                 op=MULT,
             )
-
-        def apply_signs():
-            h_view = h_bf[0, 0][:].rearrange("p (j t) -> p j t", t=PACK)
-            nc.vector.tensor_tensor(out=h_view, in0=h_view, in1=signs[:].to_broadcast([P, HALF, PACK]), op=MULT)
 
         def quantise_h(jh, b, c0, c1):
             nc.vector.quantize_mx(
@@ -212,16 +198,20 @@ def tile_list_fatigue_brand_affinity_kernel(
 
         wc_words, wc_scales = {}, {}
 
-        def quantise_wc(b):
-            wc_bf = kept([P, N, PACK], BF16, f"wc_bf{b}")
+        wc_bf = {}
+
+        def round_wc(b):
+            wc_bf[b] = kept([P, N, PACK], BF16, f"wc_bf{b}")
             nc.scalar.copy(
-                out=wc_bf[:].rearrange("p (k i) t -> p k t i", i=4),
+                out=wc_bf[b][:].rearrange("p (k i) t -> p k t i", i=4),
                 in_=weights["wc_raw"][:, b, :, :].rearrange("p t (k i) -> p k t i", i=4),
             )
+
+        def quantise_wc(b):
             wc_words[b] = kept([P, N], U32, f"wc_words{b}")
             wc_scales[b] = kept([P, N], U8, f"wc_scales{b}")
             nc.vector.quantize_mx(
-                out=wc_words[b][:].bitcast(FP8X4), scales=wc_scales[b][:], in_=wc_bf[:].rearrange("p n t -> p (n t)")
+                out=wc_words[b][:].bitcast(FP8X4), scales=wc_scales[b][:], in_=wc_bf[b][:].rearrange("p n t -> p (n t)")
             )
 
         acc = {}
@@ -286,33 +276,38 @@ def tile_list_fatigue_brand_affinity_kernel(
         pick_prod_scales()
         load_base_words()
         order_prod_scales()
-        split_margins()
         pick_prod_words(FAT, 0)
         pick_prod_words(FAT, 1)
         load_wc()
         pick_shop_scales(1)
         load_base_scales()
-        damping(0, 0)
+        square(0)
+        roots(0, 8)
         gather(v2_words[AFF][:], shop_words[AFF], idx2[:])
-        damping(0, 1)
+        for k in range(4):
+            weigh(k)
         pick_prod_words(AFF, 0)
         pick_prod_words(AFF, 1)
+        round_wc(0)
+        roots(8, 12)
         for c in range(4):
             affinity(0, 0, c)
-        damping(1, 0)
-        apply_signs()
-        quantise_wc(0)
+            weigh(4 + c)
+        round_wc(1)
         quantise_h(0, 0, 0, 4)
+        roots(12, 16)
         for c in range(4):
             affinity(0, 1, c)
-        quantise_wc(1)
-        damping(1, 1)
+            weigh(8 + c)
         quantise_h(0, 1, 0, 4)
+        quantise_wc(0)
+        quantise_wc(1)
         for c in range(4):
             affinity(1, 0, c)
+            weigh(12 + c)
             brands_wide(c)
-        affinity(1, 1, 0)
         quantise_h(1, 0, 0, 4)
+        affinity(1, 1, 0)
         for c in range(4):
             store_wide(c)
             brands_narrow(0, c)

@@ -20,6 +20,7 @@ P = 128
 PACK = 4
 HALF = 512
 AFF, FAT = 0, 1
+GROUPS = ((0, 512), (512, 256), (768, 256))
 
 
 def tile_list_fatigue_brand_affinity_kernel(
@@ -91,7 +92,6 @@ def tile_list_fatigue_brand_affinity_kernel(
 
         def load_base_scales():
             weights["base_scales"] = kept([P, 2, N], U8, "base_scales", tag="shop_scales")
-            nc.vector.memset(weights["base_scales"][:].rearrange("p b n -> p (b n)").bitcast(I32), 0)
             for q in range(4):
                 nc.sync.dma_start(
                     out=weights["base_scales"][32 * q : 32 * q + 4, :, :].bitcast(I32),
@@ -130,75 +130,76 @@ def tile_list_fatigue_brand_affinity_kernel(
                 in_=listed_scales[:].rearrange("p (b c i t) -> p b c t i", b=2, t=PACK, i=16),
             )
 
-        def table_product(dst, a, b, t, jh, cols):
-            slot = slice(t * P, (t + 1) * P)
-            shoppers = slice(jh * HALF + cols.start, jh * HALF + cols.stop)
+        def table_product(dst, a, b, t, j0, width):
+            jh, first = divmod(j0, HALF)
             nc.tensor.matmul_mx(
                 out=dst,
-                lhsT=v_words[a, b][:, slot].bitcast(FP8X4),
+                lhsT=v_words[a, b][:, t * P : (t + 1) * P].bitcast(FP8X4),
                 lhsT_scale=v_scales[4 * a :, b * HALF + t * P : b * HALF + (t + 1) * P],
-                rhs=v2_words[a][:, shoppers].bitcast(FP8X4),
-                rhs_scale=v2_scales[jh][8 + 4 * a :, cols],
+                rhs=v2_words[a][:, j0 : j0 + width].bitcast(FP8X4),
+                rhs_scale=v2_scales[jh][8 + 4 * a :, first : first + width],
                 start=True,
                 stop=True,
             )
 
-        quarters = [(jh, b) for jh in range(2) for b in range(2)]
-        damp = {q: kept([P, PACK, HALF], F32, f"damp{q[0]}{q[1]}") for q in quarters}
+        damp, h_bf, h_words, h_scales = {}, {}, {}, {}
+        slabs = []
+        for g, (j0, width) in enumerate(GROUPS):
+            for b in range(2):
+                damp[g, b] = kept([P, PACK, width], F32, f"damp{g}{b}")
+                h_bf[g, b] = kept([P, width * PACK], BF16, f"h_bf{g}{b}")
+                h_words[g, b] = kept([P, width], U32, f"h_words{g}{b}")
+                h_scales[g, b] = kept([P, width], U8, f"h_scales{g}{b}")
+                slots = HALF // width
+                slabs.extend((g, b, t0, slots) for t0 in range(0, PACK, slots))
         squared = {}
 
         def square(k):
-            (jh, b), t = quarters[k // PACK], k % PACK
-            f_bank = psum.tile([P, HALF], F32, name="f_bank")
-            table_product(f_bank[:], FAT, b, t, jh, slice(0, HALF))
-            squared[k] = ring.tile([P, HALF], F32, name="squared")
+            g, b, t0, slots = slabs[k]
+            j0, width = GROUPS[g]
+            f_bank = psum.tile([P, slots, width], F32, name="f_bank")
+            for s in range(slots):
+                table_product(f_bank[:, s, :], FAT, b, t0 + s, j0, width)
+            squared[k] = ring.tile([P, slots, width], F32, name="squared")
             nc.scalar.activation(out=squared[k][:], in_=f_bank[:], func=ACT.Square)
 
         def root(k):
-            weight = damp[quarters[k // PACK]][:, k % PACK, :]
-            nc.scalar.activation(out=weight, in_=squared[k][:], func=ACT.Abs_reciprocal_sqrt, bias=1.0)
-
-        def weigh(k):
-            (jh, b), t = quarters[k // PACK], k % PACK
-            weight = damp[jh, b][:, t, :]
-            nc.vector.scalar_tensor_tensor(
-                out=weight, in0=weight, scalar=margins[:, b, t : t + 1], in1=weight, op0=MULT, op1=MULT
+            g, b, t0, slots = slabs[k]
+            nc.scalar.activation(
+                out=damp[g, b][:, t0 : t0 + slots, :], in_=squared[k][:], func=ACT.Abs_reciprocal_sqrt, bias=1.0
             )
 
         def roots(k0, k1):
             for k in range(k0, k1):
-                if k + 1 < 4 * PACK:
+                if k + 1 < len(slabs):
                     square(k + 1)
                 root(k)
 
-        h_bf, h_words, h_scales = {}, {}, {}
+        def weigh(g, b, t):
+            weight = damp[g, b][:, t, :]
+            nc.vector.scalar_tensor_tensor(
+                out=weight, in0=weight, scalar=margins[:, b, t : t + 1], in1=weight, op0=MULT, op1=MULT
+            )
 
-        def affinity(jh, b, c):
-            if c == 0:
-                h_bf[jh, b] = kept([P, HALF * PACK], BF16, f"h_bf{jh}{b}")
-                h_words[jh, b] = kept([P, HALF], U32, f"h_words{jh}{b}")
-                h_scales[jh, b] = kept([P, HALF], U8, f"h_scales{jh}{b}")
-            cols = slice(c * P, (c + 1) * P)
-            a_bank = psum.tile([P, PACK, P], F32, name="f_bank" if (jh, b) == (1, 1) and c % 2 == 1 else "a_bank")
+        def affinity(g, b, c):
+            a_bank = psum.tile([P, PACK, P], F32, name="a_bank")
             for t in range(PACK):
-                table_product(a_bank[:, t, :], AFF, b, t, jh, cols)
+                table_product(a_bank[:, t, :], AFF, b, t, GROUPS[g][0] + c * P, P)
             nc.vector.tensor_tensor(
-                out=h_bf[jh, b][:, c * HALF : (c + 1) * HALF].rearrange("p (k i t) -> p k t i", i=2, t=PACK),
+                out=h_bf[g, b][:, c * HALF : (c + 1) * HALF].rearrange("p (k i t) -> p k t i", i=2, t=PACK),
                 in0=a_bank[:].rearrange("p t (k i) -> p k t i", i=2),
-                in1=damp[jh, b][:, :, cols].rearrange("p t (k i) -> p k t i", i=2),
+                in1=damp[g, b][:, :, c * P : (c + 1) * P].rearrange("p t (k i) -> p k t i", i=2),
                 op=MULT,
             )
 
-        def quantise_h(jh, b, c0, c1):
+        def quantise_h(g, b, c0, c1):
             nc.vector.quantize_mx(
-                out=h_words[jh, b][:, c0 * P : c1 * P].bitcast(FP8X4),
-                scales=h_scales[jh, b][:, c0 * P : c1 * P],
-                in_=h_bf[jh, b][:, c0 * HALF : c1 * HALF],
+                out=h_words[g, b][:, c0 * P : c1 * P].bitcast(FP8X4),
+                scales=h_scales[g, b][:, c0 * P : c1 * P],
+                in_=h_bf[g, b][:, c0 * HALF : c1 * HALF],
             )
 
-        wc_words, wc_scales = {}, {}
-
-        wc_bf = {}
+        wc_bf, wc_words, wc_scales = {}, {}, {}
 
         def round_wc(b):
             wc_bf[b] = kept([P, N, PACK], BF16, f"wc_bf{b}")
@@ -216,60 +217,44 @@ def tile_list_fatigue_brand_affinity_kernel(
 
         acc = {}
 
-        def brand_pair(dst, jh, b, nt, cols, start, stop):
-            brands = slice(nt * P, (nt + 1) * P)
-            nc.tensor.matmul_mx(
-                out=dst,
-                lhsT=weights["base_words"][:, b, 2 * nt * P : 2 * (nt + 1) * P].bitcast(FP4X4),
-                lhsT_scale=weights["base_scales"][:, b, brands],
-                rhs=h_words[jh, b][:, cols].bitcast(FP8X4),
-                rhs_scale=h_scales[jh, b][:, cols],
-                start=start,
-                stop=False,
-            )
-            nc.tensor.matmul_mx(
-                out=dst,
-                lhsT=wc_words[b][:, brands].bitcast(FP8X4),
-                lhsT_scale=wc_scales[b][:, brands],
-                rhs=h_words[jh, b][:, cols].bitcast(FP8X4),
-                rhs_scale=h_scales[jh, b][:, cols],
-                start=False,
-                stop=stop,
-            )
-
-        def brands_wide(nt):
-            acc[0, nt] = psum_out.tile([P, HALF], F32, name=f"acc{nt}")
-            for b in range(2):
-                brand_pair(acc[0, nt][:], 0, b, nt, slice(0, HALF), b == 0, b == 1)
-
-        def narrow_parts(c):
-            return ((0, 4),) if c < 3 else ((0, 2), (2, 4))
-
-        def brands_narrow(b, c):
-            for lo, hi in narrow_parts(c):
-                if b == 0 and lo == 0:
-                    acc[1, c, lo] = psum_out.tile([P, hi - lo, P], F32, name=f"acc{c}")
-                elif b == 0:
-                    acc[1, c, lo] = psum.tile([P, hi - lo, P], F32, name="a_bank")
-                for nt in range(lo, hi):
-                    brand_pair(
-                        acc[1, c, lo][:, nt - lo, :], 1, b, nt, slice(c * P, (c + 1) * P),
-                        b == 0 and nt == lo, b == 1 and nt == hi - 1,
-                    )
-
-        def store_wide(nt):
-            staged = ring.tile([P, HALF], F32, name="staged", bufs=4)
-            nc.scalar.copy(out=staged[:], in_=acc[0, nt][:])
-            nc.sync.dma_start(out=out[nt * P : (nt + 1) * P, 0:HALF], in_=staged[:])
-
-        def store_narrow(c):
-            for lo, hi in narrow_parts(c):
-                staged = kept([P, hi - lo, P], F32, f"staged{c}{lo}")
-                (nc.scalar.copy if lo == 0 else nc.vector.tensor_copy)(out=staged[:], in_=acc[1, c, lo][:])
-                nc.sync.dma_start(
-                    out=out[lo * P : hi * P, HALF + c * P : HALF + (c + 1) * P].rearrange("(nt p) j -> p nt j", p=P),
-                    in_=staged[:],
+        def brands(bank, b, pool, name):
+            g, first, width, lo, hi = bank
+            if b == 0:
+                acc[bank] = pool.tile([P, hi - lo, width], F32, name=name)
+            cols = slice(first, first + width)
+            for nt in range(lo, hi):
+                tile = slice(nt * P, (nt + 1) * P)
+                nc.tensor.matmul_mx(
+                    out=acc[bank][:, nt - lo, :],
+                    lhsT=weights["base_words"][:, b, 2 * nt * P : 2 * (nt + 1) * P].bitcast(FP4X4),
+                    lhsT_scale=weights["base_scales"][:, b, tile],
+                    rhs=h_words[g, b][:, cols].bitcast(FP8X4),
+                    rhs_scale=h_scales[g, b][:, cols],
+                    start=b == 0 and nt == lo,
+                    stop=False,
                 )
+                nc.tensor.matmul_mx(
+                    out=acc[bank][:, nt - lo, :],
+                    lhsT=wc_words[b][:, tile].bitcast(FP8X4),
+                    lhsT_scale=wc_scales[b][:, tile],
+                    rhs=h_words[g, b][:, cols].bitcast(FP8X4),
+                    rhs_scale=h_scales[g, b][:, cols],
+                    start=False,
+                    stop=b == 1 and nt == hi - 1,
+                )
+
+        def store(bank, copy):
+            g, first, width, lo, hi = bank
+            j0 = GROUPS[g][0] + first
+            staged = kept([P, hi - lo, width], F32, f"staged{g}_{first}_{lo}")
+            copy(out=staged[:], in_=acc[bank][:])
+            nc.sync.dma_start(
+                out=out[lo * P : hi * P, j0 : j0 + width].rearrange("(nt p) j -> p nt j", p=P), in_=staged[:]
+            )
+
+        wide = [(0, 0, HALF, nt, nt + 1) for nt in range(4)]
+        middle = [(1, 0, 2 * P, 0, 2), (1, 0, 2 * P, 2, 4)]
+        last = [(2, 0, P, 0, 4), (2, P, P, 0, 2), (2, P, P, 2, 4)]
 
         gather(v2_words[FAT][:], shop_words[FAT], idx2[:])
         pick_shop_scales(0)
@@ -282,38 +267,64 @@ def tile_list_fatigue_brand_affinity_kernel(
         pick_shop_scales(1)
         load_base_scales()
         square(0)
-        roots(0, 8)
+        roots(0, 6)
+        round_wc(0)
+        roots(6, 8)
+        round_wc(1)
         gather(v2_words[AFF][:], shop_words[AFF], idx2[:])
-        for k in range(4):
-            weigh(k)
+        for t in range(PACK):
+            weigh(0, 0, t)
         pick_prod_words(AFF, 0)
         pick_prod_words(AFF, 1)
-        round_wc(0)
-        roots(8, 12)
         for c in range(4):
             affinity(0, 0, c)
-            weigh(4 + c)
-        round_wc(1)
+            weigh(0, 1, c)
         quantise_h(0, 0, 0, 4)
-        roots(12, 16)
+        quantise_wc(0)
+        roots(8, 12)
         for c in range(4):
             affinity(0, 1, c)
-            weigh(8 + c)
-        quantise_h(0, 1, 0, 4)
-        quantise_wc(0)
+            brands(wide[c], 0, psum_out, f"acc{c}")
         quantise_wc(1)
-        for c in range(4):
+        quantise_h(0, 1, 0, 4)
+        for t in range(PACK):
+            weigh(1, 0, t)
+        roots(12, 14)
+        for c in range(2):
             affinity(1, 0, c)
-            weigh(12 + c)
-            brands_wide(c)
-        quantise_h(1, 0, 0, 4)
-        affinity(1, 1, 0)
-        for c in range(4):
-            store_wide(c)
-            brands_narrow(0, c)
-        for c in range(4):
-            if c < 3:
-                affinity(1, 1, c + 1)
-            quantise_h(1, 1, c, c + 1)
-            brands_narrow(1, c)
-            store_narrow(c)
+            for t in (2 * c, 2 * c + 1):
+                weigh(1, 1, t)
+                brands(wide[t], 1, psum_out, "")
+        quantise_h(1, 0, 0, 2)
+        for nt in range(2):
+            store(wide[nt], nc.scalar.copy)
+        roots(14, 16)
+        for c in range(2):
+            affinity(1, 1, c)
+            brands(middle[c], 0, psum_out, f"acc{c}")
+            for t in (2 * c, 2 * c + 1):
+                weigh(2, 0, t)
+        quantise_h(1, 1, 0, 2)
+        for nt in range(2, 4):
+            store(wide[nt], nc.scalar.copy)
+        for c in range(2):
+            affinity(2, 0, c)
+            brands(middle[c], 1, psum_out, "")
+            for t in (2 * c, 2 * c + 1):
+                weigh(2, 1, t)
+        quantise_h(2, 0, 0, 2)
+        for c in range(2):
+            store(middle[c], nc.scalar.copy)
+        affinity(2, 1, 0)
+        affinity(2, 1, 1)
+        brands(last[0], 0, psum_out, "acc2")
+        brands(last[1], 0, psum_out, "acc3")
+        brands(last[2], 0, psum, "f_bank")
+        quantise_h(2, 1, 0, 1)
+        brands(last[0], 1, psum_out, "")
+        quantise_h(2, 1, 1, 2)
+        store(last[0], nc.scalar.copy)
+        brands(last[1], 1, psum_out, "")
+        brands(last[2], 1, psum, "")
+        store(last[1], nc.scalar.copy)
+        store(last[2], nc.vector.tensor_copy)

@@ -40,8 +40,8 @@ def tile_list_fatigue_brand_affinity_kernel(
 
         idx = lists.tile([P, S // 16], U16, name="idx")
         idx2 = lists.tile([P, S2 // 16], U16, name="idx2")
-        prod_fatigue = reuse.tile([P, T + HALF // 4], U32, name="prod_fatigue", align_bytes=64, offset=0)
-        prod_words = {AFF: kept([P, T], U32, "prod_affinity")[:], FAT: prod_fatigue[:, 0:T]}
+        prod_fatigue = reuse.tile([P, T], U32, name="prod_fatigue", align_bytes=64, offset=0)
+        prod_words = {AFF: kept([P, T], U32, "prod_affinity")[:], FAT: prod_fatigue[:]}
         shop_words = [kept([P, T2], U32, f"shop_words{a}")[:] for a in range(2)]
         prod_scales = kept([P, T], U8, "prod_scales")
         shop_scales = kept([P, T2], U8, "shop_scales")
@@ -102,7 +102,7 @@ def tile_list_fatigue_brand_affinity_kernel(
             nc.vector.tensor_copy(out=picked, in_=window.indirect(offsets))
 
         v2_words = [kept([P, S2], U32, f"v2_words{a}") for a in range(2)]
-        v2_scales = {}
+        v2_scales = kept([P, S2], U8, "v2_scales")
         v_words = {(a, b): kept([P, HALF], U32, f"v_words{a}{b}") for a in range(2) for b in range(2)}
         listed_scales = kept([P, S], U8, "listed_scales")
         v_scales = kept([P, S], U8, "v_scales")
@@ -117,12 +117,8 @@ def tile_list_fatigue_brand_affinity_kernel(
         def pick_prod_scales():
             gather(listed_scales[:], prod_scales[:], idx[:])
 
-        def pick_shop_scales(jh):
-            if jh == 0:
-                v2_scales[jh] = kept([P, HALF], U8, "v2_scales0")
-            else:
-                v2_scales[jh] = reuse.tile([P, HALF], U8, name="v2_scales1", align_bytes=64, offset=4 * T)
-            gather(v2_scales[jh][:], shop_scales[:], idx2[:, jh * HALF // 16 : (jh + 1) * HALF // 16])
+        def pick_shop_scales():
+            gather(v2_scales[:], shop_scales[:], idx2[:])
 
         def order_prod_scales():
             nc.vector.tensor_copy(
@@ -131,13 +127,12 @@ def tile_list_fatigue_brand_affinity_kernel(
             )
 
         def table_product(dst, a, b, t, j0, width):
-            jh, first = divmod(j0, HALF)
             nc.tensor.matmul_mx(
                 out=dst,
                 lhsT=v_words[a, b][:, t * P : (t + 1) * P].bitcast(FP8X4),
                 lhsT_scale=v_scales[4 * a :, b * HALF + t * P : b * HALF + (t + 1) * P],
                 rhs=v2_words[a][:, j0 : j0 + width].bitcast(FP8X4),
-                rhs_scale=v2_scales[jh][8 + 4 * a :, first : first + width],
+                rhs_scale=v2_scales[8 + 4 * a :, j0 : j0 + width],
                 start=True,
                 stop=True,
             )
@@ -257,14 +252,13 @@ def tile_list_fatigue_brand_affinity_kernel(
         last = [(2, 0, P, 0, 4), (2, P, P, 0, 2), (2, P, P, 2, 4)]
 
         gather(v2_words[FAT][:], shop_words[FAT], idx2[:])
-        pick_shop_scales(0)
+        pick_shop_scales()
         pick_prod_scales()
         load_base_words()
         order_prod_scales()
         pick_prod_words(FAT, 0)
         pick_prod_words(FAT, 1)
         load_wc()
-        pick_shop_scales(1)
         load_base_scales()
         square(0)
         roots(0, 6)

@@ -20,6 +20,7 @@ P = 128
 PACK = 4
 HALF = 512
 AFF, FAT = 0, 1
+WC_HALF_BYTES = PACK * N * 4
 GROUPS = ((0, 512), (512, 256), (768, 256))
 
 
@@ -77,10 +78,12 @@ def tile_list_fatigue_brand_affinity_kernel(
         weights = {}
 
         def load_wc():
-            weights["wc_raw"] = reuse.tile([P, 2, PACK, N], F32, name="wc_raw", align_bytes=64, offset=0)
             for b in range(2):
+                weights["wc_raw", b] = reuse.tile(
+                    [P, PACK, N], F32, name=f"wc_raw{b}", align_bytes=64, offset=b * WC_HALF_BYTES
+                )
                 nc.sync.dma_start(
-                    out=weights["wc_raw"][:, b, :, :],
+                    out=weights["wc_raw", b][:],
                     in_=wc[b * HALF : (b + 1) * HALF, :].rearrange("(p t) n -> p t n", t=PACK),
                 )
 
@@ -103,15 +106,15 @@ def tile_list_fatigue_brand_affinity_kernel(
 
         v2_words = [kept([P, S2], U32, f"v2_words{a}") for a in range(2)]
         v2_scales = kept([P, S2], U8, "v2_scales")
-        v_words = {(a, b): kept([P, HALF], U32, f"v_words{a}{b}") for a in range(2) for b in range(2)}
+        v_words = [kept([P, 2, HALF], U32, f"v_words{a}") for a in range(2)]
         listed_scales = kept([P, S], U8, "listed_scales")
         v_scales = kept([P, S], U8, "v_scales")
 
-        def pick_prod_words(a, b):
+        def pick_prod_words(a, b0, b1):
             gather(
-                v_words[a, b][:].rearrange("p (t s) -> p s t", t=PACK),
+                v_words[a][:, b0:b1, :].rearrange("p b (t s) -> p b s t", t=PACK),
                 prod_words[a],
-                idx[:, b * HALF // 16 : (b + 1) * HALF // 16],
+                idx[:, b0 * HALF // 16 : b1 * HALF // 16],
             )
 
         def pick_prod_scales():
@@ -129,7 +132,7 @@ def tile_list_fatigue_brand_affinity_kernel(
         def table_product(dst, a, b, t, j0, width):
             nc.tensor.matmul_mx(
                 out=dst,
-                lhsT=v_words[a, b][:, t * P : (t + 1) * P].bitcast(FP8X4),
+                lhsT=v_words[a][:, b, t * P : (t + 1) * P].bitcast(FP8X4),
                 lhsT_scale=v_scales[4 * a :, b * HALF + t * P : b * HALF + (t + 1) * P],
                 rhs=v2_words[a][:, j0 : j0 + width].bitcast(FP8X4),
                 rhs_scale=v2_scales[8 + 4 * a :, j0 : j0 + width],
@@ -137,11 +140,12 @@ def tile_list_fatigue_brand_affinity_kernel(
                 stop=True,
             )
 
+        inverse_root = {}
         damp, h_bf, h_words, h_scales = {}, {}, {}, {}
         slabs = []
         for g, (j0, width) in enumerate(GROUPS):
             for b in range(2):
-                damp[g, b] = kept([P, PACK, width], F32, f"damp{g}{b}")
+                inverse_root[g, b] = damp[g, b] = kept([P, PACK, width], F32, f"damp{g}{b}")
                 h_bf[g, b] = kept([P, width * PACK], BF16, f"h_bf{g}{b}")
                 h_words[g, b] = kept([P, width], U32, f"h_words{g}{b}")
                 h_scales[g, b] = kept([P, width], U8, f"h_scales{g}{b}")
@@ -155,13 +159,18 @@ def tile_list_fatigue_brand_affinity_kernel(
             f_bank = psum.tile([P, slots, width], F32, name="f_bank")
             for s in range(slots):
                 table_product(f_bank[:, s, :], FAT, b, t0 + s, j0, width)
-            squared[k] = ring.tile([P, slots, width], F32, name="squared")
+            if k in (9, 10):
+                squared[k] = reuse.tile(
+                    [P, slots, width], F32, name=f"squared{k}", align_bytes=64, offset=(k - 9) * WC_HALF_BYTES
+                )
+            else:
+                squared[k] = ring.tile([P, slots, width], F32, name="squared")
             nc.scalar.activation(out=squared[k][:], in_=f_bank[:], func=ACT.Square)
 
         def root(k):
             g, b, t0, slots = slabs[k]
             nc.scalar.activation(
-                out=damp[g, b][:, t0 : t0 + slots, :], in_=squared[k][:], func=ACT.Abs_reciprocal_sqrt, bias=1.0
+                out=inverse_root[g, b][:, t0 : t0 + slots, :], in_=squared[k][:], func=ACT.Abs_reciprocal_sqrt, bias=1.0
             )
 
         def roots(k0, k1):
@@ -171,13 +180,13 @@ def tile_list_fatigue_brand_affinity_kernel(
                 root(k)
 
         def weigh(g, b, t):
-            weight = damp[g, b][:, t, :]
+            root_t = inverse_root[g, b][:, t, :]
             nc.vector.scalar_tensor_tensor(
-                out=weight, in0=weight, scalar=margins[:, b, t : t + 1], in1=weight, op0=MULT, op1=MULT
+                out=damp[g, b][:, t, :], in0=root_t, scalar=margins[:, b, t : t + 1], in1=root_t, op0=MULT, op1=MULT
             )
 
         def affinity(g, b, c):
-            a_bank = psum.tile([P, PACK, P], F32, name="a_bank")
+            a_bank = psum.tile([P, PACK, P], F32, name="f_bank" if (g, b, c) == (2, 1, 0) else "a_bank")
             for t in range(PACK):
                 table_product(a_bank[:, t, :], AFF, b, t, GROUPS[g][0] + c * P, P)
             nc.vector.tensor_tensor(
@@ -200,7 +209,7 @@ def tile_list_fatigue_brand_affinity_kernel(
             wc_bf[b] = kept([P, N, PACK], BF16, f"wc_bf{b}")
             nc.scalar.copy(
                 out=wc_bf[b][:].rearrange("p (k i) t -> p k t i", i=4),
-                in_=weights["wc_raw"][:, b, :, :].rearrange("p t (k i) -> p k t i", i=4),
+                in_=weights["wc_raw", b][:].rearrange("p t (k i) -> p k t i", i=4),
             )
 
         def quantise_wc(b):
@@ -238,12 +247,12 @@ def tile_list_fatigue_brand_affinity_kernel(
                     stop=b == 1 and nt == hi - 1,
                 )
 
-        def store(bank, copy):
+        def store(bank, copy, queue=nc.sync):
             g, first, width, lo, hi = bank
             j0 = GROUPS[g][0] + first
             staged = kept([P, hi - lo, width], F32, f"staged{g}_{first}_{lo}")
             copy(out=staged[:], in_=acc[bank][:])
-            nc.sync.dma_start(
+            queue.dma_start(
                 out=out[lo * P : hi * P, j0 : j0 + width].rearrange("(nt p) j -> p nt j", p=P), in_=staged[:]
             )
 
@@ -256,26 +265,26 @@ def tile_list_fatigue_brand_affinity_kernel(
         pick_prod_scales()
         load_base_words()
         order_prod_scales()
-        pick_prod_words(FAT, 0)
-        pick_prod_words(FAT, 1)
+        pick_prod_words(FAT, 0, 1)
+        pick_prod_words(FAT, 1, 2)
         load_wc()
         load_base_scales()
         square(0)
-        roots(0, 6)
+        roots(0, 8)
         round_wc(0)
-        roots(6, 8)
+        roots(8, 9)
         round_wc(1)
         gather(v2_words[AFF][:], shop_words[AFF], idx2[:])
         for t in range(PACK):
             weigh(0, 0, t)
-        pick_prod_words(AFF, 0)
-        pick_prod_words(AFF, 1)
+        pick_prod_words(AFF, 0, 2)
+        damp[0, 1] = kept([P, PACK, HALF], F32, "damp_late", tag="prod_affinity")
         for c in range(4):
             affinity(0, 0, c)
             weigh(0, 1, c)
         quantise_h(0, 0, 0, 4)
         quantise_wc(0)
-        roots(8, 12)
+        roots(9, 12)
         for c in range(4):
             affinity(0, 1, c)
             brands(wide[c], 0, psum_out, f"acc{c}")
@@ -320,5 +329,5 @@ def tile_list_fatigue_brand_affinity_kernel(
         store(last[0], nc.scalar.copy)
         brands(last[1], 1, psum_out, "")
         brands(last[2], 1, psum, "")
-        store(last[1], nc.scalar.copy)
+        store(last[1], nc.scalar.copy, nc.scalar)
         store(last[2], nc.vector.tensor_copy)

@@ -20,6 +20,8 @@ P = 128
 PACK = 4
 HALF = 512
 AFF, FAT = 0, 1
+SCALAR_SQUARES = (6, 7)
+BASE, CAMPAIGN = 0, 1
 WC_HALF_BYTES = PACK * N * 4
 GROUPS = ((0, 512), (512, 256), (768, 256))
 
@@ -46,7 +48,7 @@ def tile_list_fatigue_brand_affinity_kernel(
         shop_words = [kept([P, T2], U32, f"shop_words{a}")[:] for a in range(2)]
         prod_scales = kept([P, T], U8, "prod_scales")
         shop_scales = kept([P, T2], U8, "shop_scales")
-        margins = kept([P, 2, PACK], F32, "margins")
+        margins = kept([P, 2, 2 * PACK], F32, "margins")
 
         def load_words(queue, tile, words):
             queue.dma_start(out=tile.bitcast(I32), in_=words.rearrange("p t i -> p (t i)").bitcast(I32))
@@ -71,7 +73,7 @@ def tile_list_fatigue_brand_affinity_kernel(
         load_scales(nc.sync, shop_scales, tab2_scales, 8)
         load_scales(nc.sync, prod_scales, tab_scales, 0)
         load_words(nc.sync, prod_words[FAT], tab_words[FAT])
-        nc.sync.dma_start(out=margins[:], in_=margin.rearrange("(b p t) -> p b t", b=2, t=PACK))
+        nc.sync.dma_start(out=margins[:, :, 0:PACK], in_=margin.rearrange("(b p t) -> p b t", b=2, t=PACK))
         load_words(nc.sync, shop_words[AFF], tab2_words[AFF])
         load_words(nc.sync, prod_words[AFF], tab_words[AFF])
 
@@ -159,12 +161,7 @@ def tile_list_fatigue_brand_affinity_kernel(
             f_bank = psum.tile([P, slots, width], F32, name="f_bank")
             for s in range(slots):
                 table_product(f_bank[:, s, :], FAT, b, t0 + s, j0, width)
-            if k in (9, 10):
-                squared[k] = reuse.tile(
-                    [P, slots, width], F32, name=f"squared{k}", align_bytes=64, offset=(k - 9) * WC_HALF_BYTES
-                )
-            else:
-                squared[k] = ring.tile([P, slots, width], F32, name="squared")
+            squared[k] = ring.tile([P, slots, width], F32, name="squared")
             nc.scalar.activation(out=squared[k][:], in_=f_bank[:], func=ACT.Square)
 
         def root(k):
@@ -173,17 +170,28 @@ def tile_list_fatigue_brand_affinity_kernel(
                 out=inverse_root[g, b][:, t0 : t0 + slots, :], in_=squared[k][:], func=ACT.Abs_reciprocal_sqrt, bias=1.0
             )
 
+        def square_root(k):
+            g, b, t0, slots = slabs[k]
+            root_k = inverse_root[g, b][:, t0 : t0 + slots, :]
+            nc.scalar.activation(out=root_k, in_=root_k, func=ACT.Square)
+
         def roots(k0, k1):
             for k in range(k0, k1):
                 if k + 1 < len(slabs):
                     square(k + 1)
                 root(k)
+                if k - 1 in SCALAR_SQUARES:
+                    square_root(k - 1)
 
         def weigh(g, b, t):
             root_t = inverse_root[g, b][:, t, :]
-            nc.vector.scalar_tensor_tensor(
-                out=damp[g, b][:, t, :], in0=root_t, scalar=margins[:, b, t : t + 1], in1=root_t, op0=MULT, op1=MULT
-            )
+            if any(slabs[k][0:2] == (g, b) and 0 <= t - slabs[k][2] < slabs[k][3] for k in SCALAR_SQUARES):
+                nc.vector.tensor_scalar_mul(out=damp[g, b][:, t, :], in0=root_t, scalar1=margins[:, b, t : t + 1])
+            else:
+                nc.vector.scalar_tensor_tensor(
+                    out=damp[g, b][:, t, :], in0=root_t, scalar=margins[:, b, t : t + 1], in1=root_t,
+                    op0=MULT, op1=MULT,
+                )
 
         def affinity(g, b, c):
             a_bank = psum.tile([P, PACK, P], F32, name="f_bank" if (g, b, c) == (2, 1, 0) else "a_bank")
@@ -221,30 +229,30 @@ def tile_list_fatigue_brand_affinity_kernel(
 
         acc = {}
 
-        def brands(bank, b, pool, name):
+        def open_bank(bank, pool, name):
             g, first, width, lo, hi = bank
-            if b == 0:
-                acc[bank] = pool.tile([P, hi - lo, width], F32, name=name)
+            acc[bank] = pool.tile([P, hi - lo, width], F32, name=name)
+
+        def brands(bank, terms, opens=False, closes=False):
+            g, first, width, lo, hi = bank
             cols = slice(first, first + width)
-            for nt in range(lo, hi):
+            steps = [(nt, kind, b) for nt in range(lo, hi) for kind, b in terms]
+            for n, (nt, kind, b) in enumerate(steps):
                 tile = slice(nt * P, (nt + 1) * P)
+                if kind == BASE:
+                    codes = weights["base_words"][:, b, 2 * nt * P : 2 * (nt + 1) * P].bitcast(FP4X4)
+                    scales = weights["base_scales"][:, b, tile]
+                else:
+                    codes = wc_words[b][:, tile].bitcast(FP8X4)
+                    scales = wc_scales[b][:, tile]
                 nc.tensor.matmul_mx(
                     out=acc[bank][:, nt - lo, :],
-                    lhsT=weights["base_words"][:, b, 2 * nt * P : 2 * (nt + 1) * P].bitcast(FP4X4),
-                    lhsT_scale=weights["base_scales"][:, b, tile],
+                    lhsT=codes,
+                    lhsT_scale=scales,
                     rhs=h_words[g, b][:, cols].bitcast(FP8X4),
                     rhs_scale=h_scales[g, b][:, cols],
-                    start=b == 0 and nt == lo,
-                    stop=False,
-                )
-                nc.tensor.matmul_mx(
-                    out=acc[bank][:, nt - lo, :],
-                    lhsT=wc_words[b][:, tile].bitcast(FP8X4),
-                    lhsT_scale=wc_scales[b][:, tile],
-                    rhs=h_words[g, b][:, cols].bitcast(FP8X4),
-                    rhs_scale=h_scales[g, b][:, cols],
-                    start=False,
-                    stop=b == 1 and nt == hi - 1,
+                    start=opens and n == 0,
+                    stop=closes and n == len(steps) - 1,
                 )
 
         def store(bank, copy, queue=nc.sync):
@@ -269,10 +277,14 @@ def tile_list_fatigue_brand_affinity_kernel(
         pick_prod_words(FAT, 1, 2)
         load_wc()
         load_base_scales()
-        square(0)
-        roots(0, 8)
+        for k in (0, 2):
+            square(k)
+            square(k + 1)
+            root(k)
+            root(k + 1)
+        square(4)
+        roots(4, 12)
         round_wc(0)
-        roots(8, 9)
         round_wc(1)
         gather(v2_words[AFF][:], shop_words[AFF], idx2[:])
         for t in range(PACK):
@@ -283,51 +295,52 @@ def tile_list_fatigue_brand_affinity_kernel(
             affinity(0, 0, c)
             weigh(0, 1, c)
         quantise_h(0, 0, 0, 4)
-        quantise_wc(0)
-        roots(9, 12)
         for c in range(4):
             affinity(0, 1, c)
-            brands(wide[c], 0, psum_out, f"acc{c}")
-        quantise_wc(1)
+            weigh(1, 0, c)
+            open_bank(wide[c], psum_out, f"acc{c}")
+            brands(wide[c], [(BASE, 0)], opens=True)
         quantise_h(0, 1, 0, 4)
-        for t in range(PACK):
-            weigh(1, 0, t)
-        roots(12, 14)
+        quantise_wc(0)
+        roots(12, 16)
         for c in range(2):
             affinity(1, 0, c)
             for t in (2 * c, 2 * c + 1):
                 weigh(1, 1, t)
-                brands(wide[t], 1, psum_out, "")
+                brands(wide[t], [(BASE, 1), (CAMPAIGN, 0)])
+            if c == 0:
+                quantise_wc(1)
         quantise_h(1, 0, 0, 2)
-        for nt in range(2):
-            store(wide[nt], nc.scalar.copy)
-        roots(14, 16)
         for c in range(2):
             affinity(1, 1, c)
-            brands(middle[c], 0, psum_out, f"acc{c}")
             for t in (2 * c, 2 * c + 1):
                 weigh(2, 0, t)
+                brands(wide[t], [(CAMPAIGN, 1)], closes=True)
+                store(wide[t], nc.scalar.copy)
         quantise_h(1, 1, 0, 2)
-        for nt in range(2, 4):
-            store(wide[nt], nc.scalar.copy)
+        both = [[(BASE, b), (CAMPAIGN, b)] for b in range(2)]
         for c in range(2):
             affinity(2, 0, c)
-            brands(middle[c], 1, psum_out, "")
+            open_bank(middle[c], psum_out, f"acc{c}")
+            brands(middle[c], both[0], opens=True)
             for t in (2 * c, 2 * c + 1):
                 weigh(2, 1, t)
         quantise_h(2, 0, 0, 2)
-        for c in range(2):
-            store(middle[c], nc.scalar.copy)
         affinity(2, 1, 0)
         affinity(2, 1, 1)
-        brands(last[0], 0, psum_out, "acc2")
-        brands(last[1], 0, psum_out, "acc3")
-        brands(last[2], 0, psum, "f_bank")
+        for c in range(2):
+            brands(middle[c], both[1], closes=True)
+            store(middle[c], nc.scalar.copy)
+        open_bank(last[0], psum_out, "acc2")
+        open_bank(last[1], psum_out, "acc3")
+        open_bank(last[2], psum, "f_bank")
+        for bank in last:
+            brands(bank, both[0], opens=True)
         quantise_h(2, 1, 0, 1)
-        brands(last[0], 1, psum_out, "")
+        brands(last[0], both[1], closes=True)
         quantise_h(2, 1, 1, 2)
         store(last[0], nc.scalar.copy)
-        brands(last[1], 1, psum_out, "")
-        brands(last[2], 1, psum, "")
+        brands(last[1], both[1], closes=True)
+        brands(last[2], both[1], closes=True)
         store(last[1], nc.scalar.copy, nc.scalar)
         store(last[2], nc.vector.tensor_copy)

@@ -20,7 +20,7 @@ P = 128
 PACK = 4
 HALF = 512
 AFF, FAT = 0, 1
-SCALAR_SQUARES = (6, 7)
+SCALAR_SQUARES = (7, 14, 15)
 BASE, CAMPAIGN = 0, 1
 WC_HALF_BYTES = PACK * N * 4
 GROUPS = ((0, 512), (512, 256), (768, 256))
@@ -90,7 +90,7 @@ def tile_list_fatigue_brand_affinity_kernel(
                 )
 
         def load_base_words():
-            weights["base_words"] = kept([P, 2, 2 * N], U8, "base_words", tag="prod_scales")
+            weights["base_words"] = kept([P, 2, 2 * N], U8, "base_words", tag=f"shop_words{FAT}")
             nc.sync.dma_start(
                 out=weights["base_words"][:].bitcast(I32), in_=w4_words.rearrange("b p x -> p b x").bitcast(I32)
             )
@@ -106,11 +106,14 @@ def tile_list_fatigue_brand_affinity_kernel(
         def gather(picked, window, offsets):
             nc.vector.tensor_copy(out=picked, in_=window.indirect(offsets))
 
-        v2_words = [kept([P, S2], U32, f"v2_words{a}") for a in range(2)]
+        v2_words, v_words = {}, {}
         v2_scales = kept([P, S2], U8, "v2_scales")
-        v_words = [kept([P, 2, HALF], U32, f"v_words{a}") for a in range(2)]
         listed_scales = kept([P, S], U8, "listed_scales")
         v_scales = kept([P, S], U8, "v_scales")
+
+        def pick_shop_words(a, tag=""):
+            v2_words[a] = kept([P, S2], U32, f"v2_words{a}", tag=tag)
+            gather(v2_words[a][:], shop_words[a], idx2[:])
 
         def pick_prod_words(a, b0, b1):
             gather(
@@ -125,10 +128,11 @@ def tile_list_fatigue_brand_affinity_kernel(
         def pick_shop_scales():
             gather(v2_scales[:], shop_scales[:], idx2[:])
 
-        def order_prod_scales():
+        def order_prod_scales(b):
+            half = slice(b * HALF, (b + 1) * HALF)
             nc.vector.tensor_copy(
-                out=v_scales[:].rearrange("p (b t c i) -> p b c t i", b=2, t=PACK, i=16),
-                in_=listed_scales[:].rearrange("p (b c i t) -> p b c t i", b=2, t=PACK, i=16),
+                out=v_scales[:, half].rearrange("p (t c i) -> p c t i", t=PACK, i=16),
+                in_=listed_scales[:, half].rearrange("p (c i t) -> p c t i", t=PACK, i=16),
             )
 
         def table_product(dst, a, b, t, j0, width):
@@ -161,7 +165,10 @@ def tile_list_fatigue_brand_affinity_kernel(
             f_bank = psum.tile([P, slots, width], F32, name="f_bank")
             for s in range(slots):
                 table_product(f_bank[:, s, :], FAT, b, t0 + s, j0, width)
-            squared[k] = ring.tile([P, slots, width], F32, name="squared")
+            if k in (9, 10):
+                squared[k] = kept([P, slots, width], F32, f"squared{k}", tag=f"wc_bf{k - 9}")
+            else:
+                squared[k] = ring.tile([P, slots, width], F32, name="squared")
             nc.scalar.activation(out=squared[k][:], in_=f_bank[:], func=ACT.Square)
 
         def root(k):
@@ -194,7 +201,7 @@ def tile_list_fatigue_brand_affinity_kernel(
                 )
 
         def affinity(g, b, c):
-            a_bank = psum.tile([P, PACK, P], F32, name="f_bank" if (g, b, c) == (2, 1, 0) else "a_bank")
+            a_bank = psum.tile([P, PACK, P], F32, name="a_bank")
             for t in range(PACK):
                 table_product(a_bank[:, t, :], AFF, b, t, GROUPS[g][0] + c * P, P)
             nc.vector.tensor_tensor(
@@ -268,12 +275,15 @@ def tile_list_fatigue_brand_affinity_kernel(
         middle = [(1, 0, 2 * P, 0, 2), (1, 0, 2 * P, 2, 4)]
         last = [(2, 0, P, 0, 4), (2, P, P, 0, 2), (2, P, P, 2, 4)]
 
-        gather(v2_words[FAT][:], shop_words[FAT], idx2[:])
+        pick_shop_words(FAT)
         pick_shop_scales()
         pick_prod_scales()
         load_base_words()
-        order_prod_scales()
+        order_prod_scales(0)
+        v_words[FAT] = kept([P, 2, HALF], U32, "v_words_fatigue", tag="prod_scales")
+        v_words[AFF] = kept([P, 2, HALF], U32, "v_words_affinity")
         pick_prod_words(FAT, 0, 1)
+        order_prod_scales(1)
         pick_prod_words(FAT, 1, 2)
         load_wc()
         load_base_scales()
@@ -286,7 +296,8 @@ def tile_list_fatigue_brand_affinity_kernel(
         roots(4, 12)
         round_wc(0)
         round_wc(1)
-        gather(v2_words[AFF][:], shop_words[AFF], idx2[:])
+        pick_shop_words(AFF, tag="listed_scales")
+        damp[0, 0] = kept([P, PACK, HALF], F32, "damp_first", tag=f"shop_words{AFF}")
         for t in range(PACK):
             weigh(0, 0, t)
         pick_prod_words(AFF, 0, 2)
@@ -303,6 +314,7 @@ def tile_list_fatigue_brand_affinity_kernel(
         quantise_h(0, 1, 0, 4)
         quantise_wc(0)
         roots(12, 16)
+        square_root(15)
         for c in range(2):
             affinity(1, 0, c)
             for t in (2 * c, 2 * c + 1):
@@ -321,7 +333,7 @@ def tile_list_fatigue_brand_affinity_kernel(
         both = [[(BASE, b), (CAMPAIGN, b)] for b in range(2)]
         for c in range(2):
             affinity(2, 0, c)
-            open_bank(middle[c], psum_out, f"acc{c}")
+            open_bank(middle[c], psum, "f_bank")
             brands(middle[c], both[0], opens=True)
             for t in (2 * c, 2 * c + 1):
                 weigh(2, 1, t)
@@ -331,9 +343,8 @@ def tile_list_fatigue_brand_affinity_kernel(
         for c in range(2):
             brands(middle[c], both[1], closes=True)
             store(middle[c], nc.scalar.copy)
-        open_bank(last[0], psum_out, "acc2")
-        open_bank(last[1], psum_out, "acc3")
-        open_bank(last[2], psum, "f_bank")
+        for n, bank in enumerate(last):
+            open_bank(bank, psum_out, f"acc{n}")
         for bank in last:
             brands(bank, both[0], opens=True)
         quantise_h(2, 1, 0, 1)

@@ -20,7 +20,7 @@ P = 128
 PACK = 4
 HALF = 512
 AFF, FAT = 0, 1
-SCALAR_SQUARES = (7, 14, 15)
+SCALAR_SQUARES = (6, 7, 14, 15)
 BASE, CAMPAIGN = 0, 1
 WC_HALF_BYTES = PACK * N * 4
 GROUPS = ((0, 512), (512, 256), (768, 256))
@@ -53,12 +53,19 @@ def tile_list_fatigue_brand_affinity_kernel(
         def load_words(queue, tile, words):
             queue.dma_start(out=tile.bitcast(I32), in_=words.rearrange("p t i -> p (t i)").bitcast(I32))
 
-        def load_scales(queue, tile, scales, first):
+        def load_scales(tile, scales, first, split_quadrants):
             for q in range(4):
-                queue.dma_start(
-                    out=tile[32 * q + first : 32 * q + first + 8, :].bitcast(I32),
-                    in_=scales[:, 4 * q : 4 * q + 4, :].bitcast(I32),
-                )
+                row = 32 * q + first
+                if q < split_quadrants:
+                    for a in range(2):
+                        nc.sync.dma_start(
+                            out=tile[row + 4 * a : row + 4 * a + 4, :].bitcast(I32),
+                            in_=scales[a, 4 * q : 4 * q + 4, :].bitcast(I32),
+                        )
+                else:
+                    nc.sync.dma_start(
+                        out=tile[row : row + 8, :].bitcast(I32), in_=scales[:, 4 * q : 4 * q + 4, :].bitcast(I32)
+                    )
 
         nc.vector.memset(shop_scales[:].bitcast(I32), 0)
         nc.vector.memset(prod_scales[:].bitcast(I32), 0)
@@ -70,8 +77,8 @@ def tile_list_fatigue_brand_affinity_kernel(
         nc.sync.dma_start(idx2[:], offs2)
         load_words(nc.sync, shop_words[FAT], tab2_words[FAT])
         nc.sync.dma_start(idx[:], offs)
-        load_scales(nc.sync, shop_scales, tab2_scales, 8)
-        load_scales(nc.sync, prod_scales, tab_scales, 0)
+        load_scales(shop_scales, tab2_scales, 8, 0)
+        load_scales(prod_scales, tab_scales, 0, 2)
         load_words(nc.sync, prod_words[FAT], tab_words[FAT])
         nc.sync.dma_start(out=margins[:, :, 0:PACK], in_=margin.rearrange("(b p t) -> p b t", b=2, t=PACK))
         load_words(nc.sync, shop_words[AFF], tab2_words[AFF])
@@ -273,7 +280,7 @@ def tile_list_fatigue_brand_affinity_kernel(
 
         wide = [(0, 0, HALF, nt, nt + 1) for nt in range(4)]
         middle = [(1, 0, 2 * P, 0, 2), (1, 0, 2 * P, 2, 4)]
-        last = [(2, 0, P, 0, 4), (2, P, P, 0, 2), (2, P, P, 2, 4)]
+        last = [(2, 0, P, 0, 4), (2, P, P, 0, 3), (2, P, P, 3, 4)]
 
         pick_shop_words(FAT)
         pick_shop_scales()
@@ -320,9 +327,8 @@ def tile_list_fatigue_brand_affinity_kernel(
             for t in (2 * c, 2 * c + 1):
                 weigh(1, 1, t)
                 brands(wide[t], [(BASE, 1), (CAMPAIGN, 0)])
-            if c == 0:
-                quantise_wc(1)
         quantise_h(1, 0, 0, 2)
+        quantise_wc(1)
         for c in range(2):
             affinity(1, 1, c)
             for t in (2 * c, 2 * c + 1):
@@ -350,7 +356,7 @@ def tile_list_fatigue_brand_affinity_kernel(
         quantise_h(2, 1, 0, 1)
         brands(last[0], both[1], closes=True)
         quantise_h(2, 1, 1, 2)
-        store(last[0], nc.scalar.copy)
+        store(last[0], nc.vector.tensor_copy)
         brands(last[1], both[1], closes=True)
         brands(last[2], both[1], closes=True)
         store(last[1], nc.scalar.copy, nc.scalar)

@@ -53,35 +53,35 @@ def tile_list_fatigue_brand_affinity_kernel(
         def load_words(queue, tile, words):
             queue.dma_start(out=tile.bitcast(I32), in_=words.rearrange("p t i -> p (t i)").bitcast(I32))
 
-        def load_scales(tile, scales, first, split_quadrants):
+        def load_scales_by_quadrant(tile, scales, first):
             for q in range(4):
-                row = 32 * q + first
-                if q < split_quadrants:
-                    for a in range(2):
-                        nc.sync.dma_start(
-                            out=tile[row + 4 * a : row + 4 * a + 4, :].bitcast(I32),
-                            in_=scales[a, 4 * q : 4 * q + 4, :].bitcast(I32),
-                        )
-                else:
+                nc.sync.dma_start(
+                    out=tile[32 * q + first : 32 * q + first + 8, :].bitcast(I32),
+                    in_=scales[:, 4 * q : 4 * q + 4, :].bitcast(I32),
+                )
+
+        def load_scales_by_row(tile, scales, first):
+            for r in range(4):
+                for a in range(2):
                     nc.sync.dma_start(
-                        out=tile[row : row + 8, :].bitcast(I32), in_=scales[:, 4 * q : 4 * q + 4, :].bitcast(I32)
+                        out=tile[first + 4 * a + r : P : 32, :].bitcast(I32), in_=scales[a, r:16:4, :].bitcast(I32)
                     )
 
         nc.vector.memset(shop_scales[:].bitcast(I32), 0)
         nc.vector.memset(prod_scales[:].bitcast(I32), 0)
 
         warm = kept([P, 2], F32, "warm")
-        nc.gpsimd.memset(warm[:, 0:1], 1.0)
+        nc.vector.memset(warm[:, 0:1], 1.0)
         nc.scalar.activation(out=warm[:, 1:2], in_=warm[:, 0:1], func=ACT.Abs_reciprocal_sqrt)
 
         nc.sync.dma_start(idx2[:], offs2)
         load_words(nc.sync, shop_words[FAT], tab2_words[FAT])
         nc.sync.dma_start(idx[:], offs)
-        load_scales(shop_scales, tab2_scales, 8, 0)
-        load_scales(prod_scales, tab_scales, 0, 2)
+        load_scales_by_quadrant(shop_scales, tab2_scales, 8)
+        load_scales_by_row(prod_scales, tab_scales, 0)
         load_words(nc.sync, prod_words[FAT], tab_words[FAT])
-        nc.sync.dma_start(out=margins[:, :, 0:PACK], in_=margin.rearrange("(b p t) -> p b t", b=2, t=PACK))
         load_words(nc.sync, shop_words[AFF], tab2_words[AFF])
+        nc.sync.dma_start(out=margins[:, :, 0:PACK], in_=margin.rearrange("(b p t) -> p b t", b=2, t=PACK))
         load_words(nc.sync, prod_words[AFF], tab_words[AFF])
 
         weights = {}

@@ -15,12 +15,14 @@ FP8X4 = mybir.dt.float8_e4m3fn_x4
 FP4X4 = mybir.dt.float4_e2m1fn_x4
 ACT = mybir.ActivationFunctionType
 MULT = mybir.AluOpType.mult
+ADD = mybir.AluOpType.add
 
 P = 128
 PACK = 4
 HALF = 512
 AFF, FAT = 0, 1
-SCALAR_SQUARES = (6, 7, 14, 15)
+SCALAR_SQUARES = (8, 10, 12, 14, 15)
+GPSIMD_MARGINS = (8, 10, 12, 14)
 BASE, CAMPAIGN = 0, 1
 WC_HALF_BYTES = PACK * N * 4
 GROUPS = ((0, 512), (512, 256), (768, 256))
@@ -159,7 +161,8 @@ def tile_list_fatigue_brand_affinity_kernel(
         for g, (j0, width) in enumerate(GROUPS):
             for b in range(2):
                 inverse_root[g, b] = damp[g, b] = kept([P, PACK, width], F32, f"damp{g}{b}")
-                h_bf[g, b] = kept([P, width * PACK], BF16, f"h_bf{g}{b}")
+                if (g, b) != (0, 0):
+                    h_bf[g, b] = kept([P, width * PACK], BF16, f"h_bf{g}{b}")[:]
                 h_words[g, b] = kept([P, width], U32, f"h_words{g}{b}")
                 h_scales[g, b] = kept([P, width], U8, f"h_scales{g}{b}")
                 slots = HALF // width
@@ -172,16 +175,16 @@ def tile_list_fatigue_brand_affinity_kernel(
             f_bank = psum.tile([P, slots, width], F32, name="f_bank")
             for s in range(slots):
                 table_product(f_bank[:, s, :], FAT, b, t0 + s, j0, width)
-            if k in (9, 10):
-                squared[k] = kept([P, slots, width], F32, f"squared{k}", tag=f"wc_bf{k - 9}")
+            if k == 10:
+                squared[k] = kept([P, slots, width], F32, "squared10", tag="wc_bf1")[:]
             else:
-                squared[k] = ring.tile([P, slots, width], F32, name="squared")
-            nc.scalar.activation(out=squared[k][:], in_=f_bank[:], func=ACT.Square)
+                squared[k] = ring.tile([P, slots, width], F32, name="squared")[:]
+            nc.scalar.activation(out=squared[k], in_=f_bank[:], func=ACT.Square)
 
         def root(k):
             g, b, t0, slots = slabs[k]
             nc.scalar.activation(
-                out=inverse_root[g, b][:, t0 : t0 + slots, :], in_=squared[k][:], func=ACT.Abs_reciprocal_sqrt, bias=1.0
+                out=inverse_root[g, b][:, t0 : t0 + slots, :], in_=squared[k], func=ACT.Abs_reciprocal_sqrt, bias=1.0
             )
 
         def square_root(k):
@@ -193,13 +196,19 @@ def tile_list_fatigue_brand_affinity_kernel(
             for k in range(k0, k1):
                 if k + 1 < len(slabs):
                     square(k + 1)
-                root(k)
                 if k - 1 in SCALAR_SQUARES:
                     square_root(k - 1)
+                root(k)
 
         def weigh(g, b, t):
             root_t = inverse_root[g, b][:, t, :]
-            if any(slabs[k][0:2] == (g, b) and 0 <= t - slabs[k][2] < slabs[k][3] for k in SCALAR_SQUARES):
+            k = max(n for n, slab in enumerate(slabs) if slab[0:2] == (g, b) and slab[2] <= t)
+            if k in GPSIMD_MARGINS:
+                nc.gpsimd.tensor_scalar(
+                    out=damp[g, b][:, t, :], in0=root_t, scalar1=margins[:, b, t : t + 1], scalar2=0.0,
+                    op0=MULT, op1=ADD,
+                )
+            elif k in SCALAR_SQUARES:
                 nc.vector.tensor_scalar_mul(out=damp[g, b][:, t, :], in0=root_t, scalar1=margins[:, b, t : t + 1])
             else:
                 nc.vector.scalar_tensor_tensor(
@@ -207,8 +216,8 @@ def tile_list_fatigue_brand_affinity_kernel(
                     op0=MULT, op1=MULT,
                 )
 
-        def affinity(g, b, c):
-            a_bank = psum.tile([P, PACK, P], F32, name="a_bank")
+        def affinity(g, b, c, pool=psum, name="a_bank"):
+            a_bank = pool.tile([P, PACK, P], F32, name=name)
             for t in range(PACK):
                 table_product(a_bank[:, t, :], AFF, b, t, GROUPS[g][0] + c * P, P)
             nc.vector.tensor_tensor(
@@ -227,18 +236,24 @@ def tile_list_fatigue_brand_affinity_kernel(
 
         wc_bf, wc_words, wc_scales = {}, {}, {}
 
-        def round_wc(b):
-            wc_bf[b] = kept([P, N, PACK], BF16, f"wc_bf{b}")
+        def round_wc_scalar(b, n0, n1):
             nc.scalar.copy(
-                out=wc_bf[b][:].rearrange("p (k i) t -> p k t i", i=4),
-                in_=weights["wc_raw", b][:].rearrange("p t (k i) -> p k t i", i=4),
+                out=wc_bf[b][:, n0 * PACK : n1 * PACK].rearrange("p (k i t) -> p k t i", i=4, t=PACK),
+                in_=weights["wc_raw", b][:, :, n0:n1].rearrange("p t (k i) -> p k t i", i=4),
+            )
+
+        def round_wc_gpsimd(b, n0, n1):
+            nc.gpsimd.tensor_scalar(
+                out=wc_bf[b][:, n0 * PACK : n1 * PACK].rearrange("p (n t) -> p n t", t=PACK),
+                in0=weights["wc_raw", b][:, :, n0:n1].rearrange("p t n -> p n t"),
+                scalar1=1.0, scalar2=0.0, op0=MULT, op1=ADD,
             )
 
         def quantise_wc(b):
             wc_words[b] = kept([P, N], U32, f"wc_words{b}")
             wc_scales[b] = kept([P, N], U8, f"wc_scales{b}")
             nc.vector.quantize_mx(
-                out=wc_words[b][:].bitcast(FP8X4), scales=wc_scales[b][:], in_=wc_bf[b][:].rearrange("p n t -> p (n t)")
+                out=wc_words[b][:].bitcast(FP8X4), scales=wc_scales[b][:], in_=wc_bf[b]
             )
 
         acc = {}
@@ -280,7 +295,7 @@ def tile_list_fatigue_brand_affinity_kernel(
 
         wide = [(0, 0, HALF, nt, nt + 1) for nt in range(4)]
         middle = [(1, 0, 2 * P, 0, 2), (1, 0, 2 * P, 2, 4)]
-        last = [(2, 0, P, 0, 4), (2, P, P, 0, 3), (2, P, P, 3, 4)]
+        last = [(2, 0, 2 * P, nt, nt + 1) for nt in range(4)]
 
         pick_shop_words(FAT)
         pick_shop_scales()
@@ -301,48 +316,71 @@ def tile_list_fatigue_brand_affinity_kernel(
             root(k + 1)
         square(4)
         roots(4, 12)
-        round_wc(0)
-        round_wc(1)
+        wc_bf[1] = kept([P, N * PACK], BF16, "wc_bf1")[:]
+        round_wc_scalar(1, 0, N)
         pick_shop_words(AFF, tag="listed_scales")
         damp[0, 0] = kept([P, PACK, HALF], F32, "damp_first", tag=f"shop_words{AFF}")
         for t in range(PACK):
             weigh(0, 0, t)
         pick_prod_words(AFF, 0, 2)
         damp[0, 1] = kept([P, PACK, HALF], F32, "damp_late", tag="prod_affinity")
-        for c in range(4):
-            affinity(0, 0, c)
-            weigh(0, 1, c)
+        for t in range(PACK):
+            weigh(0, 1, t)
+        after_roots = kept([P, 2, N * PACK], BF16, "after_roots", tag="damp01")
+        wc_bf[0], h_bf[0, 0] = after_roots[:, 0, :], after_roots[:, 1, :]
+        round_wc_gpsimd(0, 0, N)
+        affinity(0, 0, 0)
+        affinity(0, 0, 1)
+        for n, (b, c) in enumerate(((0, 2), (0, 3), (1, 0), (1, 1))):
+            affinity(0, b, c, psum_out, f"acc{n}")
         quantise_h(0, 0, 0, 4)
-        for c in range(4):
-            affinity(0, 1, c)
-            weigh(1, 0, c)
-            open_bank(wide[c], psum_out, f"acc{c}")
-            brands(wide[c], [(BASE, 0)], opens=True)
-        quantise_h(0, 1, 0, 4)
         quantise_wc(0)
+        first_weights = kept([P, PACK, 2 * P], F32, "damp_after_wc", tag="damp01")
+        damp[1, 0] = first_weights
+        weigh(1, 0, 0)
+        weigh(1, 0, 1)
+        affinity(0, 1, 2)
+        affinity(0, 1, 3)
+        for c in range(4):
+            open_bank(wide[c], psum_out, f"acc{c}")
+            brands(wide[c], [(BASE, 0), (CAMPAIGN, 0)], opens=True)
+        weigh(1, 0, 2)
+        quantise_h(0, 1, 0, 4)
+        weigh(1, 0, 3)
         roots(12, 16)
         square_root(15)
+        damp[1, 1] = kept([P, PACK, 2 * P], F32, "damp_after_root10", tag="damp10")
+        for c in range(2):
+            weigh(1, 1, c)
         for c in range(2):
             affinity(1, 0, c)
             for t in (2 * c, 2 * c + 1):
-                weigh(1, 1, t)
-                brands(wide[t], [(BASE, 1), (CAMPAIGN, 0)])
+                brands(wide[t], [(BASE, 1)])
+        for c in range(2):
+            weigh(1, 1, 2 + c)
         quantise_h(1, 0, 0, 2)
         quantise_wc(1)
+        damp[2, 0] = kept([P, PACK, 2 * P], F32, "damp_after_h10", tag="h_bf10")
+        for c in range(2):
+            weigh(2, 0, c)
         for c in range(2):
             affinity(1, 1, c)
             for t in (2 * c, 2 * c + 1):
-                weigh(2, 0, t)
                 brands(wide[t], [(CAMPAIGN, 1)], closes=True)
                 store(wide[t], nc.scalar.copy)
+        for c in range(2):
+            weigh(2, 0, 2 + c)
         quantise_h(1, 1, 0, 2)
         both = [[(BASE, b), (CAMPAIGN, b)] for b in range(2)]
+        damp[2, 1] = kept([P, PACK, 2 * P], F32, "damp_after_root20", tag="damp20")
+        for c in range(2):
+            weigh(2, 1, c)
         for c in range(2):
             affinity(2, 0, c)
             open_bank(middle[c], psum, "f_bank")
             brands(middle[c], both[0], opens=True)
-            for t in (2 * c, 2 * c + 1):
-                weigh(2, 1, t)
+        for c in range(2):
+            weigh(2, 1, 2 + c)
         quantise_h(2, 0, 0, 2)
         affinity(2, 1, 0)
         affinity(2, 1, 1)
@@ -353,11 +391,10 @@ def tile_list_fatigue_brand_affinity_kernel(
             open_bank(bank, psum_out, f"acc{n}")
         for bank in last:
             brands(bank, both[0], opens=True)
-        quantise_h(2, 1, 0, 1)
-        brands(last[0], both[1], closes=True)
-        quantise_h(2, 1, 1, 2)
+        quantise_h(2, 1, 0, 2)
+        for bank in last:
+            brands(bank, both[1], closes=True)
         store(last[0], nc.vector.tensor_copy)
-        brands(last[1], both[1], closes=True)
-        brands(last[2], both[1], closes=True)
-        store(last[1], nc.scalar.copy, nc.scalar)
+        store(last[1], nc.scalar.copy)
         store(last[2], nc.vector.tensor_copy)
+        store(last[3], nc.scalar.copy, nc.scalar)

@@ -21,7 +21,7 @@ P = 128
 PACK = 4
 HALF = 512
 AFF, FAT = 0, 1
-SCALAR_SQUARES = (8, 10, 12, 14, 15)
+SCALAR_SQUARES = (8, 10, 11, 12, 14, 15)
 GPSIMD_MARGINS = (8, 10, 12, 14)
 BASE, CAMPAIGN = 0, 1
 WC_HALF_BYTES = PACK * N * 4
@@ -295,7 +295,7 @@ def tile_list_fatigue_brand_affinity_kernel(
 
         wide = [(0, 0, HALF, nt, nt + 1) for nt in range(4)]
         middle = [(1, 0, 2 * P, 0, 2), (1, 0, 2 * P, 2, 4)]
-        last = [(2, 0, 2 * P, nt, nt + 1) for nt in range(4)]
+        last = [(2, 0, P, 0, 4), (2, P, P, 0, 3), (2, P, P, 3, 4)]
 
         pick_shop_words(FAT)
         pick_shop_scales()
@@ -391,10 +391,11 @@ def tile_list_fatigue_brand_affinity_kernel(
             open_bank(bank, psum_out, f"acc{n}")
         for bank in last:
             brands(bank, both[0], opens=True)
-        quantise_h(2, 1, 0, 2)
-        for bank in last:
-            brands(bank, both[1], closes=True)
+        quantise_h(2, 1, 0, 1)
+        brands(last[0], both[1], closes=True)
+        quantise_h(2, 1, 1, 2)
         store(last[0], nc.vector.tensor_copy)
-        store(last[1], nc.scalar.copy)
+        brands(last[1], both[1], closes=True)
+        brands(last[2], both[1], closes=True)
+        store(last[1], nc.scalar.copy, nc.scalar)
         store(last[2], nc.vector.tensor_copy)
-        store(last[3], nc.scalar.copy, nc.scalar)

@@ -21,8 +21,9 @@ P = 128
 PACK = 4
 HALF = 512
 AFF, FAT = 0, 1
-SCALAR_SQUARES = (8, 10, 11, 12, 14, 15)
-GPSIMD_MARGINS = (8, 10, 12, 14)
+SCALAR_SQUARES = (8, 10, 12, 14)
+GPSIMD_MARGINS = (10, 12, 14)
+FIRST_COLUMNS = 352
 BASE, CAMPAIGN = 0, 1
 WC_HALF_BYTES = PACK * N * 4
 GROUPS = ((0, 512), (512, 256), (768, 256))
@@ -216,10 +217,17 @@ def tile_list_fatigue_brand_affinity_kernel(
                     op0=MULT, op1=MULT,
                 )
 
-        def affinity(g, b, c, pool=psum, name="a_bank"):
-            a_bank = pool.tile([P, PACK, P], F32, name=name)
+        a_banks = {}
+
+        def affinity_sums(g, b, c, pool=psum, name="a_bank"):
+            a_banks[g, b, c] = pool.tile([P, PACK, P], F32, name=name)
             for t in range(PACK):
-                table_product(a_bank[:, t, :], AFF, b, t, GROUPS[g][0] + c * P, P)
+                table_product(a_banks[g, b, c][:, t, :], AFF, b, t, GROUPS[g][0] + c * P, P)
+
+        def affinity(g, b, c, pool=psum, name="a_bank"):
+            if (g, b, c) not in a_banks:
+                affinity_sums(g, b, c, pool, name)
+            a_bank = a_banks[g, b, c]
             nc.vector.tensor_tensor(
                 out=h_bf[g, b][:, c * HALF : (c + 1) * HALF].rearrange("p (k i t) -> p k t i", i=2, t=PACK),
                 in0=a_bank[:].rearrange("p t (k i) -> p k t i", i=2),
@@ -326,36 +334,42 @@ def tile_list_fatigue_brand_affinity_kernel(
         damp[0, 1] = kept([P, PACK, HALF], F32, "damp_late", tag="prod_affinity")
         for t in range(PACK):
             weigh(0, 1, t)
-        after_roots = kept([P, 2, N * PACK], BF16, "after_roots", tag="damp01")
-        wc_bf[0], h_bf[0, 0] = after_roots[:, 0, :], after_roots[:, 1, :]
-        round_wc_gpsimd(0, 0, N)
-        affinity(0, 0, 0)
-        affinity(0, 0, 1)
-        for n, (b, c) in enumerate(((0, 2), (0, 3), (1, 0), (1, 1))):
-            affinity(0, b, c, psum_out, f"acc{n}")
-        quantise_h(0, 0, 0, 4)
-        quantise_wc(0)
-        first_weights = kept([P, PACK, 2 * P], F32, "damp_after_wc", tag="damp01")
-        damp[1, 0] = first_weights
-        weigh(1, 0, 0)
-        weigh(1, 0, 1)
-        affinity(0, 1, 2)
-        affinity(0, 1, 3)
+        after_roots = kept([P, (N + FIRST_COLUMNS) * PACK], BF16, "after_roots", tag="damp01")
+        wc_bf[0], h_bf[0, 0] = after_roots[:, : N * PACK], after_roots[:, FIRST_COLUMNS * PACK :]
+        round_wc_gpsimd(0, 0, FIRST_COLUMNS)
+        for n in range(8):
+            if n % 3 == 2:
+                affinity(0, n // 4, n % 4, psum_out, "acc3")
+            else:
+                affinity(0, n // 4, n % 4)
+            if n == 4:
+                quantise_h(0, 0, 0, 4)
+                round_wc_gpsimd(0, FIRST_COLUMNS, N)
+        for c in range(2):
+            affinity_sums(1, 0, c)
         for c in range(4):
             open_bank(wide[c], psum_out, f"acc{c}")
-            brands(wide[c], [(BASE, 0), (CAMPAIGN, 0)], opens=True)
-        weigh(1, 0, 2)
+            brands(wide[c], [(BASE, 0)], opens=True)
+        quantise_wc(0)
+        for c in range(4):
+            brands(wide[c], [(CAMPAIGN, 0)])
+        damp[1, 0] = kept([P, PACK, 2 * P], F32, "damp_middle", tag="prod_affinity")
+        for t in range(PACK):
+            weigh(1, 0, t)
         quantise_h(0, 1, 0, 4)
-        weigh(1, 0, 3)
-        roots(12, 16)
-        square_root(15)
+        roots(12, 14)
+        root(14)
+        square(15)
+        square_root(14)
+        root(15)
         damp[1, 1] = kept([P, PACK, 2 * P], F32, "damp_after_root10", tag="damp10")
         for c in range(2):
             weigh(1, 1, c)
         for c in range(2):
             affinity(1, 0, c)
-            for t in (2 * c, 2 * c + 1):
-                brands(wide[t], [(BASE, 1)])
+            affinity_sums(1, 1, c)
+        for c in range(4):
+            brands(wide[c], [(BASE, 1)])
         for c in range(2):
             weigh(1, 1, 2 + c)
         quantise_h(1, 0, 0, 2)
@@ -365,9 +379,10 @@ def tile_list_fatigue_brand_affinity_kernel(
             weigh(2, 0, c)
         for c in range(2):
             affinity(1, 1, c)
-            for t in (2 * c, 2 * c + 1):
-                brands(wide[t], [(CAMPAIGN, 1)], closes=True)
-                store(wide[t], nc.scalar.copy)
+            affinity_sums(2, 0, c)
+        for c in range(4):
+            brands(wide[c], [(CAMPAIGN, 1)], closes=True)
+            store(wide[c], nc.scalar.copy)
         for c in range(2):
             weigh(2, 0, 2 + c)
         quantise_h(1, 1, 0, 2)
@@ -377,6 +392,8 @@ def tile_list_fatigue_brand_affinity_kernel(
             weigh(2, 1, c)
         for c in range(2):
             affinity(2, 0, c)
+            affinity_sums(2, 1, c)
+        for c in range(2):
             open_bank(middle[c], psum, "f_bank")
             brands(middle[c], both[0], opens=True)
         for c in range(2):

@@ -70,8 +70,8 @@ def tile_list_fatigue_brand_affinity_kernel(
                         out=tile[first + 4 * a + r : P : 32, :].bitcast(I32), in_=scales[a, r:16:4, :].bitcast(I32)
                     )
 
-        nc.vector.memset(shop_scales[:].bitcast(I32), 0)
         nc.vector.memset(prod_scales[:].bitcast(I32), 0)
+        nc.vector.memset(shop_scales[:].bitcast(I32), 0)
 
         warm = kept([P, 2], F32, "warm")
         nc.vector.memset(warm[:, 0:1], 1.0)
@@ -80,8 +80,8 @@ def tile_list_fatigue_brand_affinity_kernel(
         nc.sync.dma_start(idx2[:], offs2)
         load_words(nc.sync, shop_words[FAT], tab2_words[FAT])
         nc.sync.dma_start(idx[:], offs)
-        load_scales_by_quadrant(shop_scales, tab2_scales, 8)
         load_scales_by_row(prod_scales, tab_scales, 0)
+        load_scales_by_quadrant(shop_scales, tab2_scales, 8)
         load_words(nc.sync, prod_words[FAT], tab_words[FAT])
         load_words(nc.sync, shop_words[AFF], tab2_words[AFF])
         nc.sync.dma_start(out=margins[:, :, 0:PACK], in_=margin.rearrange("(b p t) -> p b t", b=2, t=PACK))
@@ -306,14 +306,14 @@ def tile_list_fatigue_brand_affinity_kernel(
         last = [(2, 0, P, 0, 4), (2, P, P, 0, 3), (2, P, P, 3, 4)]
 
         pick_shop_words(FAT)
-        pick_shop_scales()
         pick_prod_scales()
         load_base_words()
         order_prod_scales(0)
+        order_prod_scales(1)
+        pick_shop_scales()
         v_words[FAT] = kept([P, 2, HALF], U32, "v_words_fatigue", tag="prod_scales")
         v_words[AFF] = kept([P, 2, HALF], U32, "v_words_affinity")
         pick_prod_words(FAT, 0, 1)
-        order_prod_scales(1)
         pick_prod_words(FAT, 1, 2)
         load_wc()
         load_base_scales()

@@ -21,9 +21,8 @@ P = 128
 PACK = 4
 HALF = 512
 AFF, FAT = 0, 1
-SCALAR_SQUARES = (8, 10, 12, 14)
+SCALAR_SQUARES = (6, 8, 10, 12, 14, 15)
 GPSIMD_MARGINS = (10, 12, 14)
-FIRST_COLUMNS = 352
 BASE, CAMPAIGN = 0, 1
 WC_HALF_BYTES = PACK * N * 4
 GROUPS = ((0, 512), (512, 256), (768, 256))
@@ -173,11 +172,14 @@ def tile_list_fatigue_brand_affinity_kernel(
         def square(k):
             g, b, t0, slots = slabs[k]
             j0, width = GROUPS[g]
-            f_bank = psum.tile([P, slots, width], F32, name="f_bank")
+            if k in (2, 3, 6, 7) or 10 <= k < 14:
+                f_bank = psum_out.tile([P, slots, width], F32, name=f"acc{k % 4 if k < 8 else k - 10}")
+            else:
+                f_bank = psum.tile([P, slots, width], F32, name="f_bank")
             for s in range(slots):
                 table_product(f_bank[:, s, :], FAT, b, t0 + s, j0, width)
-            if k == 10:
-                squared[k] = kept([P, slots, width], F32, "squared10", tag="wc_bf1")[:]
+            if k == 11:
+                squared[k] = kept([P, slots, width], F32, "squared11", tag="wc_bf1")[:]
             else:
                 squared[k] = ring.tile([P, slots, width], F32, name="squared")[:]
             nc.scalar.activation(out=squared[k], in_=f_bank[:], func=ACT.Square)
@@ -246,22 +248,24 @@ def tile_list_fatigue_brand_affinity_kernel(
 
         def round_wc_scalar(b, n0, n1):
             nc.scalar.copy(
-                out=wc_bf[b][:, n0 * PACK : n1 * PACK].rearrange("p (k i t) -> p k t i", i=4, t=PACK),
+                out=wc_bf[b, n0].rearrange("p (k i t) -> p k t i", i=4, t=PACK),
                 in_=weights["wc_raw", b][:, :, n0:n1].rearrange("p t (k i) -> p k t i", i=4),
             )
 
         def round_wc_gpsimd(b, n0, n1):
             nc.gpsimd.tensor_scalar(
-                out=wc_bf[b][:, n0 * PACK : n1 * PACK].rearrange("p (n t) -> p n t", t=PACK),
+                out=wc_bf[b, n0].rearrange("p (n t) -> p n t", t=PACK),
                 in0=weights["wc_raw", b][:, :, n0:n1].rearrange("p t n -> p n t"),
                 scalar1=1.0, scalar2=0.0, op0=MULT, op1=ADD,
             )
 
-        def quantise_wc(b):
+        for b in range(2):
             wc_words[b] = kept([P, N], U32, f"wc_words{b}")
             wc_scales[b] = kept([P, N], U8, f"wc_scales{b}")
+
+        def quantise_wc(b, n0=0, n1=N):
             nc.vector.quantize_mx(
-                out=wc_words[b][:].bitcast(FP8X4), scales=wc_scales[b][:], in_=wc_bf[b]
+                out=wc_words[b][:, n0:n1].bitcast(FP8X4), scales=wc_scales[b][:, n0:n1], in_=wc_bf[b, n0]
             )
 
         acc = {}
@@ -323,45 +327,58 @@ def tile_list_fatigue_brand_affinity_kernel(
             root(k)
             root(k + 1)
         square(4)
-        roots(4, 12)
-        wc_bf[1] = kept([P, N * PACK], BF16, "wc_bf1")[:]
-        round_wc_scalar(1, 0, N)
+        roots(4, 9)
         pick_shop_words(AFF, tag="listed_scales")
         damp[0, 0] = kept([P, PACK, HALF], F32, "damp_first", tag=f"shop_words{AFF}")
         for t in range(PACK):
             weigh(0, 0, t)
-        pick_prod_words(AFF, 0, 2)
-        damp[0, 1] = kept([P, PACK, HALF], F32, "damp_late", tag="prod_affinity")
-        for t in range(PACK):
-            weigh(0, 1, t)
-        after_roots = kept([P, (N + FIRST_COLUMNS) * PACK], BF16, "after_roots", tag="damp01")
-        wc_bf[0], h_bf[0, 0] = after_roots[:, : N * PACK], after_roots[:, FIRST_COLUMNS * PACK :]
-        round_wc_gpsimd(0, 0, FIRST_COLUMNS)
-        for n in range(8):
-            if n % 3 == 2:
-                affinity(0, n // 4, n % 4, psum_out, "acc3")
-            else:
-                affinity(0, n // 4, n % 4)
-            if n == 4:
-                quantise_h(0, 0, 0, 4)
-                round_wc_gpsimd(0, FIRST_COLUMNS, N)
-        for c in range(2):
-            affinity_sums(1, 0, c)
+        pick_prod_words(AFF, 0, 1)
+        pick_prod_words(AFF, 1, 2)
+        wc_bf[0, 0] = kept([P, N // 2 * PACK], BF16, "wc_bf_first", tag="prod_affinity")[:]
+        round_wc_gpsimd(0, 0, N // 2)
+        h_bf[0, 0] = kept([P, HALF * PACK], BF16, "h_bf00")[:]
         for c in range(4):
+            affinity_sums(0, 0, c, psum_out, f"acc{c}")
+        for c in range(4):
+            affinity_sums(0, 1, c, psum, "a_bank" if c < 2 else "f_bank")
+        for c in range(4):
+            affinity(0, 0, c)
+        roots(9, 12)
+        square(13)
+        wc_bf[1, 0] = kept([P, N * PACK], BF16, "wc_bf1")[:]
+        round_wc_scalar(1, 0, N)
+        root(12)
+        damp[0, 1] = kept([P, PACK, HALF], F32, "damp_late", tag=f"shop_words{AFF}")
+        weigh(0, 1, 0)
+        quantise_h(0, 0, 0, 4)
+        quantise_wc(0, 0, N // 2)
+        for c in range(2):
+            open_bank(wide[c], psum_out, f"acc{c}")
+            brands(wide[c], [(BASE, 0), (CAMPAIGN, 0)], opens=True)
+        for t in range(1, PACK):
+            weigh(0, 1, t)
+        wc_bf[0, N // 2] = kept([P, N // 2 * PACK], BF16, "wc_bf_second", tag="damp01")[:]
+        round_wc_gpsimd(0, N // 2, N)
+        for c in range(4):
+            affinity(0, 1, c)
+            if c < 2:
+                affinity_sums(1, 0, c)
+        for c in range(2, 4):
             open_bank(wide[c], psum_out, f"acc{c}")
             brands(wide[c], [(BASE, 0)], opens=True)
-        quantise_wc(0)
-        for c in range(4):
+        quantise_wc(0, N // 2, N)
+        for c in range(2, 4):
             brands(wide[c], [(CAMPAIGN, 0)])
-        damp[1, 0] = kept([P, PACK, 2 * P], F32, "damp_middle", tag="prod_affinity")
+        damp[1, 0] = kept([P, PACK, 2 * P], F32, "damp_middle", tag=f"shop_words{AFF}")
         for t in range(PACK):
             weigh(1, 0, t)
         quantise_h(0, 1, 0, 4)
-        roots(12, 14)
+        roots(13, 14)
         root(14)
         square(15)
         square_root(14)
         root(15)
+        square_root(15)
         damp[1, 1] = kept([P, PACK, 2 * P], F32, "damp_after_root10", tag="damp10")
         for c in range(2):
             weigh(1, 1, c)

@@ -21,7 +21,7 @@ P = 128
 PACK = 4
 HALF = 512
 AFF, FAT = 0, 1
-SCALAR_SQUARES = (6, 8, 10, 12, 14, 15)
+SCALAR_SQUARES = (6, 10, 12, 14, 15)
 GPSIMD_MARGINS = (10, 12, 14)
 BASE, CAMPAIGN = 0, 1
 WC_HALF_BYTES = PACK * N * 4
@@ -420,7 +420,7 @@ def tile_list_fatigue_brand_affinity_kernel(
         affinity(2, 1, 1)
         for c in range(2):
             brands(middle[c], both[1], closes=True)
-            store(middle[c], nc.scalar.copy)
+        store(middle[0], nc.scalar.copy)
         for n, bank in enumerate(last):
             open_bank(bank, psum_out, f"acc{n}")
         for bank in last:
@@ -428,6 +428,7 @@ def tile_list_fatigue_brand_affinity_kernel(
         quantise_h(2, 1, 0, 1)
         brands(last[0], both[1], closes=True)
         quantise_h(2, 1, 1, 2)
+        store(middle[1], nc.vector.tensor_copy)
         store(last[0], nc.vector.tensor_copy)
         brands(last[1], both[1], closes=True)
         brands(last[2], both[1], closes=True)

@@ -20,12 +20,12 @@ ADD = mybir.AluOpType.add
 P = 128
 PACK = 4
 HALF = 512
+GROUP = 256
 AFF, FAT = 0, 1
-SCALAR_SQUARES = (6, 10, 12, 14, 15)
-GPSIMD_MARGINS = (10, 12, 14)
 BASE, CAMPAIGN = 0, 1
-WC_HALF_BYTES = PACK * N * 4
-GROUPS = ((0, 512), (512, 256), (768, 256))
+BLOCKS = ((0, 0), (1, 0), (0, 1), (1, 1), (2, 0), (2, 1), (3, 0), (3, 1))
+SCALAR_SQUARES = (6, 10, 12, 13, 14)
+GPSIMD_MARGINS = (10, 12, 13, 14)
 
 
 def tile_list_fatigue_brand_affinity_kernel(
@@ -37,37 +37,29 @@ def tile_list_fatigue_brand_affinity_kernel(
         keep = ctx.enter_context(tc.tile_pool(name="keep", bufs=1))
         reuse = ctx.enter_context(tc.tile_pool(name="reuse", bufs=1))
         ring = ctx.enter_context(tc.tile_pool(name="ring", bufs=3))
-        psum = ctx.enter_context(tc.psum_pool(name="psum", bufs=2))
-        psum_out = ctx.enter_context(tc.psum_pool(name="psum_out", bufs=1))
+        psum = ctx.enter_context(tc.psum_pool(name="psum", bufs=1))
 
         def kept(shape, dtype, name, tag=""):
             return keep.tile(shape, dtype, name=name, tag=tag or name, align_bytes=64)
 
+        def bank(n, shape, name):
+            return psum.tile(shape, F32, name=name, tag=f"bank{n}")
+
         idx = lists.tile([P, S // 16], U16, name="idx")
         idx2 = lists.tile([P, S2 // 16], U16, name="idx2")
-        prod_fatigue = reuse.tile([P, T], U32, name="prod_fatigue", align_bytes=64, offset=0)
-        prod_words = {AFF: kept([P, T], U32, "prod_affinity")[:], FAT: prod_fatigue[:]}
+        prod_words = [kept([P, T], U32, f"prod_words{a}")[:] for a in range(2)]
         shop_words = [kept([P, T2], U32, f"shop_words{a}")[:] for a in range(2)]
         prod_scales = kept([P, T], U8, "prod_scales")
         shop_scales = kept([P, T2], U8, "shop_scales")
         margins = kept([P, 2, 2 * PACK], F32, "margins")
 
-        def load_words(queue, tile, words):
-            queue.dma_start(out=tile.bitcast(I32), in_=words.rearrange("p t i -> p (t i)").bitcast(I32))
+        def load_words(tile, words):
+            nc.sync.dma_start(out=tile.bitcast(I32), in_=words.rearrange("p t i -> p (t i)").bitcast(I32))
 
-        def load_scales_by_quadrant(tile, scales, first):
-            for q in range(4):
-                nc.sync.dma_start(
-                    out=tile[32 * q + first : 32 * q + first + 8, :].bitcast(I32),
-                    in_=scales[:, 4 * q : 4 * q + 4, :].bitcast(I32),
-                )
-
-        def load_scales_by_row(tile, scales, first):
-            for r in range(4):
-                for a in range(2):
-                    nc.sync.dma_start(
-                        out=tile[first + 4 * a + r : P : 32, :].bitcast(I32), in_=scales[a, r:16:4, :].bitcast(I32)
-                    )
+        def load_wc(tile, b, n0, n1):
+            nc.sync.dma_start(
+                out=tile[:], in_=wc[b * HALF : (b + 1) * HALF, n0:n1].rearrange("(p t) n -> p t n", t=PACK)
+            )
 
         nc.vector.memset(prod_scales[:].bitcast(I32), 0)
         nc.vector.memset(shop_scales[:].bitcast(I32), 0)
@@ -76,66 +68,60 @@ def tile_list_fatigue_brand_affinity_kernel(
         nc.vector.memset(warm[:, 0:1], 1.0)
         nc.scalar.activation(out=warm[:, 1:2], in_=warm[:, 0:1], func=ACT.Abs_reciprocal_sqrt)
 
-        nc.sync.dma_start(idx2[:], offs2)
-        load_words(nc.sync, shop_words[FAT], tab2_words[FAT])
-        nc.sync.dma_start(idx[:], offs)
-        load_scales_by_row(prod_scales, tab_scales, 0)
-        load_scales_by_quadrant(shop_scales, tab2_scales, 8)
-        load_words(nc.sync, prod_words[FAT], tab_words[FAT])
-        load_words(nc.sync, shop_words[AFF], tab2_words[AFF])
-        nc.sync.dma_start(out=margins[:, :, 0:PACK], in_=margin.rearrange("(b p t) -> p b t", b=2, t=PACK))
-        load_words(nc.sync, prod_words[AFF], tab_words[AFF])
+        def load_shop_scales():
+            for q in range(4):
+                nc.sync.dma_start(
+                    out=shop_scales[32 * q + 8 : 32 * q + 16, :].bitcast(I32),
+                    in_=tab2_scales[:, 4 * q : 4 * q + 4, :].bitcast(I32),
+                )
+
+        def load_prod_scales():
+            for r in range(4):
+                for a in range(2):
+                    nc.sync.dma_start(
+                        out=prod_scales[4 * a + r : P : 32, :].bitcast(I32), in_=tab_scales[a, r:16:4, :].bitcast(I32)
+                    )
+
+        def load_margins():
+            nc.sync.dma_start(out=margins[:, :, 0:PACK], in_=margin.rearrange("(b p t) -> p b t", b=2, t=PACK))
 
         weights = {}
 
-        def load_wc():
-            for b in range(2):
-                weights["wc_raw", b] = reuse.tile(
-                    [P, PACK, N], F32, name=f"wc_raw{b}", align_bytes=64, offset=b * WC_HALF_BYTES
-                )
-                nc.sync.dma_start(
-                    out=weights["wc_raw", b][:],
-                    in_=wc[b * HALF : (b + 1) * HALF, :].rearrange("(p t) n -> p t n", t=PACK),
-                )
-
         def load_base_words():
-            weights["base_words"] = kept([P, 2, 2 * N], U8, "base_words", tag=f"shop_words{FAT}")
+            weights["words"] = kept([P, 2, 2 * N], U8, "base_words")
             nc.sync.dma_start(
-                out=weights["base_words"][:].bitcast(I32), in_=w4_words.rearrange("b p x -> p b x").bitcast(I32)
+                out=weights["words"][:].bitcast(I32), in_=w4_words.rearrange("b p x -> p b x").bitcast(I32)
             )
 
         def load_base_scales():
-            weights["base_scales"] = kept([P, 2, N], U8, "base_scales", tag="shop_scales")
+            weights["scales"] = kept([P, 2, N], U8, "base_scales", tag="shop_scales")
             for q in range(4):
                 nc.sync.dma_start(
-                    out=weights["base_scales"][32 * q : 32 * q + 4, :, :].bitcast(I32),
+                    out=weights["scales"][32 * q : 32 * q + 4, :, :].bitcast(I32),
                     in_=w4_scales[:, 4 * q : 4 * q + 4, :].rearrange("b r n -> r b n").bitcast(I32),
                 )
 
         def gather(picked, window, offsets):
             nc.vector.tensor_copy(out=picked, in_=window.indirect(offsets))
 
-        v2_words, v_words = {}, {}
         v2_scales = kept([P, S2], U8, "v2_scales")
         listed_scales = kept([P, S], U8, "listed_scales")
         v_scales = kept([P, S], U8, "v_scales")
+        v_words = [kept([P, 2, HALF], U32, f"v_words{a}") for a in range(2)]
+        v2_words = [kept([P, S2], U32, f"v2_words{a}") for a in range(2)]
 
-        def pick_shop_words(a, tag=""):
-            v2_words[a] = kept([P, S2], U32, f"v2_words{a}", tag=tag)
-            gather(v2_words[a][:], shop_words[a], idx2[:])
+        def pick_shop_words(a, j0, j1):
+            gather(v2_words[a][:, j0:j1], shop_words[a], idx2[:, j0 // 16 : j1 // 16])
 
-        def pick_prod_words(a, b0, b1):
+        def pick_shop_scales(j0, j1):
+            gather(v2_scales[:, j0:j1], shop_scales[:], idx2[:, j0 // 16 : j1 // 16])
+
+        def pick_prod_words(a, b):
             gather(
-                v_words[a][:, b0:b1, :].rearrange("p b (t s) -> p b s t", t=PACK),
+                v_words[a][:, b : b + 1, :].rearrange("p b (t s) -> p b s t", t=PACK),
                 prod_words[a],
-                idx[:, b0 * HALF // 16 : b1 * HALF // 16],
+                idx[:, b * HALF // 16 : (b + 1) * HALF // 16],
             )
-
-        def pick_prod_scales():
-            gather(listed_scales[:], prod_scales[:], idx[:])
-
-        def pick_shop_scales():
-            gather(v2_scales[:], shop_scales[:], idx2[:])
 
         def order_prod_scales(b):
             half = slice(b * HALF, (b + 1) * HALF)
@@ -155,280 +141,280 @@ def tile_list_fatigue_brand_affinity_kernel(
                 stop=True,
             )
 
-        inverse_root = {}
-        damp, h_bf, h_words, h_scales = {}, {}, {}, {}
-        slabs = []
-        for g, (j0, width) in enumerate(GROUPS):
-            for b in range(2):
-                inverse_root[g, b] = damp[g, b] = kept([P, PACK, width], F32, f"damp{g}{b}")
-                if (g, b) != (0, 0):
-                    h_bf[g, b] = kept([P, width * PACK], BF16, f"h_bf{g}{b}")[:]
-                h_words[g, b] = kept([P, width], U32, f"h_words{g}{b}")
-                h_scales[g, b] = kept([P, width], U8, f"h_scales{g}{b}")
-                slots = HALF // width
-                slabs.extend((g, b, t0, slots) for t0 in range(0, PACK, slots))
-        squared = {}
+        roots, damp, squared, sums, h_bf = {}, {}, {}, {}, {}
 
-        def square(k):
-            g, b, t0, slots = slabs[k]
-            j0, width = GROUPS[g]
-            if k in (2, 3, 6, 7) or 10 <= k < 14:
-                f_bank = psum_out.tile([P, slots, width], F32, name=f"acc{k % 4 if k < 8 else k - 10}")
-            else:
-                f_bank = psum.tile([P, slots, width], F32, name="f_bank")
-            for s in range(slots):
-                table_product(f_bank[:, s, :], FAT, b, t0 + s, j0, width)
-            if k == 11:
-                squared[k] = kept([P, slots, width], F32, "squared11", tag="wc_bf1")[:]
-            else:
-                squared[k] = ring.tile([P, slots, width], F32, name="squared")[:]
-            nc.scalar.activation(out=squared[k], in_=f_bank[:], func=ACT.Square)
+        def square(k, onto=None):
+            g, b = BLOCKS[k // 2]
+            f_bank = bank(f_bank_of(k), [P, 2, GROUP], f"f{k}")
+            for s in range(2):
+                table_product(f_bank[:, s, :], FAT, b, 2 * (k % 2) + s, g * GROUP, GROUP)
+            squared[k] = onto if onto is not None else ring.tile([P, 2, GROUP], F32, name="squared")
+            nc.scalar.activation(out=squared[k][:], in_=f_bank[:], func=ACT.Square)
 
-        def root(k):
-            g, b, t0, slots = slabs[k]
-            nc.scalar.activation(
-                out=inverse_root[g, b][:, t0 : t0 + slots, :], in_=squared[k], func=ACT.Abs_reciprocal_sqrt, bias=1.0
-            )
+        def root(k, onto=None):
+            roots[k] = onto if onto is not None else kept([P, 2, GROUP], F32, f"roots{k}")
+            nc.scalar.activation(out=roots[k][:], in_=squared[k][:], func=ACT.Abs_reciprocal_sqrt, bias=1.0)
 
         def square_root(k):
-            g, b, t0, slots = slabs[k]
-            root_k = inverse_root[g, b][:, t0 : t0 + slots, :]
-            nc.scalar.activation(out=root_k, in_=root_k, func=ACT.Square)
+            nc.scalar.activation(out=roots[k][:], in_=roots[k][:], func=ACT.Square)
 
-        def roots(k0, k1):
-            for k in range(k0, k1):
-                if k + 1 < len(slabs):
-                    square(k + 1)
-                if k - 1 in SCALAR_SQUARES:
-                    square_root(k - 1)
-                root(k)
+        def weigh(k, cols=slice(0, GROUP)):
+            n = k // 2
+            b = BLOCKS[n][1]
+            for t in range(2 * (k % 2), 2 * (k % 2) + 2):
+                root_t, margin_t = roots[k][:, t % 2, cols], margins[:, b, t : t + 1]
+                if k in GPSIMD_MARGINS:
+                    nc.gpsimd.tensor_scalar(
+                        out=damp[n][:, t, cols], in0=root_t, scalar1=margin_t, scalar2=0.0, op0=MULT, op1=ADD
+                    )
+                elif k in SCALAR_SQUARES:
+                    nc.vector.tensor_scalar_mul(out=damp[n][:, t, cols], in0=root_t, scalar1=margin_t)
+                else:
+                    nc.vector.scalar_tensor_tensor(
+                        out=damp[n][:, t, cols], in0=root_t, scalar=margin_t, in1=root_t, op0=MULT, op1=MULT
+                    )
 
-        def weigh(g, b, t):
-            root_t = inverse_root[g, b][:, t, :]
-            k = max(n for n, slab in enumerate(slabs) if slab[0:2] == (g, b) and slab[2] <= t)
-            if k in GPSIMD_MARGINS:
-                nc.gpsimd.tensor_scalar(
-                    out=damp[g, b][:, t, :], in0=root_t, scalar1=margins[:, b, t : t + 1], scalar2=0.0,
-                    op0=MULT, op1=ADD,
-                )
-            elif k in SCALAR_SQUARES:
-                nc.vector.tensor_scalar_mul(out=damp[g, b][:, t, :], in0=root_t, scalar1=margins[:, b, t : t + 1])
-            else:
-                nc.vector.scalar_tensor_tensor(
-                    out=damp[g, b][:, t, :], in0=root_t, scalar=margins[:, b, t : t + 1], in1=root_t,
-                    op0=MULT, op1=MULT,
-                )
-
-        a_banks = {}
-
-        def affinity_sums(g, b, c, pool=psum, name="a_bank"):
-            a_banks[g, b, c] = pool.tile([P, PACK, P], F32, name=name)
+        def affinity_sums(n, c, where):
+            g, b = BLOCKS[n]
+            sums[n, c] = bank(where, [P, PACK, P], f"a{n}{c}")
             for t in range(PACK):
-                table_product(a_banks[g, b, c][:, t, :], AFF, b, t, GROUPS[g][0] + c * P, P)
+                table_product(sums[n, c][:, t, :], AFF, b, t, g * GROUP + c * P, P)
 
-        def affinity(g, b, c, pool=psum, name="a_bank"):
-            if (g, b, c) not in a_banks:
-                affinity_sums(g, b, c, pool, name)
-            a_bank = a_banks[g, b, c]
+        def affinity(n, c):
             nc.vector.tensor_tensor(
-                out=h_bf[g, b][:, c * HALF : (c + 1) * HALF].rearrange("p (k i t) -> p k t i", i=2, t=PACK),
-                in0=a_bank[:].rearrange("p t (k i) -> p k t i", i=2),
-                in1=damp[g, b][:, :, c * P : (c + 1) * P].rearrange("p t (k i) -> p k t i", i=2),
+                out=h_bf[n][:, c * HALF : (c + 1) * HALF].rearrange("p (k i t) -> p k t i", i=2, t=PACK),
+                in0=sums[n, c][:].rearrange("p t (k i) -> p k t i", i=2),
+                in1=damp[n][:, :, c * P : (c + 1) * P].rearrange("p t (k i) -> p k t i", i=2),
                 op=MULT,
             )
 
-        def quantise_h(g, b, c0, c1):
-            nc.vector.quantize_mx(
-                out=h_words[g, b][:, c0 * P : c1 * P].bitcast(FP8X4),
-                scales=h_scales[g, b][:, c0 * P : c1 * P],
-                in_=h_bf[g, b][:, c0 * HALF : c1 * HALF],
-            )
+        h_words = [kept([P, S2], U32, f"h_words{b}") for b in range(2)]
+        h_scales = [kept([P, S2], U8, f"h_scales{b}") for b in range(2)]
+        wc_words = [kept([P, N], U32, f"wc_words{b}") for b in range(2)]
+        wc_scales = [kept([P, N], U8, f"wc_scales{b}") for b in range(2)]
 
-        wc_bf, wc_words, wc_scales = {}, {}, {}
+        def quantise_h(b, j0, rounded):
+            cols = slice(j0, j0 + rounded.shape[1] // PACK)
+            nc.vector.quantize_mx(out=h_words[b][:, cols].bitcast(FP8X4), scales=h_scales[b][:, cols], in_=rounded)
 
-        def round_wc_scalar(b, n0, n1):
+        def quantise_wc(b, n0, rounded):
+            cols = slice(n0, n0 + rounded.shape[1] // PACK)
+            nc.vector.quantize_mx(out=wc_words[b][:, cols].bitcast(FP8X4), scales=wc_scales[b][:, cols], in_=rounded)
+
+        def round_wc_scalar(rounded, raw):
             nc.scalar.copy(
-                out=wc_bf[b, n0].rearrange("p (k i t) -> p k t i", i=4, t=PACK),
-                in_=weights["wc_raw", b][:, :, n0:n1].rearrange("p t (k i) -> p k t i", i=4),
+                out=rounded.rearrange("p (k i t) -> p k t i", i=4, t=PACK),
+                in_=raw.rearrange("p t (k i) -> p k t i", i=4),
             )
 
-        def round_wc_gpsimd(b, n0, n1):
+        def round_wc_gpsimd(rounded, raw):
             nc.gpsimd.tensor_scalar(
-                out=wc_bf[b, n0].rearrange("p (n t) -> p n t", t=PACK),
-                in0=weights["wc_raw", b][:, :, n0:n1].rearrange("p t n -> p n t"),
+                out=rounded.rearrange("p (n t) -> p n t", t=PACK),
+                in0=raw.rearrange("p t n -> p n t"),
                 scalar1=1.0, scalar2=0.0, op0=MULT, op1=ADD,
-            )
-
-        for b in range(2):
-            wc_words[b] = kept([P, N], U32, f"wc_words{b}")
-            wc_scales[b] = kept([P, N], U8, f"wc_scales{b}")
-
-        def quantise_wc(b, n0=0, n1=N):
-            nc.vector.quantize_mx(
-                out=wc_words[b][:, n0:n1].bitcast(FP8X4), scales=wc_scales[b][:, n0:n1], in_=wc_bf[b, n0]
             )
 
         acc = {}
 
-        def open_bank(bank, pool, name):
-            g, first, width, lo, hi = bank
-            acc[bank] = pool.tile([P, hi - lo, width], F32, name=name)
+        def open_part(part, where):
+            j0, width, lo, hi = part
+            acc[part] = bank(where, [P, hi - lo, width], f"acc{j0}_{lo}")
 
-        def brands(bank, terms, opens=False, closes=False):
-            g, first, width, lo, hi = bank
-            cols = slice(first, first + width)
+        def brands(part, terms, opens=False, closes=False):
+            j0, width, lo, hi = part
+            cols = slice(j0, j0 + width)
             steps = [(nt, kind, b) for nt in range(lo, hi) for kind, b in terms]
-            for n, (nt, kind, b) in enumerate(steps):
+            for m, (nt, kind, b) in enumerate(steps):
                 tile = slice(nt * P, (nt + 1) * P)
                 if kind == BASE:
-                    codes = weights["base_words"][:, b, 2 * nt * P : 2 * (nt + 1) * P].bitcast(FP4X4)
-                    scales = weights["base_scales"][:, b, tile]
+                    codes = weights["words"][:, b, 2 * nt * P : 2 * (nt + 1) * P].bitcast(FP4X4)
+                    scales = weights["scales"][:, b, tile]
                 else:
                     codes = wc_words[b][:, tile].bitcast(FP8X4)
                     scales = wc_scales[b][:, tile]
                 nc.tensor.matmul_mx(
-                    out=acc[bank][:, nt - lo, :],
+                    out=acc[part][:, nt - lo, :],
                     lhsT=codes,
                     lhsT_scale=scales,
-                    rhs=h_words[g, b][:, cols].bitcast(FP8X4),
-                    rhs_scale=h_scales[g, b][:, cols],
-                    start=opens and n == 0,
-                    stop=closes and n == len(steps) - 1,
+                    rhs=h_words[b][:, cols].bitcast(FP8X4),
+                    rhs_scale=h_scales[b][:, cols],
+                    start=opens and m == 0,
+                    stop=closes and m == len(steps) - 1,
                 )
 
-        def store(bank, copy, queue=nc.sync):
-            g, first, width, lo, hi = bank
-            j0 = GROUPS[g][0] + first
-            staged = kept([P, hi - lo, width], F32, f"staged{g}_{first}_{lo}")
-            copy(out=staged[:], in_=acc[bank][:])
+        def store(part, copy, queue=nc.sync):
+            j0, width, lo, hi = part
+            staged = kept([P, hi - lo, width], F32, f"staged{j0}_{lo}")
+            copy(out=staged[:], in_=acc[part][:])
             queue.dma_start(
                 out=out[lo * P : hi * P, j0 : j0 + width].rearrange("(nt p) j -> p nt j", p=P), in_=staged[:]
             )
 
-        wide = [(0, 0, HALF, nt, nt + 1) for nt in range(4)]
-        middle = [(1, 0, 2 * P, 0, 2), (1, 0, 2 * P, 2, 4)]
-        last = [(2, 0, P, 0, 4), (2, P, P, 0, 3), (2, P, P, 3, 4)]
+        wide = [(0, HALF, nt, nt + 1) for nt in range(4)]
+        middle = [(HALF, GROUP, 0, 2), (HALF, GROUP, 2, 4)]
+        last = [(768, P, 0, 4), (896, P, 0, 3), (896, P, 3, 4)]
+        both = [[(BASE, b), (CAMPAIGN, b)] for b in range(2)]
 
-        pick_shop_words(FAT)
-        pick_prod_scales()
+        def f_bank_of(k):
+            return k % 2 if k < 9 else 2 + (k - 9) % 2
+
+        def a_bank_of(n, c):
+            return 1 - c
+
+        wc_first = kept([P, PACK, GROUP], F32, "wc_first")
+        wc_second = kept([P, PACK, GROUP], F32, "wc_second")
+        wc_upper = reuse.tile([P, PACK, N], F32, name="wc_upper", align_bytes=64, offset=0)
+
+        nc.sync.dma_start(idx2[:], offs2)
+        load_words(shop_words[FAT], tab2_words[FAT])
+        nc.sync.dma_start(idx[:], offs)
+        load_prod_scales()
+        load_shop_scales()
+        load_words(prod_words[FAT], tab_words[FAT])
+        load_words(shop_words[AFF], tab2_words[AFF])
+        load_margins()
+        load_words(prod_words[AFF], tab_words[AFF])
+        load_wc(wc_first, 0, 0, GROUP)
         load_base_words()
+        pick_shop_words(FAT, 0, S2)
+        gather(listed_scales[:], prod_scales[:], idx[:])
         order_prod_scales(0)
         order_prod_scales(1)
-        pick_shop_scales()
-        v_words[FAT] = kept([P, 2, HALF], U32, "v_words_fatigue", tag="prod_scales")
-        v_words[AFF] = kept([P, 2, HALF], U32, "v_words_affinity")
-        pick_prod_words(FAT, 0, 1)
-        pick_prod_words(FAT, 1, 2)
-        load_wc()
+        pick_shop_scales(0, S2)
         load_base_scales()
+        load_wc(wc_upper, 1, 0, N)
+        load_wc(wc_second, 0, GROUP, N)
+
+        pick_prod_words(FAT, 0)
+        pick_prod_words(FAT, 1)
         for k in (0, 2):
             square(k)
             square(k + 1)
             root(k)
             root(k + 1)
         square(4)
-        roots(4, 9)
-        pick_shop_words(AFF, tag="listed_scales")
-        damp[0, 0] = kept([P, PACK, HALF], F32, "damp_first", tag=f"shop_words{AFF}")
-        for t in range(PACK):
-            weigh(0, 0, t)
-        pick_prod_words(AFF, 0, 1)
-        pick_prod_words(AFF, 1, 2)
-        wc_bf[0, 0] = kept([P, N // 2 * PACK], BF16, "wc_bf_first", tag="prod_affinity")[:]
-        round_wc_gpsimd(0, 0, N // 2)
-        h_bf[0, 0] = kept([P, HALF * PACK], BF16, "h_bf00")[:]
-        for c in range(4):
-            affinity_sums(0, 0, c, psum_out, f"acc{c}")
-        for c in range(4):
-            affinity_sums(0, 1, c, psum, "a_bank" if c < 2 else "f_bank")
-        for c in range(4):
-            affinity(0, 0, c)
-        roots(9, 12)
-        square(13)
-        wc_bf[1, 0] = kept([P, N * PACK], BF16, "wc_bf1")[:]
-        round_wc_scalar(1, 0, N)
-        root(12)
-        damp[0, 1] = kept([P, PACK, HALF], F32, "damp_late", tag=f"shop_words{AFF}")
-        weigh(0, 1, 0)
-        quantise_h(0, 0, 0, 4)
-        quantise_wc(0, 0, N // 2)
+        for k in range(4, 8):
+            square(k + 1)
+            if k - 1 in SCALAR_SQUARES:
+                square_root(k - 1)
+            root(k)
+        pick_shop_words(AFF, 0, S2)
+        pair = kept([P, 2, PACK, GROUP], F32, "damp01", tag=f"shop_words{AFF}")
+        damp[0], damp[1] = pair[:, 0], pair[:, 1]
+        for k in range(4):
+            weigh(k)
+        pick_prod_words(AFF, 0)
+        pick_prod_words(AFF, 1)
+        for n in range(2):
+            for c in range(2):
+                affinity_sums(n, c, 2 + 2 * n + c)
         for c in range(2):
-            open_bank(wide[c], psum_out, f"acc{c}")
-            brands(wide[c], [(BASE, 0), (CAMPAIGN, 0)], opens=True)
-        for t in range(1, PACK):
-            weigh(0, 1, t)
-        wc_bf[0, N // 2] = kept([P, N // 2 * PACK], BF16, "wc_bf_second", tag="damp01")[:]
-        round_wc_gpsimd(0, N // 2, N)
-        for c in range(4):
-            affinity(0, 1, c)
-            if c < 2:
-                affinity_sums(1, 0, c)
-        for c in range(2, 4):
-            open_bank(wide[c], psum_out, f"acc{c}")
-            brands(wide[c], [(BASE, 0)], opens=True)
-        quantise_wc(0, N // 2, N)
-        for c in range(2, 4):
-            brands(wide[c], [(CAMPAIGN, 0)])
-        damp[1, 0] = kept([P, PACK, 2 * P], F32, "damp_middle", tag=f"shop_words{AFF}")
-        for t in range(PACK):
-            weigh(1, 0, t)
-        quantise_h(0, 1, 0, 4)
-        roots(13, 14)
-        root(14)
-        square(15)
+            affinity_sums(2, c, a_bank_of(2, c))
+        for c in range(2):
+            affinity_sums(3, c, 6 + c)
+        wc_bf = kept([P, GROUP * PACK], BF16, "wc_bf_first", tag=f"prod_words{AFF}")
+        round_wc_gpsimd(wc_bf[:], wc_first[:])
+        rounded = kept([P, 2 * GROUP * PACK], BF16, "h_bf01")
+        h_bf[0], h_bf[1] = rounded[:, : GROUP * PACK], rounded[:, GROUP * PACK :]
+        for n in range(2):
+            for c in range(2):
+                affinity(n, c)
+        square(9)
+        root(8)
+        square(10)
+        root(9)
+        square(11, kept([P, 2, GROUP], F32, "squared11"))
+        root(10)
+        square(12, kept([P, 2, GROUP], F32, "squared12"))
+        square_root(10)
+        for k in range(13, 16):
+            square(k, kept([P, 2, GROUP], F32, f"squared{k}"))
+        wc_bf_upper = kept([P, N * PACK], BF16, "wc_bf_upper")
+        round_wc_scalar(wc_bf_upper[:], wc_upper[:])
+        for k in range(11, 14):
+            root(k, reuse.tile([P, 2, GROUP], F32, name=f"roots{k}", align_bytes=64, offset=(k - 11) * 2048))
+        square_root(12)
+        square_root(13)
+        root(14, reuse.tile([P, 2, GROUP], F32, name="roots14", align_bytes=64, offset=3 * 2048))
+        root(15, kept([P, 2, GROUP], F32, "roots15", tag="squared11"))
         square_root(14)
-        root(15)
-        square_root(15)
-        damp[1, 1] = kept([P, PACK, 2 * P], F32, "damp_after_root10", tag="damp10")
+        pair = kept([P, 2, PACK, GROUP], F32, "damp23", tag=f"shop_words{AFF}")
+        damp[2], damp[3] = pair[:, 0], pair[:, 1]
+        weigh(4)
+        quantise_h(0, 0, rounded[:])
+        quantise_wc(0, 0, wc_bf[:])
+        for nt in range(2):
+            open_part(wide[nt], 4 + nt)
+            brands(wide[nt], both[0], opens=True)
+        for k in range(5, 8):
+            weigh(k)
+        wc_bf = kept([P, GROUP * PACK], BF16, "wc_bf_second", tag="roots7")
+        round_wc_gpsimd(wc_bf[:], wc_second[:])
+        rounded = kept([P, 2 * GROUP * PACK], BF16, "h_bf23")
+        h_bf[2], h_bf[3] = rounded[:, : GROUP * PACK], rounded[:, GROUP * PACK :]
+        for n in (2, 3):
+            for c in range(2):
+                affinity(n, c)
         for c in range(2):
-            weigh(1, 1, c)
+            affinity_sums(4, c, a_bank_of(4, c))
+        for nt in range(2, 4):
+            open_part(wide[nt], 4 + nt)
+            brands(wide[nt], [(BASE, 0)], opens=True)
+        damp[4] = kept([P, PACK, GROUP], F32, "damp4", tag=f"shop_words{AFF}")
+        weigh(8)
+        quantise_h(1, 0, rounded[:])
+        weigh(9)
+        for nt in range(4):
+            brands(wide[nt], [(BASE, 1)])
+        quantise_wc(0, GROUP, wc_bf[:])
+        for nt in range(2, 4):
+            brands(wide[nt], [(CAMPAIGN, 0)])
+        damp[5] = kept([P, PACK, GROUP], F32, "damp5", tag="roots7")
+        weigh(10)
+        for n in range(4, 8):
+            h_bf[n] = kept([P, GROUP * PACK], BF16, f"h_bf{n}")[:]
         for c in range(2):
-            affinity(1, 0, c)
-            affinity_sums(1, 1, c)
-        for c in range(4):
-            brands(wide[c], [(BASE, 1)])
+            affinity(4, c)
+            affinity_sums(5, c, a_bank_of(5, c))
+        quantise_wc(1, 0, wc_bf_upper[:])
+        for nt in range(4):
+            brands(wide[nt], [(CAMPAIGN, 1)], closes=True)
+        weigh(11)
+        quantise_h(0, 2 * GROUP, h_bf[4])
         for c in range(2):
-            weigh(1, 1, 2 + c)
-        quantise_h(1, 0, 0, 2)
-        quantise_wc(1)
-        damp[2, 0] = kept([P, PACK, 2 * P], F32, "damp_after_h10", tag="h_bf10")
-        for c in range(2):
-            weigh(2, 0, c)
-        for c in range(2):
-            affinity(1, 1, c)
-            affinity_sums(2, 0, c)
-        for c in range(4):
-            brands(wide[c], [(CAMPAIGN, 1)], closes=True)
-            store(wide[c], nc.scalar.copy)
-        for c in range(2):
-            weigh(2, 0, 2 + c)
-        quantise_h(1, 1, 0, 2)
-        both = [[(BASE, b), (CAMPAIGN, b)] for b in range(2)]
-        damp[2, 1] = kept([P, PACK, 2 * P], F32, "damp_after_root20", tag="damp20")
-        for c in range(2):
-            weigh(2, 1, c)
-        for c in range(2):
-            affinity(2, 0, c)
-            affinity_sums(2, 1, c)
-        for c in range(2):
-            open_bank(middle[c], psum, "f_bank")
+            open_part(middle[c], 2 + c)
             brands(middle[c], both[0], opens=True)
+        damp[6] = kept([P, PACK, GROUP], F32, "damp6", tag="h_bf4")
+        weigh(12)
+        weigh(13)
         for c in range(2):
-            weigh(2, 1, 2 + c)
-        quantise_h(2, 0, 0, 2)
-        affinity(2, 1, 0)
-        affinity(2, 1, 1)
+            affinity(5, c)
+            affinity_sums(6, c, a_bank_of(6, c))
+        for c in range(2):
+            store(wide[c], nc.vector.tensor_copy)
+        quantise_h(1, 2 * GROUP, h_bf[5])
+        damp[7] = kept([P, PACK, GROUP], F32, "damp7", tag="h_bf5")
+        weigh(14)
+        for c in range(2):
+            affinity(6, c)
+            affinity_sums(7, c, a_bank_of(7, c))
         for c in range(2):
             brands(middle[c], both[1], closes=True)
-        store(middle[0], nc.scalar.copy)
-        for n, bank in enumerate(last):
-            open_bank(bank, psum_out, f"acc{n}")
-        for bank in last:
-            brands(bank, both[0], opens=True)
-        quantise_h(2, 1, 0, 1)
+        for nt in range(2, 4):
+            store(wide[nt], nc.scalar.copy)
+        weigh(15, slice(0, P))
+        quantise_h(0, 3 * GROUP, h_bf[6])
+        for part, where in zip(last, (4, 5, 6)):
+            open_part(part, where)
+            brands(part, both[0], opens=True)
+        affinity(7, 0)
+        weigh(15, slice(P, GROUP))
+        for c in range(2):
+            store(middle[c], nc.scalar.copy)
+        quantise_h(1, 3 * GROUP, h_bf[7][:, :HALF])
         brands(last[0], both[1], closes=True)
-        quantise_h(2, 1, 1, 2)
-        store(middle[1], nc.vector.tensor_copy)
+        affinity(7, 1)
+        quantise_h(1, 3 * GROUP + P, h_bf[7][:, HALF:])
         store(last[0], nc.vector.tensor_copy)
         brands(last[1], both[1], closes=True)
         brands(last[2], both[1], closes=True)

@@ -23,9 +23,10 @@ HALF = 512
 GROUP = 256
 AFF, FAT = 0, 1
 BASE, CAMPAIGN = 0, 1
-BLOCKS = ((0, 0), (1, 0), (0, 1), (1, 1), (2, 0), (2, 1), (3, 0), (3, 1))
-SCALAR_SQUARES = (6, 10, 12, 13, 14)
-GPSIMD_MARGINS = (10, 12, 13, 14)
+BLOCKS = ((0, 512, 0), (0, 512, 1), (512, 256, 0), (512, 256, 1), (768, 256, 0), (768, 256, 1))
+SLABS = tuple((n, t, HALF // BLOCKS[n][1]) for n in range(6) for t in range(0, PACK, HALF // BLOCKS[n][1]))
+SCALAR_SQUARES = (6, 10, 12, 14, 15)
+GPSIMD_MARGINS = (10, 12, 14)
 
 
 def tile_list_fatigue_brand_affinity_kernel(
@@ -144,41 +145,43 @@ def tile_list_fatigue_brand_affinity_kernel(
         roots, damp, squared, sums, h_bf = {}, {}, {}, {}, {}
 
         def square(k, onto=None):
-            g, b = BLOCKS[k // 2]
-            f_bank = bank(f_bank_of(k), [P, 2, GROUP], f"f{k}")
-            for s in range(2):
-                table_product(f_bank[:, s, :], FAT, b, 2 * (k % 2) + s, g * GROUP, GROUP)
-            squared[k] = onto if onto is not None else ring.tile([P, 2, GROUP], F32, name="squared")
+            n, t0, slots = SLABS[k]
+            j0, width, b = BLOCKS[n]
+            f_bank = bank(f_bank_of(k), [P, HALF], f"f{k}")
+            for s in range(slots):
+                table_product(f_bank[:, s * width : (s + 1) * width], FAT, b, t0 + s, j0, width)
+            squared[k] = onto if onto is not None else ring.tile([P, HALF], F32, name="squared")
             nc.scalar.activation(out=squared[k][:], in_=f_bank[:], func=ACT.Square)
 
         def root(k, onto=None):
-            roots[k] = onto if onto is not None else kept([P, 2, GROUP], F32, f"roots{k}")
+            roots[k] = onto if onto is not None else kept([P, HALF], F32, f"roots{k}")
             nc.scalar.activation(out=roots[k][:], in_=squared[k][:], func=ACT.Abs_reciprocal_sqrt, bias=1.0)
 
         def square_root(k):
             nc.scalar.activation(out=roots[k][:], in_=roots[k][:], func=ACT.Square)
 
-        def weigh(k, cols=slice(0, GROUP)):
-            n = k // 2
-            b = BLOCKS[n][1]
-            for t in range(2 * (k % 2), 2 * (k % 2) + 2):
-                root_t, margin_t = roots[k][:, t % 2, cols], margins[:, b, t : t + 1]
+        def weigh(k, only=None):
+            n, t0, slots = SLABS[k]
+            j0, width, b = BLOCKS[n]
+            for s in range(slots) if only is None else (only,):
+                t = t0 + s
+                root_t, margin_t = roots[k][:, s * width : (s + 1) * width], margins[:, b, t : t + 1]
                 if k in GPSIMD_MARGINS:
                     nc.gpsimd.tensor_scalar(
-                        out=damp[n][:, t, cols], in0=root_t, scalar1=margin_t, scalar2=0.0, op0=MULT, op1=ADD
+                        out=damp[n][:, t, :], in0=root_t, scalar1=margin_t, scalar2=0.0, op0=MULT, op1=ADD
                     )
                 elif k in SCALAR_SQUARES:
-                    nc.vector.tensor_scalar_mul(out=damp[n][:, t, cols], in0=root_t, scalar1=margin_t)
+                    nc.vector.tensor_scalar_mul(out=damp[n][:, t, :], in0=root_t, scalar1=margin_t)
                 else:
                     nc.vector.scalar_tensor_tensor(
-                        out=damp[n][:, t, cols], in0=root_t, scalar=margin_t, in1=root_t, op0=MULT, op1=MULT
+                        out=damp[n][:, t, :], in0=root_t, scalar=margin_t, in1=root_t, op0=MULT, op1=MULT
                     )
 
         def affinity_sums(n, c, where):
-            g, b = BLOCKS[n]
+            j0, width, b = BLOCKS[n]
             sums[n, c] = bank(where, [P, PACK, P], f"a{n}{c}")
             for t in range(PACK):
-                table_product(sums[n, c][:, t, :], AFF, b, t, g * GROUP + c * P, P)
+                table_product(sums[n, c][:, t, :], AFF, b, t, j0 + c * P, P)
 
         def affinity(n, c):
             nc.vector.tensor_tensor(
@@ -258,9 +261,6 @@ def tile_list_fatigue_brand_affinity_kernel(
         def f_bank_of(k):
             return k % 2 if k < 9 else 2 + (k - 9) % 2
 
-        def a_bank_of(n, c):
-            return 1 - c
-
         wc_first = kept([P, PACK, GROUP], F32, "wc_first")
         wc_second = kept([P, PACK, GROUP], F32, "wc_second")
         wc_upper = reuse.tile([P, PACK, N], F32, name="wc_upper", align_bytes=64, offset=0)
@@ -299,122 +299,119 @@ def tile_list_fatigue_brand_affinity_kernel(
                 square_root(k - 1)
             root(k)
         pick_shop_words(AFF, 0, S2)
-        pair = kept([P, 2, PACK, GROUP], F32, "damp01", tag=f"shop_words{AFF}")
-        damp[0], damp[1] = pair[:, 0], pair[:, 1]
+        damp[0] = kept([P, PACK, HALF], F32, "damp0", tag=f"shop_words{AFF}")
         for k in range(4):
             weigh(k)
         pick_prod_words(AFF, 0)
         pick_prod_words(AFF, 1)
-        for n in range(2):
-            for c in range(2):
-                affinity_sums(n, c, 2 + 2 * n + c)
-        for c in range(2):
-            affinity_sums(2, c, a_bank_of(2, c))
-        for c in range(2):
-            affinity_sums(3, c, 6 + c)
+        for c in range(4):
+            affinity_sums(0, c, 2 + c)
+        for c, where in enumerate((1, 0, 6, 7)):
+            affinity_sums(1, c, where)
         wc_bf = kept([P, GROUP * PACK], BF16, "wc_bf_first", tag=f"prod_words{AFF}")
         round_wc_gpsimd(wc_bf[:], wc_first[:])
-        rounded = kept([P, 2 * GROUP * PACK], BF16, "h_bf01")
-        h_bf[0], h_bf[1] = rounded[:, : GROUP * PACK], rounded[:, GROUP * PACK :]
-        for n in range(2):
-            for c in range(2):
-                affinity(n, c)
+        for n in range(len(BLOCKS)):
+            h_bf[n] = kept([P, BLOCKS[n][1] * PACK], BF16, f"h_bf{n}")[:]
+        for c in range(4):
+            affinity(0, c)
         square(9)
         root(8)
         square(10)
         root(9)
-        square(11, kept([P, 2, GROUP], F32, "squared11"))
+        square(11, kept([P, HALF], F32, "squared11"))
         root(10)
-        square(12, kept([P, 2, GROUP], F32, "squared12"))
+        square(12, kept([P, HALF], F32, "squared12"))
         square_root(10)
-        for k in range(13, 16):
-            square(k, kept([P, 2, GROUP], F32, f"squared{k}"))
+        square(13, kept([P, HALF], F32, "squared13"))
         wc_bf_upper = kept([P, N * PACK], BF16, "wc_bf_upper")
         round_wc_scalar(wc_bf_upper[:], wc_upper[:])
-        for k in range(11, 14):
-            root(k, reuse.tile([P, 2, GROUP], F32, name=f"roots{k}", align_bytes=64, offset=(k - 11) * 2048))
+        freed = [
+            reuse.tile([P, HALF], F32, name=f"freed{q}", align_bytes=64, offset=q * HALF * 4) for q in range(PACK)
+        ]
+        root(11, freed[0])
+        square(14, freed[1])
+        root(12, freed[2])
+        square(15, freed[3])
+        root(13, kept([P, HALF], F32, "roots13", tag="squared11"))
         square_root(12)
-        square_root(13)
-        root(14, reuse.tile([P, 2, GROUP], F32, name="roots14", align_bytes=64, offset=3 * 2048))
-        root(15, kept([P, 2, GROUP], F32, "roots15", tag="squared11"))
+        root(14)
+        root(15)
         square_root(14)
-        pair = kept([P, 2, PACK, GROUP], F32, "damp23", tag=f"shop_words{AFF}")
-        damp[2], damp[3] = pair[:, 0], pair[:, 1]
+        square_root(15)
+        damp[1] = kept([P, PACK, HALF], F32, "damp1", tag=f"shop_words{AFF}")
         weigh(4)
-        quantise_h(0, 0, rounded[:])
-        quantise_wc(0, 0, wc_bf[:])
+        quantise_h(0, 0, h_bf[0])
         for nt in range(2):
             open_part(wide[nt], 4 + nt)
-            brands(wide[nt], both[0], opens=True)
+            brands(wide[nt], [(BASE, 0)], opens=True)
         for k in range(5, 8):
             weigh(k)
-        wc_bf = kept([P, GROUP * PACK], BF16, "wc_bf_second", tag="roots7")
+        quantise_wc(0, 0, wc_bf[:])
+        for nt in range(2):
+            brands(wide[nt], [(CAMPAIGN, 0)])
+        wc_bf = kept([P, GROUP * PACK], BF16, "wc_bf_second", tag=f"prod_words{AFF}")
         round_wc_gpsimd(wc_bf[:], wc_second[:])
-        rounded = kept([P, 2 * GROUP * PACK], BF16, "h_bf23")
-        h_bf[2], h_bf[3] = rounded[:, : GROUP * PACK], rounded[:, GROUP * PACK :]
-        for n in (2, 3):
-            for c in range(2):
-                affinity(n, c)
+        for c in range(4):
+            affinity(1, c)
         for c in range(2):
-            affinity_sums(4, c, a_bank_of(4, c))
+            affinity_sums(2, c, 1 - c)
         for nt in range(2, 4):
             open_part(wide[nt], 4 + nt)
             brands(wide[nt], [(BASE, 0)], opens=True)
-        damp[4] = kept([P, PACK, GROUP], F32, "damp4", tag=f"shop_words{AFF}")
+        damp[2] = kept([P, PACK, GROUP], F32, "damp2", tag=f"shop_words{AFF}")
         weigh(8)
-        quantise_h(1, 0, rounded[:])
+        quantise_h(1, 0, h_bf[1])
         weigh(9)
         for nt in range(4):
             brands(wide[nt], [(BASE, 1)])
         quantise_wc(0, GROUP, wc_bf[:])
         for nt in range(2, 4):
             brands(wide[nt], [(CAMPAIGN, 0)])
-        damp[5] = kept([P, PACK, GROUP], F32, "damp5", tag="roots7")
+        damp[3] = kept([P, PACK, GROUP], F32, "damp3", tag=f"prod_words{AFF}")
         weigh(10)
-        for n in range(4, 8):
-            h_bf[n] = kept([P, GROUP * PACK], BF16, f"h_bf{n}")[:]
         for c in range(2):
-            affinity(4, c)
-            affinity_sums(5, c, a_bank_of(5, c))
+            affinity(2, c)
+            affinity_sums(3, c, 1 - c)
         quantise_wc(1, 0, wc_bf_upper[:])
         for nt in range(4):
             brands(wide[nt], [(CAMPAIGN, 1)], closes=True)
         weigh(11)
-        quantise_h(0, 2 * GROUP, h_bf[4])
+        quantise_h(0, 2 * GROUP, h_bf[2])
         for c in range(2):
             open_part(middle[c], 2 + c)
             brands(middle[c], both[0], opens=True)
-        damp[6] = kept([P, PACK, GROUP], F32, "damp6", tag="h_bf4")
+        damp[4] = kept([P, PACK, GROUP], F32, "damp4", tag="h_bf2")
         weigh(12)
-        weigh(13)
         for c in range(2):
-            affinity(5, c)
-            affinity_sums(6, c, a_bank_of(6, c))
+            affinity(3, c)
+            affinity_sums(4, c, 1 - c)
         for c in range(2):
             store(wide[c], nc.vector.tensor_copy)
-        quantise_h(1, 2 * GROUP, h_bf[5])
-        damp[7] = kept([P, PACK, GROUP], F32, "damp7", tag="h_bf5")
+        weigh(13)
+        quantise_h(1, 2 * GROUP, h_bf[3])
+        damp[5] = kept([P, PACK, GROUP], F32, "damp5", tag="h_bf3")
         weigh(14)
         for c in range(2):
-            affinity(6, c)
-            affinity_sums(7, c, a_bank_of(7, c))
+            affinity(4, c)
+            affinity_sums(5, c, 1 - c)
         for c in range(2):
             brands(middle[c], both[1], closes=True)
         for nt in range(2, 4):
             store(wide[nt], nc.scalar.copy)
-        weigh(15, slice(0, P))
-        quantise_h(0, 3 * GROUP, h_bf[6])
+        weigh(15, 0)
+        quantise_h(0, 3 * GROUP, h_bf[4][:, :HALF])
+        weigh(15, 1)
+        quantise_h(0, 3 * GROUP + P, h_bf[4][:, HALF:])
         for part, where in zip(last, (4, 5, 6)):
             open_part(part, where)
             brands(part, both[0], opens=True)
-        affinity(7, 0)
-        weigh(15, slice(P, GROUP))
+        for c in range(2):
+            affinity(5, c)
         for c in range(2):
             store(middle[c], nc.scalar.copy)
-        quantise_h(1, 3 * GROUP, h_bf[7][:, :HALF])
+        quantise_h(1, 3 * GROUP, h_bf[5][:, :HALF])
         brands(last[0], both[1], closes=True)
-        affinity(7, 1)
-        quantise_h(1, 3 * GROUP + P, h_bf[7][:, HALF:])
+        quantise_h(1, 3 * GROUP + P, h_bf[5][:, HALF:])
         store(last[0], nc.vector.tensor_copy)
         brands(last[1], both[1], closes=True)
         brands(last[2], both[1], closes=True)

@@ -21,12 +21,13 @@ P = 128
 PACK = 4
 HALF = 512
 GROUP = 256
+SHARE = 320
 AFF, FAT = 0, 1
 BASE, CAMPAIGN = 0, 1
 BLOCKS = ((0, 512, 0), (0, 512, 1), (512, 256, 0), (512, 256, 1), (768, 256, 0), (768, 256, 1))
 SLABS = tuple((n, t, HALF // BLOCKS[n][1]) for n in range(6) for t in range(0, PACK, HALF // BLOCKS[n][1]))
-SCALAR_SQUARES = (6, 10, 12, 14, 15)
-GPSIMD_MARGINS = (10, 12, 14)
+SCALAR_SQUARES = (6, 10, 12, 13, 14, 15)
+GPSIMD_MARGINS = (10, 12, 13, 14)
 
 
 def tile_list_fatigue_brand_affinity_kernel(
@@ -48,7 +49,10 @@ def tile_list_fatigue_brand_affinity_kernel(
 
         idx = lists.tile([P, S // 16], U16, name="idx")
         idx2 = lists.tile([P, S2 // 16], U16, name="idx2")
-        prod_words = [kept([P, T], U32, f"prod_words{a}")[:] for a in range(2)]
+        def placed(shape, dtype, name, kib):
+            return reuse.tile(shape, dtype, name=name, align_bytes=64, offset=kib * 1024)
+
+        prod_words = {AFF: placed([P, T], U32, "prod_affinity", 8)[:], FAT: kept([P, T], U32, "prod_fatigue")[:]}
         shop_words = [kept([P, T2], U32, f"shop_words{a}")[:] for a in range(2)]
         prod_scales = kept([P, T], U8, "prod_scales")
         shop_scales = kept([P, T2], U8, "shop_scales")
@@ -59,7 +63,7 @@ def tile_list_fatigue_brand_affinity_kernel(
 
         def load_wc(tile, b, n0, n1):
             nc.sync.dma_start(
-                out=tile[:], in_=wc[b * HALF : (b + 1) * HALF, n0:n1].rearrange("(p t) n -> p t n", t=PACK)
+                out=tile, in_=wc[b * HALF : (b + 1) * HALF, n0:n1].rearrange("(p t) n -> p t n", t=PACK)
             )
 
         nc.vector.memset(prod_scales[:].bitcast(I32), 0)
@@ -95,7 +99,8 @@ def tile_list_fatigue_brand_affinity_kernel(
             )
 
         def load_base_scales():
-            weights["scales"] = kept([P, 2, N], U8, "base_scales", tag="shop_scales")
+            weights["scales"] = kept([P, 2, N], U8, "base_scales")
+            nc.gpsimd.memset(weights["scales"][:].rearrange("p b n -> p (b n)").bitcast(I32), 0)
             for q in range(4):
                 nc.sync.dma_start(
                     out=weights["scales"][32 * q : 32 * q + 4, :, :].bitcast(I32),
@@ -261,9 +266,9 @@ def tile_list_fatigue_brand_affinity_kernel(
         def f_bank_of(k):
             return k % 2 if k < 9 else 2 + (k - 9) % 2
 
-        wc_first = kept([P, PACK, GROUP], F32, "wc_first")
-        wc_second = kept([P, PACK, GROUP], F32, "wc_second")
-        wc_upper = reuse.tile([P, PACK, N], F32, name="wc_upper", align_bytes=64, offset=0)
+        wc_first = kept([P, PACK, SHARE], F32, "wc_first")
+        wc_second = kept([P, PACK, SHARE], F32, "wc_second")
+        wc_upper = placed([P, PACK, 2 * N - 2 * SHARE], F32, "wc_upper", 0)
 
         nc.sync.dma_start(idx2[:], offs2)
         load_words(shop_words[FAT], tab2_words[FAT])
@@ -274,7 +279,7 @@ def tile_list_fatigue_brand_affinity_kernel(
         load_words(shop_words[AFF], tab2_words[AFF])
         load_margins()
         load_words(prod_words[AFF], tab_words[AFF])
-        load_wc(wc_first, 0, 0, GROUP)
+        load_wc(wc_first[:], 0, 0, SHARE)
         load_base_words()
         pick_shop_words(FAT, 0, S2)
         gather(listed_scales[:], prod_scales[:], idx[:])
@@ -282,8 +287,9 @@ def tile_list_fatigue_brand_affinity_kernel(
         order_prod_scales(1)
         pick_shop_scales(0, S2)
         load_base_scales()
-        load_wc(wc_upper, 1, 0, N)
-        load_wc(wc_second, 0, GROUP, N)
+        load_wc(wc_second[:, :, : N - SHARE], 0, SHARE, N)
+        load_wc(wc_second[:, :, N - SHARE :], 1, 0, 2 * SHARE - N)
+        load_wc(wc_upper[:], 1, 2 * SHARE - N, N)
 
         pick_prod_words(FAT, 0)
         pick_prod_words(FAT, 1)
@@ -293,7 +299,7 @@ def tile_list_fatigue_brand_affinity_kernel(
             root(k)
             root(k + 1)
         square(4)
-        for k in range(4, 8):
+        for k in range(4, 7):
             square(k + 1)
             if k - 1 in SCALAR_SQUARES:
                 square_root(k - 1)
@@ -304,36 +310,39 @@ def tile_list_fatigue_brand_affinity_kernel(
             weigh(k)
         pick_prod_words(AFF, 0)
         pick_prod_words(AFF, 1)
+        rounded = placed([P, (GROUP + 2 * N) * PACK], BF16, "rounded", 8)
+        wc_bf = rounded[:, GROUP * PACK :]
+        square(8)
+        if 6 in SCALAR_SQUARES:
+            square_root(6)
+        root(7, wc_bf[:, SHARE * PACK : SHARE * PACK + 2 * HALF].bitcast(F32))
         for c in range(4):
             affinity_sums(0, c, 2 + c)
-        for c, where in enumerate((1, 0, 6, 7)):
+        for c, where in ((2, 1), (3, 0), (0, 6), (1, 7)):
             affinity_sums(1, c, where)
-        wc_bf = kept([P, GROUP * PACK], BF16, "wc_bf_first", tag=f"prod_words{AFF}")
-        round_wc_gpsimd(wc_bf[:], wc_first[:])
-        for n in range(len(BLOCKS)):
+        round_wc_gpsimd(wc_bf[:, : SHARE * PACK], wc_first[:])
+        h_bf[1], h_bf[2] = rounded[:, : HALF * PACK], rounded[:, HALF * PACK : (HALF + GROUP) * PACK]
+        for n in (0, 4, 5):
             h_bf[n] = kept([P, BLOCKS[n][1] * PACK], BF16, f"h_bf{n}")[:]
         for c in range(4):
             affinity(0, c)
         square(9)
         root(8)
         square(10)
-        root(9)
+        root(9, placed([P, HALF], F32, "roots9", 18))
         square(11, kept([P, HALF], F32, "squared11"))
         root(10)
         square(12, kept([P, HALF], F32, "squared12"))
         square_root(10)
         square(13, kept([P, HALF], F32, "squared13"))
-        wc_bf_upper = kept([P, N * PACK], BF16, "wc_bf_upper")
-        round_wc_scalar(wc_bf_upper[:], wc_upper[:])
-        freed = [
-            reuse.tile([P, HALF], F32, name=f"freed{q}", align_bytes=64, offset=q * HALF * 4) for q in range(PACK)
-        ]
-        root(11, freed[0])
-        square(14, freed[1])
-        root(12, freed[2])
-        square(15, freed[3])
-        root(13, kept([P, HALF], F32, "roots13", tag="squared11"))
+        round_wc_scalar(wc_bf[:, 2 * SHARE * PACK :], wc_upper[:])
+        root(11, placed([P, HALF], F32, "roots11", 4))
+        root(12, placed([P, HALF], F32, "roots12", 0))
+        square(14, placed([P, HALF], F32, "squared14", 2))
         square_root(12)
+        root(13, kept([P, HALF], F32, "roots13", tag="squared12"))
+        square(15, kept([P, HALF], F32, "squared15", tag="squared11"))
+        square_root(13)
         root(14)
         root(15)
         square_root(14)
@@ -346,33 +355,33 @@ def tile_list_fatigue_brand_affinity_kernel(
             brands(wide[nt], [(BASE, 0)], opens=True)
         for k in range(5, 8):
             weigh(k)
-        quantise_wc(0, 0, wc_bf[:])
+        quantise_wc(0, 0, wc_bf[:, : GROUP * PACK])
         for nt in range(2):
             brands(wide[nt], [(CAMPAIGN, 0)])
-        wc_bf = kept([P, GROUP * PACK], BF16, "wc_bf_second", tag=f"prod_words{AFF}")
-        round_wc_gpsimd(wc_bf[:], wc_second[:])
-        for c in range(4):
+        round_wc_gpsimd(wc_bf[:, SHARE * PACK : 2 * SHARE * PACK], wc_second[:])
+        for c in (2, 3, 0, 1):
             affinity(1, c)
         for c in range(2):
             affinity_sums(2, c, 1 - c)
         for nt in range(2, 4):
             open_part(wide[nt], 4 + nt)
             brands(wide[nt], [(BASE, 0)], opens=True)
-        damp[2] = kept([P, PACK, GROUP], F32, "damp2", tag=f"shop_words{AFF}")
+        damp[2] = kept([P, PACK, GROUP], F32, "damp2", tag="h_bf0")
         weigh(8)
         quantise_h(1, 0, h_bf[1])
         weigh(9)
         for nt in range(4):
             brands(wide[nt], [(BASE, 1)])
-        quantise_wc(0, GROUP, wc_bf[:])
+        quantise_wc(0, GROUP, wc_bf[:, GROUP * PACK : N * PACK])
         for nt in range(2, 4):
             brands(wide[nt], [(CAMPAIGN, 0)])
-        damp[3] = kept([P, PACK, GROUP], F32, "damp3", tag=f"prod_words{AFF}")
+        damp[3] = placed([P, PACK, GROUP], F32, "damp3", 18)
+        h_bf[3] = placed([P, GROUP * PACK], BF16, "h_bf3", 22)[:]
         weigh(10)
         for c in range(2):
             affinity(2, c)
             affinity_sums(3, c, 1 - c)
-        quantise_wc(1, 0, wc_bf_upper[:])
+        quantise_wc(1, 0, wc_bf[:, N * PACK :])
         for nt in range(4):
             brands(wide[nt], [(CAMPAIGN, 1)], closes=True)
         weigh(11)
@@ -380,20 +389,20 @@ def tile_list_fatigue_brand_affinity_kernel(
         for c in range(2):
             open_part(middle[c], 2 + c)
             brands(middle[c], both[0], opens=True)
-        damp[4] = kept([P, PACK, GROUP], F32, "damp4", tag="h_bf2")
+        damp[4] = placed([P, PACK, GROUP], F32, "damp4", 4)
         weigh(12)
+        weigh(13)
         for c in range(2):
             affinity(3, c)
             affinity_sums(4, c, 1 - c)
         for c in range(2):
             store(wide[c], nc.vector.tensor_copy)
-        weigh(13)
+            affinity_sums(5, c, 4 + c)
         quantise_h(1, 2 * GROUP, h_bf[3])
-        damp[5] = kept([P, PACK, GROUP], F32, "damp5", tag="h_bf3")
+        damp[5] = placed([P, PACK, GROUP], F32, "damp5", 22)
         weigh(14)
         for c in range(2):
             affinity(4, c)
-            affinity_sums(5, c, 1 - c)
         for c in range(2):
             brands(middle[c], both[1], closes=True)
         for nt in range(2, 4):
@@ -402,7 +411,7 @@ def tile_list_fatigue_brand_affinity_kernel(
         quantise_h(0, 3 * GROUP, h_bf[4][:, :HALF])
         weigh(15, 1)
         quantise_h(0, 3 * GROUP + P, h_bf[4][:, HALF:])
-        for part, where in zip(last, (4, 5, 6)):
+        for part, where in zip(last, (1, 0, 6)):
             open_part(part, where)
             brands(part, both[0], opens=True)
         for c in range(2):

@@ -52,10 +52,10 @@ def tile_list_fatigue_brand_affinity_kernel(
         def placed(shape, dtype, name, kib):
             return reuse.tile(shape, dtype, name=name, align_bytes=64, offset=kib * 1024)
 
-        prod_words = {AFF: placed([P, T], U32, "prod_affinity", 8)[:], FAT: kept([P, T], U32, "prod_fatigue")[:]}
-        shop_words = [kept([P, T2], U32, f"shop_words{a}")[:] for a in range(2)]
-        prod_scales = kept([P, T], U8, "prod_scales")
-        shop_scales = kept([P, T2], U8, "shop_scales")
+        prod_words = {FAT: kept([P, T], U32, "prod_fatigue")[:]}
+        prod_scales = placed([P, T], U8, "prod_scales", 36)
+        shop_scales = placed([P, T2], U8, "shop_scales", 8)
+        shop_words = {FAT: kept([P, T2], U32, "shop_fatigue")[:]}
         margins = kept([P, 2, 2 * PACK], F32, "margins")
 
         def load_words(tile, words):
@@ -93,14 +93,13 @@ def tile_list_fatigue_brand_affinity_kernel(
         weights = {}
 
         def load_base_words():
-            weights["words"] = kept([P, 2, 2 * N], U8, "base_words")
+            weights["words"] = placed([P, 2, 2 * N], U8, "base_words", 40)
             nc.sync.dma_start(
                 out=weights["words"][:].bitcast(I32), in_=w4_words.rearrange("b p x -> p b x").bitcast(I32)
             )
 
         def load_base_scales():
-            weights["scales"] = kept([P, 2, N], U8, "base_scales")
-            nc.gpsimd.memset(weights["scales"][:].rearrange("p b n -> p (b n)").bitcast(I32), 0)
+            weights["scales"] = kept([P, 2, N], U8, "base_scales", tag="listed_scales")
             for q in range(4):
                 nc.sync.dma_start(
                     out=weights["scales"][32 * q : 32 * q + 4, :, :].bitcast(I32),
@@ -266,38 +265,30 @@ def tile_list_fatigue_brand_affinity_kernel(
         def f_bank_of(k):
             return k % 2 if k < 9 else 2 + (k - 9) % 2
 
-        wc_first = kept([P, PACK, SHARE], F32, "wc_first")
-        wc_second = kept([P, PACK, SHARE], F32, "wc_second")
-        wc_upper = placed([P, PACK, 2 * N - 2 * SHARE], F32, "wc_upper", 0)
-
         nc.sync.dma_start(idx2[:], offs2)
         load_words(shop_words[FAT], tab2_words[FAT])
         nc.sync.dma_start(idx[:], offs)
         load_prod_scales()
         load_shop_scales()
         load_words(prod_words[FAT], tab_words[FAT])
-        load_words(shop_words[AFF], tab2_words[AFF])
         load_margins()
-        load_words(prod_words[AFF], tab_words[AFF])
-        load_wc(wc_first[:], 0, 0, SHARE)
-        load_base_words()
         pick_shop_words(FAT, 0, S2)
         gather(listed_scales[:], prod_scales[:], idx[:])
+        shop_words[AFF] = placed([P, T2], U32, "shop_affinity", 36)[:]
+        load_words(shop_words[AFF], tab2_words[AFF])
         order_prod_scales(0)
         order_prod_scales(1)
-        pick_shop_scales(0, S2)
         load_base_scales()
-        load_wc(wc_second[:, :, : N - SHARE], 0, SHARE, N)
-        load_wc(wc_second[:, :, N - SHARE :], 1, 0, 2 * SHARE - N)
-        load_wc(wc_upper[:], 1, 2 * SHARE - N, N)
-
+        pick_shop_scales(0, S2)
+        prod_words[AFF] = placed([P, T], U32, "prod_affinity", 8)[:]
+        load_words(prod_words[AFF], tab_words[AFF])
         pick_prod_words(FAT, 0)
         pick_prod_words(FAT, 1)
         for k in (0, 2):
             square(k)
             square(k + 1)
             root(k)
-            root(k + 1)
+            root(k + 1, placed([P, HALF], F32, "roots1", 0) if k == 0 else None)
         square(4)
         for k in range(4, 7):
             square(k + 1)
@@ -305,9 +296,17 @@ def tile_list_fatigue_brand_affinity_kernel(
                 square_root(k - 1)
             root(k)
         pick_shop_words(AFF, 0, S2)
-        damp[0] = kept([P, PACK, HALF], F32, "damp0", tag=f"shop_words{AFF}")
+        wc_first = placed([P, PACK, SHARE], F32, "wc_first", 42)
+        load_wc(wc_first[:], 0, 0, SHARE)
+        load_base_words()
+        damp[0] = placed([P, PACK, HALF], F32, "damp0", 32)
         for k in range(4):
             weigh(k)
+        wc_second = kept([P, PACK, SHARE], F32, "wc_second", tag="roots0")
+        wc_upper = placed([P, PACK, 2 * N - 2 * SHARE], F32, "wc_upper", 0)
+        load_wc(wc_second[:, :, : N - SHARE], 0, SHARE, N)
+        load_wc(wc_second[:, :, N - SHARE :], 1, 0, 2 * SHARE - N)
+        load_wc(wc_upper[:], 1, 2 * SHARE - N, N)
         pick_prod_words(AFF, 0)
         pick_prod_words(AFF, 1)
         rounded = placed([P, (GROUP + 2 * N) * PACK], BF16, "rounded", 8)
@@ -347,7 +346,7 @@ def tile_list_fatigue_brand_affinity_kernel(
         root(15)
         square_root(14)
         square_root(15)
-        damp[1] = kept([P, PACK, HALF], F32, "damp1", tag=f"shop_words{AFF}")
+        damp[1] = placed([P, PACK, HALF], F32, "damp1", 32)
         weigh(4)
         quantise_h(0, 0, h_bf[0])
         for nt in range(2):

@@ -26,8 +26,8 @@ AFF, FAT = 0, 1
 BASE, CAMPAIGN = 0, 1
 BLOCKS = ((0, 512, 0), (0, 512, 1), (512, 256, 0), (512, 256, 1), (768, 256, 0), (768, 256, 1))
 SLABS = tuple((n, t, HALF // BLOCKS[n][1]) for n in range(6) for t in range(0, PACK, HALF // BLOCKS[n][1]))
-SCALAR_SQUARES = (6, 10, 12, 13, 14, 15)
-GPSIMD_MARGINS = (10, 12, 13, 14)
+SCALAR_SQUARES = (6, 10, 12, 14, 15)
+GPSIMD_MARGINS = (10, 12, 14)
 
 
 def tile_list_fatigue_brand_affinity_kernel(
@@ -249,9 +249,9 @@ def tile_list_fatigue_brand_affinity_kernel(
                     stop=closes and m == len(steps) - 1,
                 )
 
-        def store(part, copy, queue=nc.sync):
+        def store(part, copy, queue=nc.sync, tag=""):
             j0, width, lo, hi = part
-            staged = kept([P, hi - lo, width], F32, f"staged{j0}_{lo}")
+            staged = kept([P, hi - lo, width], F32, f"staged{j0}_{lo}", tag=tag)
             copy(out=staged[:], in_=acc[part][:])
             queue.dma_start(
                 out=out[lo * P : hi * P, j0 : j0 + width].rearrange("(nt p) j -> p nt j", p=P), in_=staged[:]
@@ -331,7 +331,7 @@ def tile_list_fatigue_brand_affinity_kernel(
         root(9, placed([P, HALF], F32, "roots9", 18))
         square(11, kept([P, HALF], F32, "squared11"))
         root(10)
-        square(12, kept([P, HALF], F32, "squared12"))
+        square(12, placed([P, HALF], F32, "squared12", 24))
         square_root(10)
         square(13, kept([P, HALF], F32, "squared13"))
         round_wc_scalar(wc_bf[:, 2 * SHARE * PACK :], wc_upper[:])
@@ -339,9 +339,8 @@ def tile_list_fatigue_brand_affinity_kernel(
         root(12, placed([P, HALF], F32, "roots12", 0))
         square(14, placed([P, HALF], F32, "squared14", 2))
         square_root(12)
-        root(13, kept([P, HALF], F32, "roots13", tag="squared12"))
+        root(13, placed([P, HALF], F32, "roots13", 24))
         square(15, kept([P, HALF], F32, "squared15", tag="squared11"))
-        square_root(13)
         root(14)
         root(15)
         square_root(14)
@@ -390,36 +389,34 @@ def tile_list_fatigue_brand_affinity_kernel(
             brands(middle[c], both[0], opens=True)
         damp[4] = placed([P, PACK, GROUP], F32, "damp4", 4)
         weigh(12)
-        weigh(13)
         for c in range(2):
             affinity(3, c)
             affinity_sums(4, c, 1 - c)
-        for c in range(2):
-            store(wide[c], nc.vector.tensor_copy)
-            affinity_sums(5, c, 4 + c)
+        weigh(13)
         quantise_h(1, 2 * GROUP, h_bf[3])
         damp[5] = placed([P, PACK, GROUP], F32, "damp5", 22)
         weigh(14)
         for c in range(2):
             affinity(4, c)
+            affinity_sums(5, c, 1 - c)
         for c in range(2):
             brands(middle[c], both[1], closes=True)
-        for nt in range(2, 4):
+        for nt in range(4):
             store(wide[nt], nc.scalar.copy)
         weigh(15, 0)
         quantise_h(0, 3 * GROUP, h_bf[4][:, :HALF])
         weigh(15, 1)
         quantise_h(0, 3 * GROUP + P, h_bf[4][:, HALF:])
-        for part, where in zip(last, (1, 0, 6)):
+        for part, where in zip(last, (4, 5, 6)):
             open_part(part, where)
             brands(part, both[0], opens=True)
         for c in range(2):
             affinity(5, c)
-        for c in range(2):
-            store(middle[c], nc.scalar.copy)
+        store(middle[0], nc.scalar.copy)
         quantise_h(1, 3 * GROUP, h_bf[5][:, :HALF])
         brands(last[0], both[1], closes=True)
         quantise_h(1, 3 * GROUP + P, h_bf[5][:, HALF:])
+        store(middle[1], nc.vector.tensor_copy, tag="h_bf5")
         store(last[0], nc.vector.tensor_copy)
         brands(last[1], both[1], closes=True)
         brands(last[2], both[1], closes=True)

@@ -263,7 +263,7 @@ def tile_list_fatigue_brand_affinity_kernel(
         both = [[(BASE, b), (CAMPAIGN, b)] for b in range(2)]
 
         def f_bank_of(k):
-            return k % 2 if k < 9 else 2 + (k - 9) % 2
+            return k % 2 if k < 8 else 6 if k == 8 else 2 + (k - 9) % 2
 
         nc.sync.dma_start(idx2[:], offs2)
         load_words(shop_words[FAT], tab2_words[FAT])
@@ -317,7 +317,7 @@ def tile_list_fatigue_brand_affinity_kernel(
         root(7, wc_bf[:, SHARE * PACK : SHARE * PACK + 2 * HALF].bitcast(F32))
         for c in range(4):
             affinity_sums(0, c, 2 + c)
-        for c, where in ((2, 1), (3, 0), (0, 6), (1, 7)):
+        for c, where in ((2, 0), (3, 7), (0, 1), (1, 6)):
             affinity_sums(1, c, where)
         round_wc_gpsimd(wc_bf[:, : SHARE * PACK], wc_first[:])
         h_bf[1], h_bf[2] = rounded[:, : HALF * PACK], rounded[:, HALF * PACK : (HALF + GROUP) * PACK]
@@ -334,17 +334,16 @@ def tile_list_fatigue_brand_affinity_kernel(
         square(12, placed([P, HALF], F32, "squared12", 24))
         square_root(10)
         square(13, kept([P, HALF], F32, "squared13"))
+        square(14, kept([P, HALF], F32, "squared14"))
         round_wc_scalar(wc_bf[:, 2 * SHARE * PACK :], wc_upper[:])
         root(11, placed([P, HALF], F32, "roots11", 4))
         root(12, placed([P, HALF], F32, "roots12", 0))
-        square(14, placed([P, HALF], F32, "squared14", 2))
+        square(15, placed([P, HALF], F32, "squared15", 2))
         square_root(12)
+        root(14, kept([P, HALF], F32, "roots14", tag="squared11"))
         root(13, placed([P, HALF], F32, "roots13", 24))
-        square(15, kept([P, HALF], F32, "squared15", tag="squared11"))
-        root(14)
-        root(15)
         square_root(14)
-        square_root(15)
+        root(15)
         damp[1] = placed([P, PACK, HALF], F32, "damp1", 32)
         weigh(4)
         quantise_h(0, 0, h_bf[0])
@@ -360,8 +359,8 @@ def tile_list_fatigue_brand_affinity_kernel(
         for c in (2, 3, 0, 1):
             affinity(1, c)
         for c in range(2):
-            affinity_sums(2, c, 1 - c)
-        for nt in range(2, 4):
+            affinity_sums(2, c, c)
+        for nt in (3, 2):
             open_part(wide[nt], 4 + nt)
             brands(wide[nt], [(BASE, 0)], opens=True)
         damp[2] = kept([P, PACK, GROUP], F32, "damp2", tag="h_bf0")
@@ -378,7 +377,7 @@ def tile_list_fatigue_brand_affinity_kernel(
         weigh(10)
         for c in range(2):
             affinity(2, c)
-            affinity_sums(3, c, 1 - c)
+            affinity_sums(3, c, c)
         quantise_wc(1, 0, wc_bf[:, N * PACK :])
         for nt in range(4):
             brands(wide[nt], [(CAMPAIGN, 1)], closes=True)
@@ -391,17 +390,19 @@ def tile_list_fatigue_brand_affinity_kernel(
         weigh(12)
         for c in range(2):
             affinity(3, c)
-            affinity_sums(4, c, 1 - c)
+            affinity_sums(4, c, c)
         weigh(13)
         quantise_h(1, 2 * GROUP, h_bf[3])
         damp[5] = placed([P, PACK, GROUP], F32, "damp5", 22)
         weigh(14)
         for c in range(2):
             affinity(4, c)
-            affinity_sums(5, c, 1 - c)
+            affinity_sums(5, c, c)
         for c in range(2):
             brands(middle[c], both[1], closes=True)
-        for nt in range(4):
+        store(wide[0], nc.scalar.copy)
+        square_root(15)
+        for nt in range(1, 4):
             store(wide[nt], nc.scalar.copy)
         weigh(15, 0)
         quantise_h(0, 3 * GROUP, h_bf[4][:, :HALF])
@@ -412,11 +413,11 @@ def tile_list_fatigue_brand_affinity_kernel(
             brands(part, both[0], opens=True)
         for c in range(2):
             affinity(5, c)
-        store(middle[0], nc.scalar.copy)
+        for c in range(2):
+            store(middle[c], nc.scalar.copy)
         quantise_h(1, 3 * GROUP, h_bf[5][:, :HALF])
         brands(last[0], both[1], closes=True)
         quantise_h(1, 3 * GROUP + P, h_bf[5][:, HALF:])
-        store(middle[1], nc.vector.tensor_copy, tag="h_bf5")
         store(last[0], nc.vector.tensor_copy)
         brands(last[1], both[1], closes=True)
         brands(last[2], both[1], closes=True)

@@ -53,9 +53,9 @@ def tile_list_fatigue_brand_affinity_kernel(
             return reuse.tile(shape, dtype, name=name, align_bytes=64, offset=kib * 1024)
 
         prod_words = {FAT: kept([P, T], U32, "prod_fatigue")[:]}
-        prod_scales = placed([P, T], U8, "prod_scales", 36)
+        prod_scales = kept([P, T], U8, "prod_scales")
         shop_scales = placed([P, T2], U8, "shop_scales", 8)
-        shop_words = {FAT: kept([P, T2], U32, "shop_fatigue")[:]}
+        shop_words = {FAT: placed([P, T2], U32, "shop_fatigue", 36)[:]}
         margins = kept([P, 2, 2 * PACK], F32, "margins")
 
         def load_words(tile, words):
@@ -66,8 +66,11 @@ def tile_list_fatigue_brand_affinity_kernel(
                 out=tile, in_=wc[b * HALF : (b + 1) * HALF, n0:n1].rearrange("(p t) n -> p t n", t=PACK)
             )
 
-        nc.vector.memset(prod_scales[:].bitcast(I32), 0)
+        v_scales = [kept([P, S], U8, f"v_scales{a}") for a in range(2)]
         nc.vector.memset(shop_scales[:].bitcast(I32), 0)
+        nc.vector.memset(prod_scales[32:64, :].bitcast(I32), 0)
+        nc.vector.memset(prod_scales[64:P, :].bitcast(I32), 0)
+        nc.vector.memset(v_scales[1][:].bitcast(I32), 0)
 
         warm = kept([P, 2], F32, "warm")
         nc.vector.memset(warm[:, 0:1], 1.0)
@@ -81,10 +84,17 @@ def tile_list_fatigue_brand_affinity_kernel(
                 )
 
         def load_prod_scales():
-            for r in range(4):
-                for a in range(2):
-                    nc.sync.dma_start(
-                        out=prod_scales[4 * a + r : P : 32, :].bitcast(I32), in_=tab_scales[a, r:16:4, :].bitcast(I32)
+            nc.sync.dma_start(
+                out=prod_scales[0:32, :].bitcast(I32), in_=tab_scales.rearrange("a q t -> (a q) t").bitcast(I32)
+            )
+
+        def move_prod_scales():
+            for a in (FAT, AFF):
+                for q in range(1 - a, 4):
+                    row = 16 * a + 4 * q
+                    nc.scalar.dma_start(
+                        out=v_scales[a][32 * q : 32 * q + 4, :].bitcast(I32),
+                        in_=v_scales[0][row : row + 4, :].bitcast(I32),
                     )
 
         def load_margins():
@@ -93,13 +103,13 @@ def tile_list_fatigue_brand_affinity_kernel(
         weights = {}
 
         def load_base_words():
-            weights["words"] = placed([P, 2, 2 * N], U8, "base_words", 40)
-            nc.sync.dma_start(
+            weights["words"] = kept([P, 2, 2 * N], U8, "base_words", tag="listed_scales")
+            nc.scalar.dma_start(
                 out=weights["words"][:].bitcast(I32), in_=w4_words.rearrange("b p x -> p b x").bitcast(I32)
             )
 
         def load_base_scales():
-            weights["scales"] = kept([P, 2, N], U8, "base_scales", tag="listed_scales")
+            weights["scales"] = placed([P, 2, N], U8, "base_scales", 42)
             for q in range(4):
                 nc.sync.dma_start(
                     out=weights["scales"][32 * q : 32 * q + 4, :, :].bitcast(I32),
@@ -111,7 +121,6 @@ def tile_list_fatigue_brand_affinity_kernel(
 
         v2_scales = kept([P, S2], U8, "v2_scales")
         listed_scales = kept([P, S], U8, "listed_scales")
-        v_scales = kept([P, S], U8, "v_scales")
         v_words = [kept([P, 2, HALF], U32, f"v_words{a}") for a in range(2)]
         v2_words = [kept([P, S2], U32, f"v2_words{a}") for a in range(2)]
 
@@ -131,7 +140,7 @@ def tile_list_fatigue_brand_affinity_kernel(
         def order_prod_scales(b):
             half = slice(b * HALF, (b + 1) * HALF)
             nc.vector.tensor_copy(
-                out=v_scales[:, half].rearrange("p (t c i) -> p c t i", t=PACK, i=16),
+                out=v_scales[0][:, half].rearrange("p (t c i) -> p c t i", t=PACK, i=16),
                 in_=listed_scales[:, half].rearrange("p (c i t) -> p c t i", t=PACK, i=16),
             )
 
@@ -139,7 +148,7 @@ def tile_list_fatigue_brand_affinity_kernel(
             nc.tensor.matmul_mx(
                 out=dst,
                 lhsT=v_words[a][:, b, t * P : (t + 1) * P].bitcast(FP8X4),
-                lhsT_scale=v_scales[4 * a :, b * HALF + t * P : b * HALF + (t + 1) * P],
+                lhsT_scale=v_scales[a][:, b * HALF + t * P : b * HALF + (t + 1) * P],
                 rhs=v2_words[a][:, j0 : j0 + width].bitcast(FP8X4),
                 rhs_scale=v2_scales[8 + 4 * a :, j0 : j0 + width],
                 start=True,
@@ -265,20 +274,21 @@ def tile_list_fatigue_brand_affinity_kernel(
         def f_bank_of(k):
             return k % 2 if k < 8 else 6 if k == 8 else 2 + (k - 9) % 2
 
-        nc.sync.dma_start(idx2[:], offs2)
-        load_words(shop_words[FAT], tab2_words[FAT])
         nc.sync.dma_start(idx[:], offs)
         load_prod_scales()
+        nc.sync.dma_start(idx2[:], offs2)
+        load_words(shop_words[FAT], tab2_words[FAT])
         load_shop_scales()
-        load_words(prod_words[FAT], tab_words[FAT])
         load_margins()
-        pick_shop_words(FAT, 0, S2)
+        load_words(prod_words[FAT], tab_words[FAT])
         gather(listed_scales[:], prod_scales[:], idx[:])
-        shop_words[AFF] = placed([P, T2], U32, "shop_affinity", 36)[:]
-        load_words(shop_words[AFF], tab2_words[AFF])
         order_prod_scales(0)
         order_prod_scales(1)
-        load_base_scales()
+        move_prod_scales()
+        load_base_words()
+        pick_shop_words(FAT, 0, S2)
+        shop_words[AFF] = placed([P, T2], U32, "shop_affinity", 36)[:]
+        load_words(shop_words[AFF], tab2_words[AFF])
         pick_shop_scales(0, S2)
         prod_words[AFF] = placed([P, T], U32, "prod_affinity", 8)[:]
         load_words(prod_words[AFF], tab_words[AFF])
@@ -296,9 +306,9 @@ def tile_list_fatigue_brand_affinity_kernel(
                 square_root(k - 1)
             root(k)
         pick_shop_words(AFF, 0, S2)
-        wc_first = placed([P, PACK, SHARE], F32, "wc_first", 42)
+        wc_first = placed([P, PACK, SHARE], F32, "wc_first", 43)
         load_wc(wc_first[:], 0, 0, SHARE)
-        load_base_words()
+        load_base_scales()
         damp[0] = placed([P, PACK, HALF], F32, "damp0", 32)
         for k in range(4):
             weigh(k)

@@ -272,7 +272,7 @@ def tile_list_fatigue_brand_affinity_kernel(
         both = [[(BASE, b), (CAMPAIGN, b)] for b in range(2)]
 
         def f_bank_of(k):
-            return k % 2 if k < 8 else 6 if k == 8 else 2 + (k - 9) % 2
+            return k % 2 if k < 9 else 2 + (k - 9) % 2
 
         nc.sync.dma_start(idx[:], offs)
         load_prod_scales()
@@ -327,7 +327,7 @@ def tile_list_fatigue_brand_affinity_kernel(
         root(7, wc_bf[:, SHARE * PACK : SHARE * PACK + 2 * HALF].bitcast(F32))
         for c in range(4):
             affinity_sums(0, c, 2 + c)
-        for c, where in ((2, 0), (3, 7), (0, 1), (1, 6)):
+        for c, where in ((2, 1), (3, 0), (0, 6), (1, 7)):
             affinity_sums(1, c, where)
         round_wc_gpsimd(wc_bf[:, : SHARE * PACK], wc_first[:])
         h_bf[1], h_bf[2] = rounded[:, : HALF * PACK], rounded[:, HALF * PACK : (HALF + GROUP) * PACK]
@@ -344,16 +344,17 @@ def tile_list_fatigue_brand_affinity_kernel(
         square(12, placed([P, HALF], F32, "squared12", 24))
         square_root(10)
         square(13, kept([P, HALF], F32, "squared13"))
-        square(14, kept([P, HALF], F32, "squared14"))
         round_wc_scalar(wc_bf[:, 2 * SHARE * PACK :], wc_upper[:])
         root(11, placed([P, HALF], F32, "roots11", 4))
         root(12, placed([P, HALF], F32, "roots12", 0))
-        square(15, placed([P, HALF], F32, "squared15", 2))
+        square(14, placed([P, HALF], F32, "squared14", 2))
         square_root(12)
-        root(14, kept([P, HALF], F32, "roots14", tag="squared11"))
         root(13, placed([P, HALF], F32, "roots13", 24))
-        square_root(14)
+        square(15, kept([P, HALF], F32, "squared15", tag="squared11"))
+        root(14)
         root(15)
+        square_root(14)
+        square_root(15)
         damp[1] = placed([P, PACK, HALF], F32, "damp1", 32)
         weigh(4)
         quantise_h(0, 0, h_bf[0])
@@ -369,8 +370,8 @@ def tile_list_fatigue_brand_affinity_kernel(
         for c in (2, 3, 0, 1):
             affinity(1, c)
         for c in range(2):
-            affinity_sums(2, c, c)
-        for nt in (3, 2):
+            affinity_sums(2, c, 1 - c)
+        for nt in range(2, 4):
             open_part(wide[nt], 4 + nt)
             brands(wide[nt], [(BASE, 0)], opens=True)
         damp[2] = kept([P, PACK, GROUP], F32, "damp2", tag="h_bf0")
@@ -387,7 +388,7 @@ def tile_list_fatigue_brand_affinity_kernel(
         weigh(10)
         for c in range(2):
             affinity(2, c)
-            affinity_sums(3, c, c)
+            affinity_sums(3, c, 1 - c)
         quantise_wc(1, 0, wc_bf[:, N * PACK :])
         for nt in range(4):
             brands(wide[nt], [(CAMPAIGN, 1)], closes=True)
@@ -400,19 +401,17 @@ def tile_list_fatigue_brand_affinity_kernel(
         weigh(12)
         for c in range(2):
             affinity(3, c)
-            affinity_sums(4, c, c)
+            affinity_sums(4, c, 1 - c)
         weigh(13)
         quantise_h(1, 2 * GROUP, h_bf[3])
         damp[5] = placed([P, PACK, GROUP], F32, "damp5", 22)
         weigh(14)
         for c in range(2):
             affinity(4, c)
-            affinity_sums(5, c, c)
+            affinity_sums(5, c, 1 - c)
         for c in range(2):
             brands(middle[c], both[1], closes=True)
-        store(wide[0], nc.scalar.copy)
-        square_root(15)
-        for nt in range(1, 4):
+        for nt in range(4):
             store(wide[nt], nc.scalar.copy)
         weigh(15, 0)
         quantise_h(0, 3 * GROUP, h_bf[4][:, :HALF])
@@ -423,11 +422,11 @@ def tile_list_fatigue_brand_affinity_kernel(
             brands(part, both[0], opens=True)
         for c in range(2):
             affinity(5, c)
-        for c in range(2):
-            store(middle[c], nc.scalar.copy)
+        store(middle[0], nc.scalar.copy)
         quantise_h(1, 3 * GROUP, h_bf[5][:, :HALF])
         brands(last[0], both[1], closes=True)
         quantise_h(1, 3 * GROUP + P, h_bf[5][:, HALF:])
+        store(middle[1], nc.vector.tensor_copy, tag="h_bf5")
         store(last[0], nc.vector.tensor_copy)
         brands(last[1], both[1], closes=True)
         brands(last[2], both[1], closes=True)

@@ -21,12 +21,12 @@ P = 128
 PACK = 4
 HALF = 512
 GROUP = 256
-SHARE = 320
+SHARE = 192
 AFF, FAT = 0, 1
 BASE, CAMPAIGN = 0, 1
 BLOCKS = ((0, 512, 0), (0, 512, 1), (512, 256, 0), (512, 256, 1), (768, 256, 0), (768, 256, 1))
 SLABS = tuple((n, t, HALF // BLOCKS[n][1]) for n in range(6) for t in range(0, PACK, HALF // BLOCKS[n][1]))
-SCALAR_SQUARES = (6, 10, 12, 14, 15)
+SCALAR_SQUARES = (5, 6, 7, 10, 12, 14, 15)
 GPSIMD_MARGINS = (10, 12, 14)
 
 
@@ -217,12 +217,6 @@ def tile_list_fatigue_brand_affinity_kernel(
             cols = slice(n0, n0 + rounded.shape[1] // PACK)
             nc.vector.quantize_mx(out=wc_words[b][:, cols].bitcast(FP8X4), scales=wc_scales[b][:, cols], in_=rounded)
 
-        def round_wc_scalar(rounded, raw):
-            nc.scalar.copy(
-                out=rounded.rearrange("p (k i t) -> p k t i", i=4, t=PACK),
-                in_=raw.rearrange("p t (k i) -> p k t i", i=4),
-            )
-
         def round_wc_gpsimd(rounded, raw):
             nc.gpsimd.tensor_scalar(
                 out=rounded.rearrange("p (n t) -> p n t", t=PACK),
@@ -298,7 +292,7 @@ def tile_list_fatigue_brand_affinity_kernel(
             square(k)
             square(k + 1)
             root(k)
-            root(k + 1, placed([P, HALF], F32, "roots1", 0) if k == 0 else None)
+            root(k + 1, placed([P, HALF], F32, f"roots{k + 1}", 2 if k == 0 else 48))
         square(4)
         for k in range(4, 7):
             square(k + 1)
@@ -306,36 +300,40 @@ def tile_list_fatigue_brand_affinity_kernel(
                 square_root(k - 1)
             root(k)
         pick_shop_words(AFF, 0, S2)
-        wc_first = placed([P, PACK, SHARE], F32, "wc_first", 43)
-        load_wc(wc_first[:], 0, 0, SHARE)
+        wc_first = placed([P, PACK, GROUP], F32, "wc_first", 43)
+        load_wc(wc_first[:], 0, 0, GROUP)
         load_base_scales()
         damp[0] = placed([P, PACK, HALF], F32, "damp0", 32)
         for k in range(4):
             weigh(k)
-        wc_second = kept([P, PACK, SHARE], F32, "wc_second", tag="roots0")
-        wc_upper = placed([P, PACK, 2 * N - 2 * SHARE], F32, "wc_upper", 0)
-        load_wc(wc_second[:, :, : N - SHARE], 0, SHARE, N)
-        load_wc(wc_second[:, :, N - SHARE :], 1, 0, 2 * SHARE - N)
-        load_wc(wc_upper[:], 1, 2 * SHARE - N, N)
+        wc_second = kept([P, PACK, GROUP], F32, "wc_second", tag="roots0")
+        wc_third = placed([P, PACK, SHARE], F32, "wc_third", 0)
+        wc_fourth = placed([P, PACK, N - SHARE], F32, "wc_fourth", 3)
+        load_wc(wc_second[:], 0, GROUP, N)
+        load_wc(wc_third[:], 1, 0, SHARE)
+        load_wc(wc_fourth[:], 1, SHARE, N)
         pick_prod_words(AFF, 0)
         pick_prod_words(AFF, 1)
-        rounded = placed([P, (GROUP + 2 * N) * PACK], BF16, "rounded", 8)
+        rounded = placed([P, (GROUP + 2 * N) * PACK], BF16, "rounded", 48)
         wc_bf = rounded[:, GROUP * PACK :]
+        round_wc_gpsimd(wc_bf[:, : GROUP * PACK], wc_first[:])
+        round_wc_gpsimd(wc_bf[:, GROUP * PACK : N * PACK], wc_second[:])
+        round_wc_gpsimd(wc_bf[:, N * PACK : (N + SHARE) * PACK], wc_third[:])
         square(8)
         if 6 in SCALAR_SQUARES:
             square_root(6)
-        root(7, wc_bf[:, SHARE * PACK : SHARE * PACK + 2 * HALF].bitcast(F32))
+        root(7, wc_bf[:, (N + SHARE) * PACK : (N + SHARE) * PACK + 2 * HALF].bitcast(F32))
         for c in range(4):
             affinity_sums(0, c, 2 + c)
         for c, where in ((2, 1), (3, 0), (0, 6), (1, 7)):
             affinity_sums(1, c, where)
-        round_wc_gpsimd(wc_bf[:, : SHARE * PACK], wc_first[:])
         h_bf[1], h_bf[2] = rounded[:, : HALF * PACK], rounded[:, HALF * PACK : (HALF + GROUP) * PACK]
         for n in (0, 4, 5):
             h_bf[n] = kept([P, BLOCKS[n][1] * PACK], BF16, f"h_bf{n}")[:]
         for c in range(4):
             affinity(0, c)
         square(9)
+        square_root(7)
         root(8)
         square(10)
         root(9, placed([P, HALF], F32, "roots9", 18))
@@ -344,7 +342,6 @@ def tile_list_fatigue_brand_affinity_kernel(
         square(12, placed([P, HALF], F32, "squared12", 24))
         square_root(10)
         square(13, kept([P, HALF], F32, "squared13"))
-        round_wc_scalar(wc_bf[:, 2 * SHARE * PACK :], wc_upper[:])
         root(11, placed([P, HALF], F32, "roots11", 4))
         root(12, placed([P, HALF], F32, "roots12", 0))
         square(14, placed([P, HALF], F32, "squared14", 2))
@@ -366,7 +363,7 @@ def tile_list_fatigue_brand_affinity_kernel(
         quantise_wc(0, 0, wc_bf[:, : GROUP * PACK])
         for nt in range(2):
             brands(wide[nt], [(CAMPAIGN, 0)])
-        round_wc_gpsimd(wc_bf[:, SHARE * PACK : 2 * SHARE * PACK], wc_second[:])
+        round_wc_gpsimd(wc_bf[:, (N + SHARE) * PACK :], wc_fourth[:])
         for c in (2, 3, 0, 1):
             affinity(1, c)
         for c in range(2):

@@ -21,13 +21,16 @@ P = 128
 PACK = 4
 HALF = 512
 GROUP = 256
+EARLY = 128
 SHARE = 192
 AFF, FAT = 0, 1
 BASE, CAMPAIGN = 0, 1
 BLOCKS = ((0, 512, 0), (0, 512, 1), (512, 256, 0), (512, 256, 1), (768, 256, 0), (768, 256, 1))
-SLABS = tuple((n, t, HALF // BLOCKS[n][1]) for n in range(6) for t in range(0, PACK, HALF // BLOCKS[n][1]))
-SCALAR_SQUARES = (5, 6, 7, 10, 12, 14, 15)
-GPSIMD_MARGINS = (10, 12, 14)
+SLABS = tuple((n, t, 1) for n in range(2) for t in range(PACK)) + ((2, 2, 2), (2, 0, 2)) + tuple(
+    (n, t, 2) for n in range(3, 6) for t in (0, 2)
+)
+SCALAR_SQUARES = (6, 7, 8, 10, 12, 14, 15)
+GPSIMD_MARGINS = (8, 10, 12, 14)
 
 
 def tile_list_fatigue_brand_affinity_kernel(
@@ -38,7 +41,7 @@ def tile_list_fatigue_brand_affinity_kernel(
         lists = ctx.enter_context(tc.tile_pool(name="lists", bufs=1))
         keep = ctx.enter_context(tc.tile_pool(name="keep", bufs=1))
         reuse = ctx.enter_context(tc.tile_pool(name="reuse", bufs=1))
-        ring = ctx.enter_context(tc.tile_pool(name="ring", bufs=3))
+        ring = ctx.enter_context(tc.tile_pool(name="ring", bufs=4))
         psum = ctx.enter_context(tc.psum_pool(name="psum", bufs=1))
 
         def kept(shape, dtype, name, tag=""):
@@ -50,12 +53,12 @@ def tile_list_fatigue_brand_affinity_kernel(
         idx = lists.tile([P, S // 16], U16, name="idx")
         idx2 = lists.tile([P, S2 // 16], U16, name="idx2")
         def placed(shape, dtype, name, kib):
-            return reuse.tile(shape, dtype, name=name, align_bytes=64, offset=kib * 1024)
+            return reuse.tile(shape, dtype, name=name, align_bytes=64, offset=int(kib * 1024))
 
-        prod_words = {FAT: kept([P, T], U32, "prod_fatigue")[:]}
-        prod_scales = kept([P, T], U8, "prod_scales")
-        shop_scales = placed([P, T2], U8, "shop_scales", 8)
-        shop_words = {FAT: placed([P, T2], U32, "shop_fatigue", 36)[:]}
+        prod_words = {FAT: placed([P, T], U32, "prod_fatigue", 72)[:]}
+        prod_scales = placed([P, T], U8, "prod_scales", 62)
+        shop_scales = placed([P, T2], U8, "shop_scales", 7)
+        shop_words = {FAT: placed([P, T2], U32, "shop_fatigue", 41.5)[:]}
         margins = kept([P, 2, 2 * PACK], F32, "margins")
 
         def load_words(tile, words):
@@ -66,11 +69,11 @@ def tile_list_fatigue_brand_affinity_kernel(
                 out=tile, in_=wc[b * HALF : (b + 1) * HALF, n0:n1].rearrange("(p t) n -> p t n", t=PACK)
             )
 
-        v_scales = [kept([P, S], U8, f"v_scales{a}") for a in range(2)]
+        ordered_scales = kept([P, S], U8, "ordered_scales")
+        v_scales = {}
         nc.vector.memset(shop_scales[:].bitcast(I32), 0)
         nc.vector.memset(prod_scales[32:64, :].bitcast(I32), 0)
         nc.vector.memset(prod_scales[64:P, :].bitcast(I32), 0)
-        nc.vector.memset(v_scales[1][:].bitcast(I32), 0)
 
         warm = kept([P, 2], F32, "warm")
         nc.vector.memset(warm[:, 0:1], 1.0)
@@ -88,14 +91,13 @@ def tile_list_fatigue_brand_affinity_kernel(
                 out=prod_scales[0:32, :].bitcast(I32), in_=tab_scales.rearrange("a q t -> (a q) t").bitcast(I32)
             )
 
-        def move_prod_scales():
-            for a in (FAT, AFF):
-                for q in range(1 - a, 4):
-                    row = 16 * a + 4 * q
-                    nc.scalar.dma_start(
-                        out=v_scales[a][32 * q : 32 * q + 4, :].bitcast(I32),
-                        in_=v_scales[0][row : row + 4, :].bitcast(I32),
-                    )
+        def move_prod_scales(a):
+            for q in range(4):
+                row = 16 * a + 4 * q
+                nc.sync.dma_start(
+                    out=v_scales[a][32 * q : 32 * q + 4, :].bitcast(I32),
+                    in_=ordered_scales[row : row + 4, :].bitcast(I32),
+                )
 
         def load_margins():
             nc.sync.dma_start(out=margins[:, :, 0:PACK], in_=margin.rearrange("(b p t) -> p b t", b=2, t=PACK))
@@ -103,13 +105,13 @@ def tile_list_fatigue_brand_affinity_kernel(
         weights = {}
 
         def load_base_words():
-            weights["words"] = kept([P, 2, 2 * N], U8, "base_words", tag="listed_scales")
-            nc.scalar.dma_start(
+            weights["words"] = placed([P, 2, 2 * N], U8, "base_words", 54)
+            nc.sync.dma_start(
                 out=weights["words"][:].bitcast(I32), in_=w4_words.rearrange("b p x -> p b x").bitcast(I32)
             )
 
         def load_base_scales():
-            weights["scales"] = placed([P, 2, N], U8, "base_scales", 42)
+            weights["scales"] = placed([P, 2, N], U8, "base_scales", 10)
             for q in range(4):
                 nc.sync.dma_start(
                     out=weights["scales"][32 * q : 32 * q + 4, :, :].bitcast(I32),
@@ -119,10 +121,10 @@ def tile_list_fatigue_brand_affinity_kernel(
         def gather(picked, window, offsets):
             nc.vector.tensor_copy(out=picked, in_=window.indirect(offsets))
 
-        v2_scales = kept([P, S2], U8, "v2_scales")
-        listed_scales = kept([P, S], U8, "listed_scales")
+        v2_scales = placed([P, S2], U8, "v2_scales", 49)
+        listed_scales = [placed([P, HALF], U8, f"listed_scales{b}", 66 + 4 * b) for b in range(2)]
         v_words = [kept([P, 2, HALF], U32, f"v_words{a}") for a in range(2)]
-        v2_words = [kept([P, S2], U32, f"v2_words{a}") for a in range(2)]
+        v2_words = {}
 
         def pick_shop_words(a, j0, j1):
             gather(v2_words[a][:, j0:j1], shop_words[a], idx2[:, j0 // 16 : j1 // 16])
@@ -140,8 +142,8 @@ def tile_list_fatigue_brand_affinity_kernel(
         def order_prod_scales(b):
             half = slice(b * HALF, (b + 1) * HALF)
             nc.vector.tensor_copy(
-                out=v_scales[0][:, half].rearrange("p (t c i) -> p c t i", t=PACK, i=16),
-                in_=listed_scales[:, half].rearrange("p (c i t) -> p c t i", t=PACK, i=16),
+                out=ordered_scales[:, half].rearrange("p (t c i) -> p c t i", t=PACK, i=16),
+                in_=listed_scales[b][:].rearrange("p (c i t) -> p c t i", t=PACK, i=16),
             )
 
         def table_product(dst, a, b, t, j0, width):
@@ -155,31 +157,38 @@ def tile_list_fatigue_brand_affinity_kernel(
                 stop=True,
             )
 
-        roots, damp, squared, sums, h_bf = {}, {}, {}, {}, {}
+        fatigue, roots, damp, squared, sums, h_bf = {}, {}, {}, {}, {}, {}
 
-        def square(k, onto=None):
+        def fatigue_sums(k):
             n, t0, slots = SLABS[k]
             j0, width, b = BLOCKS[n]
-            f_bank = bank(f_bank_of(k), [P, HALF], f"f{k}")
+            fatigue[k] = bank(k % 2 if k < 8 else 6 if k == 8 else 3 - k % 2, [P, HALF], f"f{k}")
             for s in range(slots):
-                table_product(f_bank[:, s * width : (s + 1) * width], FAT, b, t0 + s, j0, width)
+                table_product(fatigue[k][:, s * width : (s + 1) * width], FAT, b, t0 + s, j0, width)
+
+        def square(k, onto=None):
             squared[k] = onto if onto is not None else ring.tile([P, HALF], F32, name="squared")
-            nc.scalar.activation(out=squared[k][:], in_=f_bank[:], func=ACT.Square)
+            nc.scalar.activation(out=squared[k][:], in_=fatigue[k][:], func=ACT.Square)
+            if k + 2 < len(SLABS) and k + 2 not in (8, 9, 10):
+                fatigue_sums(k + 2)
 
         def root(k, onto=None):
             roots[k] = onto if onto is not None else kept([P, HALF], F32, f"roots{k}")
             nc.scalar.activation(out=roots[k][:], in_=squared[k][:], func=ACT.Abs_reciprocal_sqrt, bias=1.0)
 
-        def square_root(k):
-            nc.scalar.activation(out=roots[k][:], in_=roots[k][:], func=ACT.Square)
+        def square_root(k, onto=None):
+            plain = roots[k]
+            if onto is not None:
+                roots[k] = onto
+            nc.scalar.activation(out=roots[k][:], in_=plain[:], func=ACT.Square)
 
-        def weigh(k, only=None):
+        def weigh(k, only=None, on_vector=False):
             n, t0, slots = SLABS[k]
             j0, width, b = BLOCKS[n]
             for s in range(slots) if only is None else (only,):
                 t = t0 + s
                 root_t, margin_t = roots[k][:, s * width : (s + 1) * width], margins[:, b, t : t + 1]
-                if k in GPSIMD_MARGINS:
+                if k in GPSIMD_MARGINS and not on_vector:
                     nc.gpsimd.tensor_scalar(
                         out=damp[n][:, t, :], in0=root_t, scalar1=margin_t, scalar2=0.0, op0=MULT, op1=ADD
                     )
@@ -206,7 +215,7 @@ def tile_list_fatigue_brand_affinity_kernel(
 
         h_words = [kept([P, S2], U32, f"h_words{b}") for b in range(2)]
         h_scales = [kept([P, S2], U8, f"h_scales{b}") for b in range(2)]
-        wc_words = [kept([P, N], U32, f"wc_words{b}") for b in range(2)]
+        wc_words = {1: kept([P, N], U32, "wc_words1")}
         wc_scales = [kept([P, N], U8, f"wc_scales{b}") for b in range(2)]
 
         def quantise_h(b, j0, rounded):
@@ -216,6 +225,12 @@ def tile_list_fatigue_brand_affinity_kernel(
         def quantise_wc(b, n0, rounded):
             cols = slice(n0, n0 + rounded.shape[1] // PACK)
             nc.vector.quantize_mx(out=wc_words[b][:, cols].bitcast(FP8X4), scales=wc_scales[b][:, cols], in_=rounded)
+
+        def round_wc_scalar(rounded, raw):
+            nc.scalar.copy(
+                out=rounded.rearrange("p (k i t) -> p k t i", i=4, t=PACK),
+                in_=raw.rearrange("p t (k i) -> p k t i", i=4),
+            )
 
         def round_wc_gpsimd(rounded, raw):
             nc.gpsimd.tensor_scalar(
@@ -230,9 +245,10 @@ def tile_list_fatigue_brand_affinity_kernel(
             j0, width, lo, hi = part
             acc[part] = bank(where, [P, hi - lo, width], f"acc{j0}_{lo}")
 
-        def brands(part, terms, opens=False, closes=False):
+        def brands(part, terms, opens=False, closes=False, within=None):
             j0, width, lo, hi = part
-            cols = slice(j0, j0 + width)
+            first, count = within or (0, width)
+            cols = slice(j0 + first, j0 + first + count)
             steps = [(nt, kind, b) for nt in range(lo, hi) for kind, b in terms]
             for m, (nt, kind, b) in enumerate(steps):
                 tile = slice(nt * P, (nt + 1) * P)
@@ -243,7 +259,7 @@ def tile_list_fatigue_brand_affinity_kernel(
                     codes = wc_words[b][:, tile].bitcast(FP8X4)
                     scales = wc_scales[b][:, tile]
                 nc.tensor.matmul_mx(
-                    out=acc[part][:, nt - lo, :],
+                    out=acc[part][:, nt - lo, first : first + count],
                     lhsT=codes,
                     lhsT_scale=scales,
                     rhs=h_words[b][:, cols].bitcast(FP8X4),
@@ -265,9 +281,6 @@ def tile_list_fatigue_brand_affinity_kernel(
         last = [(768, P, 0, 4), (896, P, 0, 3), (896, P, 3, 4)]
         both = [[(BASE, b), (CAMPAIGN, b)] for b in range(2)]
 
-        def f_bank_of(k):
-            return k % 2 if k < 9 else 2 + (k - 9) % 2
-
         nc.sync.dma_start(idx[:], offs)
         load_prod_scales()
         nc.sync.dma_start(idx2[:], offs2)
@@ -275,139 +288,168 @@ def tile_list_fatigue_brand_affinity_kernel(
         load_shop_scales()
         load_margins()
         load_words(prod_words[FAT], tab_words[FAT])
-        gather(listed_scales[:], prod_scales[:], idx[:])
+        for b in range(2):
+            gather(listed_scales[b][:], prod_scales[:], idx[:, b * HALF // 16 : (b + 1) * HALF // 16])
         order_prod_scales(0)
         order_prod_scales(1)
-        move_prod_scales()
-        load_base_words()
+        v_scales[FAT] = placed([P, S], U8, "v_scales_fatigue", 62)
+        move_prod_scales(FAT)
+        v2_words[FAT] = placed([P, S2], U32, "v2_words_fatigue", 66)
         pick_shop_words(FAT, 0, S2)
+        wc_early = placed([P, PACK, EARLY], F32, "wc_early", 45)
+        load_wc(wc_early[:], 0, 0, EARLY)
         shop_words[AFF] = placed([P, T2], U32, "shop_affinity", 36)[:]
         load_words(shop_words[AFF], tab2_words[AFF])
+        v_scales[AFF] = placed([P, S], U8, "v_scales_affinity", 48)
+        move_prod_scales(AFF)
         pick_shop_scales(0, S2)
         prod_words[AFF] = placed([P, T], U32, "prod_affinity", 8)[:]
         load_words(prod_words[AFF], tab_words[AFF])
         pick_prod_words(FAT, 0)
         pick_prod_words(FAT, 1)
+        wc_bf_early = kept([P, EARLY * PACK], BF16, "wc_bf_early")
+        round_wc_scalar(wc_bf_early[:], wc_early[:])
+        fatigue_sums(0)
+        fatigue_sums(1)
+        fatigue_sums(8)
         for k in (0, 2):
-            square(k)
-            square(k + 1)
-            root(k)
-            root(k + 1, placed([P, HALF], F32, f"roots{k + 1}", 2 if k == 0 else 48))
-        square(4)
-        for k in range(4, 7):
-            square(k + 1)
-            if k - 1 in SCALAR_SQUARES:
-                square_root(k - 1)
-            root(k)
+            square(k, placed([P, HALF], F32, "squared0", 44) if k == 0 else None)
+            square(k + 1, placed([P, HALF], F32, "squared1", 46) if k == 0 else None)
+            root(k, placed([P, HALF], F32, "roots2", 0) if k == 2 else None)
+            root(k + 1, placed([P, HALF], F32, f"roots{k + 1}", 53 if k == 0 else 25))
+        v2_words[AFF] = placed([P, S2], U32, "v2_words_affinity", 72)
         pick_shop_words(AFF, 0, S2)
-        wc_first = placed([P, PACK, GROUP], F32, "wc_first", 43)
-        load_wc(wc_first[:], 0, 0, GROUP)
-        load_base_scales()
-        damp[0] = placed([P, PACK, HALF], F32, "damp0", 32)
+        wc_words[0] = placed([P, N], U32, "wc_words0", 76)
+        quantise_wc(0, 0, wc_bf_early[:])
+        wc_first = placed([P, PACK, SHARE], F32, "wc_first", 43)
+        load_wc(wc_first[:], 0, EARLY, EARLY + SHARE)
+        damp[0] = placed([P, PACK, HALF], F32, "damp0", 33)
         for k in range(4):
             weigh(k)
-        wc_second = kept([P, PACK, GROUP], F32, "wc_second", tag="roots0")
-        wc_third = placed([P, PACK, SHARE], F32, "wc_third", 0)
-        wc_fourth = placed([P, PACK, N - SHARE], F32, "wc_fourth", 3)
-        load_wc(wc_second[:], 0, GROUP, N)
-        load_wc(wc_third[:], 1, 0, SHARE)
-        load_wc(wc_fourth[:], 1, SHARE, N)
+        wc_second = kept([P, PACK, SHARE], F32, "wc_second", tag="roots0")
+        wc_third = placed([P, PACK, GROUP], F32, "wc_third", 50)
+        wc_fourth = placed([P, PACK, GROUP], F32, "wc_fourth", 0)
+        load_wc(wc_second[:], 0, EARLY + SHARE, N)
+        load_wc(wc_third[:], 1, 0, GROUP)
+        load_base_words()
+        load_wc(wc_fourth[:], 1, GROUP, N)
+        square(4)
+        square(5)
+        root(4)
         pick_prod_words(AFF, 0)
         pick_prod_words(AFF, 1)
-        rounded = placed([P, (GROUP + 2 * N) * PACK], BF16, "rounded", 48)
-        wc_bf = rounded[:, GROUP * PACK :]
-        round_wc_gpsimd(wc_bf[:, : GROUP * PACK], wc_first[:])
-        round_wc_gpsimd(wc_bf[:, GROUP * PACK : N * PACK], wc_second[:])
-        round_wc_gpsimd(wc_bf[:, N * PACK : (N + SHARE) * PACK], wc_third[:])
-        square(8)
-        if 6 in SCALAR_SQUARES:
-            square_root(6)
-        root(7, wc_bf[:, (N + SHARE) * PACK : (N + SHARE) * PACK + 2 * HALF].bitcast(F32))
         for c in range(4):
             affinity_sums(0, c, 2 + c)
-        for c, where in ((2, 1), (3, 0), (0, 6), (1, 7)):
+        square(6)
+        load_base_scales()
+        wc_low = placed([P, (2 * SHARE + GROUP) * PACK], BF16, "wc_low", 26.5)
+        round_wc_gpsimd(wc_low[:, : SHARE * PACK], wc_first[:])
+        round_wc_gpsimd(wc_low[:, SHARE * PACK : 2 * SHARE * PACK], wc_second[:])
+        round_wc_gpsimd(wc_low[:, 2 * SHARE * PACK :], wc_third[:])
+        root(5)
+        square(7)
+        root(6)
+        square(8)
+        for c, where in enumerate((7, 0, 1)):
             affinity_sums(1, c, where)
-        h_bf[1], h_bf[2] = rounded[:, : HALF * PACK], rounded[:, HALF * PACK : (HALF + GROUP) * PACK]
-        for n in (0, 4, 5):
+        for n in (0, 2, 4, 5):
             h_bf[n] = kept([P, BLOCKS[n][1] * PACK], BF16, f"h_bf{n}")[:]
+        square_root(6)
+        root(7)
         for c in range(4):
             affinity(0, c)
+            if c < 2:
+                fatigue_sums(9 + c)
         square(9)
-        square_root(7)
+        quantise_h(0, 0, h_bf[0][:, : GROUP * PACK])
+        quantise_wc(0, EARLY, wc_low[:, : 2 * SHARE * PACK])
+        quantise_wc(1, 0, wc_low[:, 2 * SHARE * PACK :])
+        quantise_h(0, GROUP, h_bf[0][:, GROUP * PACK : (GROUP + P) * PACK])
+        for nt in range(3):
+            open_part(wide[nt], 4 + nt)
+            brands(wide[nt], [(CAMPAIGN, 0), (BASE, 0)], opens=True, within=(0, GROUP))
+        shared = placed([P, 6 * HALF], F32, "shared", 31)
+        damp[1] = shared[:, : PACK * HALF].rearrange("p (t j) -> p t j", t=PACK)
+        damp[2] = shared[:, 3 * HALF : 5 * HALF].rearrange("p (t j) -> p t j", t=PACK)
+        wc_high = shared[:, 5 * HALF :].bitcast(BF16)
         root(8)
-        square(10)
-        root(9, placed([P, HALF], F32, "roots9", 18))
-        square(11, kept([P, HALF], F32, "squared11"))
+        square_root(7, shared[:, 5 * HALF - GROUP : 5 * HALF + GROUP])
+        square(10, placed([P, HALF], F32, "squared10", 25))
+        for k in range(4, 8):
+            weigh(k)
+        quantise_h(0, GROUP + P, h_bf[0][:, (GROUP + P) * PACK :])
+        for nt in range(3):
+            brands(wide[nt], [(CAMPAIGN, 0), (BASE, 0)], within=(GROUP, GROUP))
+        square_root(8)
+        root(9, placed([P, HALF], F32, "roots9", 29))
+        square(11, placed([P, HALF], F32, "squared11", 27))
+        round_wc_gpsimd(wc_high, wc_fourth[:])
+        weigh(8, 1)
+        h_bf[1] = kept([P, HALF * PACK], BF16, "h_bf1")[:]
+        affinity(1, 0)
+        affinity_sums(1, 3, 7)
+        affinity(1, 1)
         root(10)
-        square(12, placed([P, HALF], F32, "squared12", 24))
+        square(12)
+        affinity_sums(2, 0, 0)
+        affinity(1, 2)
+        affinity_sums(2, 1, 1)
+        affinity(1, 3)
         square_root(10)
-        square(13, kept([P, HALF], F32, "squared13"))
         root(11, placed([P, HALF], F32, "roots11", 4))
-        root(12, placed([P, HALF], F32, "roots12", 0))
-        square(14, placed([P, HALF], F32, "squared14", 2))
+        square(13)
+        quantise_h(1, 0, h_bf[1][:, : GROUP * PACK])
+        open_part(wide[3], 7)
+        brands(wide[3], [(CAMPAIGN, 0), (BASE, 0)], opens=True)
+        for nt in range(2):
+            brands(wide[nt], both[1], within=(0, GROUP))
+        weigh(8, 0, on_vector=True)
+        weigh(9, 0)
+        quantise_h(1, GROUP, h_bf[1][:, GROUP * PACK :])
+        weigh(9, 1)
+        quantise_wc(1, GROUP, wc_high)
+        root(12)
+        square(14)
+        for nt in range(2):
+            brands(wide[nt], both[1], within=(GROUP, GROUP), closes=True)
+        damp[3] = placed([P, PACK, GROUP], F32, "damp3", 27)
+        h_bf[3] = placed([P, GROUP * PACK], BF16, "h_bf3", 22)[:]
+        weigh(10)
+        affinity(2, 0)
+        brands(wide[2], both[1], closes=True)
+        affinity_sums(3, 0, 0)
+        affinity(2, 1)
         square_root(12)
+        square(15)
+        affinity_sums(3, 1, 1)
+        brands(wide[3], both[1], closes=True)
+        weigh(11)
+        quantise_h(0, 2 * GROUP, h_bf[2])
+        damp[4] = placed([P, PACK, GROUP], F32, "damp4", 3)
+        weigh(12)
         root(13, placed([P, HALF], F32, "roots13", 24))
-        square(15, kept([P, HALF], F32, "squared15", tag="squared11"))
         root(14)
         root(15)
         square_root(14)
         square_root(15)
-        damp[1] = placed([P, PACK, HALF], F32, "damp1", 32)
-        weigh(4)
-        quantise_h(0, 0, h_bf[0])
-        for nt in range(2):
-            open_part(wide[nt], 4 + nt)
-            brands(wide[nt], [(BASE, 0)], opens=True)
-        for k in range(5, 8):
-            weigh(k)
-        quantise_wc(0, 0, wc_bf[:, : GROUP * PACK])
-        for nt in range(2):
-            brands(wide[nt], [(CAMPAIGN, 0)])
-        round_wc_gpsimd(wc_bf[:, (N + SHARE) * PACK :], wc_fourth[:])
-        for c in (2, 3, 0, 1):
-            affinity(1, c)
-        for c in range(2):
-            affinity_sums(2, c, 1 - c)
-        for nt in range(2, 4):
-            open_part(wide[nt], 4 + nt)
-            brands(wide[nt], [(BASE, 0)], opens=True)
-        damp[2] = kept([P, PACK, GROUP], F32, "damp2", tag="h_bf0")
-        weigh(8)
-        quantise_h(1, 0, h_bf[1])
-        weigh(9)
-        for nt in range(4):
-            brands(wide[nt], [(BASE, 1)])
-        quantise_wc(0, GROUP, wc_bf[:, GROUP * PACK : N * PACK])
-        for nt in range(2, 4):
-            brands(wide[nt], [(CAMPAIGN, 0)])
-        damp[3] = placed([P, PACK, GROUP], F32, "damp3", 18)
-        h_bf[3] = placed([P, GROUP * PACK], BF16, "h_bf3", 22)[:]
-        weigh(10)
-        for c in range(2):
-            affinity(2, c)
-            affinity_sums(3, c, 1 - c)
-        quantise_wc(1, 0, wc_bf[:, N * PACK :])
-        for nt in range(4):
-            brands(wide[nt], [(CAMPAIGN, 1)], closes=True)
-        weigh(11)
-        quantise_h(0, 2 * GROUP, h_bf[2])
-        for c in range(2):
-            open_part(middle[c], 2 + c)
-            brands(middle[c], both[0], opens=True)
-        damp[4] = placed([P, PACK, GROUP], F32, "damp4", 4)
-        weigh(12)
-        for c in range(2):
-            affinity(3, c)
-            affinity_sums(4, c, 1 - c)
+        affinity(3, 0)
+        open_part(middle[0], 3)
+        brands(middle[0], both[0], opens=True)
+        affinity_sums(4, 0, 0)
+        affinity(3, 1)
+        affinity_sums(4, 1, 1)
+        open_part(middle[1], 2)
+        brands(middle[1], both[0], opens=True)
         weigh(13)
         quantise_h(1, 2 * GROUP, h_bf[3])
         damp[5] = placed([P, PACK, GROUP], F32, "damp5", 22)
         weigh(14)
-        for c in range(2):
-            affinity(4, c)
-            affinity_sums(5, c, 1 - c)
-        for c in range(2):
-            brands(middle[c], both[1], closes=True)
+        affinity(4, 0)
+        brands(middle[0], both[1], closes=True)
+        affinity_sums(5, 0, 0)
+        affinity(4, 1)
+        affinity_sums(5, 1, 1)
+        brands(middle[1], both[1], closes=True)
         for nt in range(4):
             store(wide[nt], nc.scalar.copy)
         weigh(15, 0)

@@ -21,16 +21,14 @@ P = 128
 PACK = 4
 HALF = 512
 GROUP = 256
-EARLY = 128
-SHARE = 192
+SHARE = 320
+FIRST = 128
 AFF, FAT = 0, 1
 BASE, CAMPAIGN = 0, 1
 BLOCKS = ((0, 512, 0), (0, 512, 1), (512, 256, 0), (512, 256, 1), (768, 256, 0), (768, 256, 1))
-SLABS = tuple((n, t, 1) for n in range(2) for t in range(PACK)) + ((2, 2, 2), (2, 0, 2)) + tuple(
-    (n, t, 2) for n in range(3, 6) for t in (0, 2)
-)
-SCALAR_SQUARES = (6, 7, 8, 10, 12, 14, 15)
-GPSIMD_MARGINS = (8, 10, 12, 14)
+SLABS = tuple((n, t, HALF // BLOCKS[n][1]) for n in range(6) for t in range(0, PACK, HALF // BLOCKS[n][1]))
+SCALAR_SQUARES = (6, 7, 10, 12, 14, 15)
+GPSIMD_MARGINS = (10, 12, 14)
 
 
 def tile_list_fatigue_brand_affinity_kernel(
@@ -55,10 +53,10 @@ def tile_list_fatigue_brand_affinity_kernel(
         def placed(shape, dtype, name, kib):
             return reuse.tile(shape, dtype, name=name, align_bytes=64, offset=int(kib * 1024))
 
-        prod_words = {FAT: placed([P, T], U32, "prod_fatigue", 72)[:]}
-        prod_scales = placed([P, T], U8, "prod_scales", 62)
-        shop_scales = placed([P, T2], U8, "shop_scales", 7)
-        shop_words = {FAT: placed([P, T2], U32, "shop_fatigue", 41.5)[:]}
+        prod_words = {FAT: kept([P, T], U32, "prod_fatigue")[:]}
+        prod_scales = kept([P, T], U8, "prod_scales")
+        shop_scales = placed([P, T2], U8, "shop_scales", 8)
+        shop_words = {FAT: placed([P, T2], U32, "shop_fatigue", 36)[:]}
         margins = kept([P, 2, 2 * PACK], F32, "margins")
 
         def load_words(tile, words):
@@ -69,11 +67,11 @@ def tile_list_fatigue_brand_affinity_kernel(
                 out=tile, in_=wc[b * HALF : (b + 1) * HALF, n0:n1].rearrange("(p t) n -> p t n", t=PACK)
             )
 
-        ordered_scales = kept([P, S], U8, "ordered_scales")
-        v_scales = {}
+        v_scales = [kept([P, S], U8, f"v_scales{a}") for a in range(2)]
         nc.vector.memset(shop_scales[:].bitcast(I32), 0)
         nc.vector.memset(prod_scales[32:64, :].bitcast(I32), 0)
         nc.vector.memset(prod_scales[64:P, :].bitcast(I32), 0)
+        nc.vector.memset(v_scales[1][:].bitcast(I32), 0)
 
         warm = kept([P, 2], F32, "warm")
         nc.vector.memset(warm[:, 0:1], 1.0)
@@ -91,13 +89,14 @@ def tile_list_fatigue_brand_affinity_kernel(
                 out=prod_scales[0:32, :].bitcast(I32), in_=tab_scales.rearrange("a q t -> (a q) t").bitcast(I32)
             )
 
-        def move_prod_scales(a):
-            for q in range(4):
-                row = 16 * a + 4 * q
-                nc.sync.dma_start(
-                    out=v_scales[a][32 * q : 32 * q + 4, :].bitcast(I32),
-                    in_=ordered_scales[row : row + 4, :].bitcast(I32),
-                )
+        def move_prod_scales():
+            for a in (FAT, AFF):
+                for q in range(1 - a, 4):
+                    row = 16 * a + 4 * q
+                    nc.scalar.dma_start(
+                        out=v_scales[a][32 * q : 32 * q + 4, :].bitcast(I32),
+                        in_=v_scales[0][row : row + 4, :].bitcast(I32),
+                    )
 
         def load_margins():
             nc.sync.dma_start(out=margins[:, :, 0:PACK], in_=margin.rearrange("(b p t) -> p b t", b=2, t=PACK))
@@ -105,13 +104,13 @@ def tile_list_fatigue_brand_affinity_kernel(
         weights = {}
 
         def load_base_words():
-            weights["words"] = placed([P, 2, 2 * N], U8, "base_words", 54)
-            nc.sync.dma_start(
+            weights["words"] = kept([P, 2, 2 * N], U8, "base_words", tag="listed_scales")
+            nc.scalar.dma_start(
                 out=weights["words"][:].bitcast(I32), in_=w4_words.rearrange("b p x -> p b x").bitcast(I32)
             )
 
         def load_base_scales():
-            weights["scales"] = placed([P, 2, N], U8, "base_scales", 10)
+            weights["scales"] = placed([P, 2, N], U8, "base_scales", 42)
             for q in range(4):
                 nc.sync.dma_start(
                     out=weights["scales"][32 * q : 32 * q + 4, :, :].bitcast(I32),
@@ -121,10 +120,10 @@ def tile_list_fatigue_brand_affinity_kernel(
         def gather(picked, window, offsets):
             nc.vector.tensor_copy(out=picked, in_=window.indirect(offsets))
 
-        v2_scales = placed([P, S2], U8, "v2_scales", 49)
-        listed_scales = [placed([P, HALF], U8, f"listed_scales{b}", 66 + 4 * b) for b in range(2)]
+        v2_scales = kept([P, S2], U8, "v2_scales")
+        listed_scales = kept([P, S], U8, "listed_scales")
         v_words = [kept([P, 2, HALF], U32, f"v_words{a}") for a in range(2)]
-        v2_words = {}
+        v2_words = [kept([P, S2], U32, f"v2_words{a}") for a in range(2)]
 
         def pick_shop_words(a, j0, j1):
             gather(v2_words[a][:, j0:j1], shop_words[a], idx2[:, j0 // 16 : j1 // 16])
@@ -142,8 +141,8 @@ def tile_list_fatigue_brand_affinity_kernel(
         def order_prod_scales(b):
             half = slice(b * HALF, (b + 1) * HALF)
             nc.vector.tensor_copy(
-                out=ordered_scales[:, half].rearrange("p (t c i) -> p c t i", t=PACK, i=16),
-                in_=listed_scales[b][:].rearrange("p (c i t) -> p c t i", t=PACK, i=16),
+                out=v_scales[0][:, half].rearrange("p (t c i) -> p c t i", t=PACK, i=16),
+                in_=listed_scales[:, half].rearrange("p (c i t) -> p c t i", t=PACK, i=16),
             )
 
         def table_product(dst, a, b, t, j0, width):
@@ -182,13 +181,13 @@ def tile_list_fatigue_brand_affinity_kernel(
                 roots[k] = onto
             nc.scalar.activation(out=roots[k][:], in_=plain[:], func=ACT.Square)
 
-        def weigh(k, only=None, on_vector=False):
+        def weigh(k, only=None):
             n, t0, slots = SLABS[k]
             j0, width, b = BLOCKS[n]
             for s in range(slots) if only is None else (only,):
                 t = t0 + s
                 root_t, margin_t = roots[k][:, s * width : (s + 1) * width], margins[:, b, t : t + 1]
-                if k in GPSIMD_MARGINS and not on_vector:
+                if k in GPSIMD_MARGINS:
                     nc.gpsimd.tensor_scalar(
                         out=damp[n][:, t, :], in0=root_t, scalar1=margin_t, scalar2=0.0, op0=MULT, op1=ADD
                     )
@@ -215,7 +214,7 @@ def tile_list_fatigue_brand_affinity_kernel(
 
         h_words = [kept([P, S2], U32, f"h_words{b}") for b in range(2)]
         h_scales = [kept([P, S2], U8, f"h_scales{b}") for b in range(2)]
-        wc_words = {1: kept([P, N], U32, "wc_words1")}
+        wc_words = [kept([P, N], U32, f"wc_words{b}") for b in range(2)]
         wc_scales = [kept([P, N], U8, f"wc_scales{b}") for b in range(2)]
 
         def quantise_h(b, j0, rounded):
@@ -245,10 +244,9 @@ def tile_list_fatigue_brand_affinity_kernel(
             j0, width, lo, hi = part
             acc[part] = bank(where, [P, hi - lo, width], f"acc{j0}_{lo}")
 
-        def brands(part, terms, opens=False, closes=False, within=None):
+        def brands(part, terms, opens=False, closes=False):
             j0, width, lo, hi = part
-            first, count = within or (0, width)
-            cols = slice(j0 + first, j0 + first + count)
+            cols = slice(j0, j0 + width)
             steps = [(nt, kind, b) for nt in range(lo, hi) for kind, b in terms]
             for m, (nt, kind, b) in enumerate(steps):
                 tile = slice(nt * P, (nt + 1) * P)
@@ -259,7 +257,7 @@ def tile_list_fatigue_brand_affinity_kernel(
                     codes = wc_words[b][:, tile].bitcast(FP8X4)
                     scales = wc_scales[b][:, tile]
                 nc.tensor.matmul_mx(
-                    out=acc[part][:, nt - lo, first : first + count],
+                    out=acc[part][:, nt - lo, :],
                     lhsT=codes,
                     lhsT_scale=scales,
                     rhs=h_words[b][:, cols].bitcast(FP8X4),
@@ -288,71 +286,61 @@ def tile_list_fatigue_brand_affinity_kernel(
         load_shop_scales()
         load_margins()
         load_words(prod_words[FAT], tab_words[FAT])
-        for b in range(2):
-            gather(listed_scales[b][:], prod_scales[:], idx[:, b * HALF // 16 : (b + 1) * HALF // 16])
+        gather(listed_scales[:], prod_scales[:], idx[:])
         order_prod_scales(0)
         order_prod_scales(1)
-        v_scales[FAT] = placed([P, S], U8, "v_scales_fatigue", 62)
-        move_prod_scales(FAT)
-        v2_words[FAT] = placed([P, S2], U32, "v2_words_fatigue", 66)
+        move_prod_scales()
+        load_base_words()
         pick_shop_words(FAT, 0, S2)
-        wc_early = placed([P, PACK, EARLY], F32, "wc_early", 45)
-        load_wc(wc_early[:], 0, 0, EARLY)
         shop_words[AFF] = placed([P, T2], U32, "shop_affinity", 36)[:]
         load_words(shop_words[AFF], tab2_words[AFF])
-        v_scales[AFF] = placed([P, S], U8, "v_scales_affinity", 48)
-        move_prod_scales(AFF)
         pick_shop_scales(0, S2)
         prod_words[AFF] = placed([P, T], U32, "prod_affinity", 8)[:]
         load_words(prod_words[AFF], tab_words[AFF])
         pick_prod_words(FAT, 0)
         pick_prod_words(FAT, 1)
-        wc_bf_early = kept([P, EARLY * PACK], BF16, "wc_bf_early")
-        round_wc_scalar(wc_bf_early[:], wc_early[:])
-        fatigue_sums(0)
-        fatigue_sums(1)
-        fatigue_sums(8)
+        for k in (0, 1, 8):
+            fatigue_sums(k)
         for k in (0, 2):
-            square(k, placed([P, HALF], F32, "squared0", 44) if k == 0 else None)
-            square(k + 1, placed([P, HALF], F32, "squared1", 46) if k == 0 else None)
-            root(k, placed([P, HALF], F32, "roots2", 0) if k == 2 else None)
-            root(k + 1, placed([P, HALF], F32, f"roots{k + 1}", 53 if k == 0 else 25))
-        v2_words[AFF] = placed([P, S2], U32, "v2_words_affinity", 72)
+            square(k)
+            square(k + 1)
+            root(k, placed([P, HALF], F32, f"roots{k}", 47 if k == 0 else 0))
+            root(k + 1, placed([P, HALF], F32, f"roots{k + 1}", 68 if k == 0 else 54))
         pick_shop_words(AFF, 0, S2)
-        wc_words[0] = placed([P, N], U32, "wc_words0", 76)
-        quantise_wc(0, 0, wc_bf_early[:])
-        wc_first = placed([P, PACK, SHARE], F32, "wc_first", 43)
-        load_wc(wc_first[:], 0, EARLY, EARLY + SHARE)
+        wc_raw = [placed([P, PACK, FIRST], F32, "wc_first", 43)]
+        load_wc(wc_raw[0][:], 0, 0, FIRST)
+        load_base_scales()
         damp[0] = placed([P, PACK, HALF], F32, "damp0", 33)
         for k in range(4):
             weigh(k)
-        wc_second = kept([P, PACK, SHARE], F32, "wc_second", tag="roots0")
-        wc_third = placed([P, PACK, GROUP], F32, "wc_third", 50)
-        wc_fourth = placed([P, PACK, GROUP], F32, "wc_fourth", 0)
-        load_wc(wc_second[:], 0, EARLY + SHARE, N)
-        load_wc(wc_third[:], 1, 0, GROUP)
-        load_base_words()
-        load_wc(wc_fourth[:], 1, GROUP, N)
+        wc_raw.append(placed([P, PACK, FIRST], F32, "wc_second", 46))
+        wc_raw.append(placed([P, PACK, GROUP], F32, "wc_third", 48))
+        wc_raw.append(placed([P, PACK, SHARE], F32, "wc_fourth", 69))
+        wc_raw.append(placed([P, PACK, N - SHARE], F32, "wc_fifth", 0))
+        load_wc(wc_raw[1][:], 0, FIRST, GROUP)
+        load_wc(wc_raw[2][:], 0, GROUP, N)
+        load_wc(wc_raw[3][:], 1, 0, SHARE)
+        load_wc(wc_raw[4][:], 1, SHARE, N)
         square(4)
         square(5)
-        root(4)
+        root(4, placed([P, HALF], F32, "roots4", 62))
         pick_prod_words(AFF, 0)
         pick_prod_words(AFF, 1)
         for c in range(4):
             affinity_sums(0, c, 2 + c)
         square(6)
-        load_base_scales()
-        wc_low = placed([P, (2 * SHARE + GROUP) * PACK], BF16, "wc_low", 26.5)
-        round_wc_gpsimd(wc_low[:, : SHARE * PACK], wc_first[:])
-        round_wc_gpsimd(wc_low[:, SHARE * PACK : 2 * SHARE * PACK], wc_second[:])
-        round_wc_gpsimd(wc_low[:, 2 * SHARE * PACK :], wc_third[:])
-        root(5)
+        rounded = placed([P, 10 * HALF], BF16, "rounded", 52)
+        wc_bf = [rounded[:, 2 * HALF : 6 * HALF], rounded[:, 6 * HALF :]]
+        round_wc_gpsimd(wc_bf[0][:, : FIRST * PACK], wc_raw[0][:])
+        round_wc_gpsimd(wc_bf[0][:, FIRST * PACK : GROUP * PACK], wc_raw[1][:])
+        round_wc_gpsimd(wc_bf[0][:, GROUP * PACK :], wc_raw[2][:])
+        root(5, placed([P, HALF], F32, "roots5", 64))
         square(7)
-        root(6)
+        root(6, placed([P, HALF], F32, "roots6", 66))
         square(8)
         for c, where in enumerate((7, 0, 1)):
             affinity_sums(1, c, where)
-        for n in (0, 2, 4, 5):
+        for n in (0, 3, 4, 5):
             h_bf[n] = kept([P, BLOCKS[n][1] * PACK], BF16, f"h_bf{n}")[:]
         square_root(6)
         root(7)
@@ -361,101 +349,87 @@ def tile_list_fatigue_brand_affinity_kernel(
             if c < 2:
                 fatigue_sums(9 + c)
         square(9)
+        square_root(7, rounded[:, 7 * HALF : 9 * HALF].bitcast(F32))
+        root(8)
+        late = placed([P, 10 * HALF + P], F32, "late", 20.5)
+        damp[1] = late[:, 6 * HALF + P :].rearrange("p (t j) -> p t j", t=PACK)
+        for n in range(2, 6):
+            damp[n] = late[:, (10 - 2 * n) * HALF + P : (12 - 2 * n) * HALF + P].rearrange("p (t j) -> p t j", t=PACK)
         quantise_h(0, 0, h_bf[0][:, : GROUP * PACK])
-        quantise_wc(0, EARLY, wc_low[:, : 2 * SHARE * PACK])
-        quantise_wc(1, 0, wc_low[:, 2 * SHARE * PACK :])
-        quantise_h(0, GROUP, h_bf[0][:, GROUP * PACK : (GROUP + P) * PACK])
+        weigh(4)
+        quantise_h(0, GROUP, h_bf[0][:, GROUP * PACK :])
         for nt in range(3):
             open_part(wide[nt], 4 + nt)
-            brands(wide[nt], [(CAMPAIGN, 0), (BASE, 0)], opens=True, within=(0, GROUP))
-        shared = placed([P, 6 * HALF], F32, "shared", 31)
-        damp[1] = shared[:, : PACK * HALF].rearrange("p (t j) -> p t j", t=PACK)
-        damp[2] = shared[:, 3 * HALF : 5 * HALF].rearrange("p (t j) -> p t j", t=PACK)
-        wc_high = shared[:, 5 * HALF :].bitcast(BF16)
-        root(8)
-        square_root(7, shared[:, 5 * HALF - GROUP : 5 * HALF + GROUP])
-        square(10, placed([P, HALF], F32, "squared10", 25))
-        for k in range(4, 8):
+            brands(wide[nt], [(BASE, 0)], opens=True)
+        square(10, placed([P, HALF], F32, "squared10", 62))
+        root(9, late[:, 4 * HALF : 5 * HALF])
+        for k in range(5, 8):
             weigh(k)
-        quantise_h(0, GROUP + P, h_bf[0][:, (GROUP + P) * PACK :])
-        for nt in range(3):
-            brands(wide[nt], [(CAMPAIGN, 0), (BASE, 0)], within=(GROUP, GROUP))
-        square_root(8)
-        root(9, placed([P, HALF], F32, "roots9", 29))
-        square(11, placed([P, HALF], F32, "squared11", 27))
-        round_wc_gpsimd(wc_high, wc_fourth[:])
-        weigh(8, 1)
-        h_bf[1] = kept([P, HALF * PACK], BF16, "h_bf1")[:]
+        quantise_wc(0, 0, wc_bf[0][:, : GROUP * PACK])
+        for nt in range(2):
+            brands(wide[nt], [(CAMPAIGN, 0)])
+        square(11, placed([P, HALF], F32, "squared11", 64))
+        root(10)
+        round_wc_gpsimd(wc_bf[1][:, : SHARE * PACK], wc_raw[3][:])
+        h_bf[1] = rounded[:, : HALF * PACK]
         affinity(1, 0)
         affinity_sums(1, 3, 7)
         affinity(1, 1)
-        root(10)
-        square(12)
+        square(12, placed([P, HALF], F32, "squared12", 66))
+        round_wc_scalar(wc_bf[1][:, SHARE * PACK :], wc_raw[4][:])
+        square_root(10, placed([P, HALF], F32, "squared_roots10", 69))
         affinity_sums(2, 0, 0)
         affinity(1, 2)
         affinity_sums(2, 1, 1)
         affinity(1, 3)
-        square_root(10)
-        root(11, placed([P, HALF], F32, "roots11", 4))
-        square(13)
+        square(13, placed([P, HALF], F32, "squared13", 0))
+        root(11, late[:, 2 * HALF : 3 * HALF])
         quantise_h(1, 0, h_bf[1][:, : GROUP * PACK])
         open_part(wide[3], 7)
-        brands(wide[3], [(CAMPAIGN, 0), (BASE, 0)], opens=True)
-        for nt in range(2):
-            brands(wide[nt], both[1], within=(0, GROUP))
-        weigh(8, 0, on_vector=True)
-        weigh(9, 0)
+        brands(wide[3], [(BASE, 0)], opens=True)
+        weigh(8, 0)
         quantise_h(1, GROUP, h_bf[1][:, GROUP * PACK :])
-        weigh(9, 1)
-        quantise_wc(1, GROUP, wc_high)
-        root(12)
+        weigh(8, 1)
+        for nt in range(4):
+            brands(wide[nt], [(BASE, 1)])
+        weigh(9)
+        quantise_wc(0, GROUP, wc_bf[0][:, GROUP * PACK :])
+        for nt in range(2, 4):
+            brands(wide[nt], [(CAMPAIGN, 0)])
+        h_bf[2] = rounded[:, 3 * HALF : 5 * HALF]
+        root(12, placed([P, HALF], F32, "roots12", 2))
         square(14)
-        for nt in range(2):
-            brands(wide[nt], both[1], within=(GROUP, GROUP), closes=True)
-        damp[3] = placed([P, PACK, GROUP], F32, "damp3", 27)
-        h_bf[3] = placed([P, GROUP * PACK], BF16, "h_bf3", 22)[:]
-        weigh(10)
-        affinity(2, 0)
-        brands(wide[2], both[1], closes=True)
-        affinity_sums(3, 0, 0)
-        affinity(2, 1)
         square_root(12)
-        square(15)
-        affinity_sums(3, 1, 1)
-        brands(wide[3], both[1], closes=True)
-        weigh(11)
-        quantise_h(0, 2 * GROUP, h_bf[2])
-        damp[4] = placed([P, PACK, GROUP], F32, "damp4", 3)
-        weigh(12)
-        root(13, placed([P, HALF], F32, "roots13", 24))
+        root(13, late[:, :HALF])
         root(14)
-        root(15)
+        square(15)
         square_root(14)
+        root(15)
         square_root(15)
-        affinity(3, 0)
-        open_part(middle[0], 3)
-        brands(middle[0], both[0], opens=True)
-        affinity_sums(4, 0, 0)
-        affinity(3, 1)
-        affinity_sums(4, 1, 1)
-        open_part(middle[1], 2)
-        brands(middle[1], both[0], opens=True)
-        weigh(13)
-        quantise_h(1, 2 * GROUP, h_bf[3])
-        damp[5] = placed([P, PACK, GROUP], F32, "damp5", 22)
-        weigh(14)
-        affinity(4, 0)
-        brands(middle[0], both[1], closes=True)
-        affinity_sums(5, 0, 0)
-        affinity(4, 1)
-        affinity_sums(5, 1, 1)
-        brands(middle[1], both[1], closes=True)
+        for n in (2, 3, 4):
+            j0, width, half = BLOCKS[n]
+            weigh(2 * n + 6)
+            for c in range(2):
+                affinity(n, c)
+                affinity_sums(n + 1, c, c)
+            if n == 2:
+                quantise_wc(1, 0, wc_bf[1])
+                for nt in range(4):
+                    brands(wide[nt], [(CAMPAIGN, 1)], closes=True)
+            if n == 4:
+                weigh(15, 0)
+                quantise_h(half, j0, h_bf[n][:, :HALF])
+                weigh(15, 1)
+                quantise_h(half, j0 + P, h_bf[n][:, HALF:])
+            else:
+                weigh(2 * n + 7)
+                quantise_h(half, j0, h_bf[n])
+                for c in range(2):
+                    if n == 2:
+                        open_part(middle[c], 3 - c)
+                    brands(middle[c], both[half], opens=n == 2, closes=n == 3)
         for nt in range(4):
             store(wide[nt], nc.scalar.copy)
-        weigh(15, 0)
-        quantise_h(0, 3 * GROUP, h_bf[4][:, :HALF])
-        weigh(15, 1)
-        quantise_h(0, 3 * GROUP + P, h_bf[4][:, HALF:])
         for part, where in zip(last, (4, 5, 6)):
             open_part(part, where)
             brands(part, both[0], opens=True)

from contextlib import ExitStack

import concourse.mybir as mybir

K, T, T2, S, S2, N = 1024, 4096, 2048, 1024, 1024, 512
FLOPS = 2 * K * S * S2 + 2 * 2 * S * N * S2

F32 = mybir.dt.float32
BF16 = mybir.dt.bfloat16
I32 = mybir.dt.int32
U32 = mybir.dt.uint32
U16 = mybir.dt.uint16
U8 = mybir.dt.uint8
FP8X4 = mybir.dt.float8_e4m3fn_x4
FP4X4 = mybir.dt.float4_e2m1fn_x4
ACT = mybir.ActivationFunctionType
MULT = mybir.AluOpType.mult
ADD = mybir.AluOpType.add

P = 128
PACK = 4
HALF = 512
GROUP = 256
SHARE = 320
FIRST = 128
AFF, FAT = 0, 1
BASE, CAMPAIGN = 0, 1
BLOCKS = ((0, 512, 0), (0, 512, 1), (512, 256, 0), (512, 256, 1), (768, 256, 0), (768, 256, 1))
SLABS = tuple((n, t, HALF // BLOCKS[n][1]) for n in range(6) for t in range(0, PACK, HALF // BLOCKS[n][1]))
SCALAR_SQUARES = (6, 7, 10, 12, 14, 15)
GPSIMD_MARGINS = (10, 12, 14)


def tile_list_fatigue_brand_affinity_kernel(
    tc, tab_words, tab_scales, tab2_words, tab2_scales, offs, offs2, margin, wc, w4_words, w4_scales, out
):
    nc = tc.nc
    with ExitStack() as ctx:
        lists = ctx.enter_context(tc.tile_pool(name="lists", bufs=1))
        keep = ctx.enter_context(tc.tile_pool(name="keep", bufs=1))
        reuse = ctx.enter_context(tc.tile_pool(name="reuse", bufs=1))
        ring = ctx.enter_context(tc.tile_pool(name="ring", bufs=4))
        psum = ctx.enter_context(tc.psum_pool(name="psum", bufs=1))

        def kept(shape, dtype, name, tag=""):
            return keep.tile(shape, dtype, name=name, tag=tag or name, align_bytes=64)

        def bank(n, shape, name):
            return psum.tile(shape, F32, name=name, tag=f"bank{n}")

        idx = lists.tile([P, S // 16], U16, name="idx")
        idx2 = lists.tile([P, S2 // 16], U16, name="idx2")
        def placed(shape, dtype, name, kib):
            return reuse.tile(shape, dtype, name=name, align_bytes=64, offset=int(kib * 1024))

        prod_words = {FAT: kept([P, T], U32, "prod_fatigue")[:]}
        prod_scales = kept([P, T], U8, "prod_scales")
        shop_scales = placed([P, T2], U8, "shop_scales", 8)
        shop_words = {FAT: placed([P, T2], U32, "shop_fatigue", 36)[:]}
        margins = kept([P, 2, 2 * PACK], F32, "margins")

        def load_words(tile, words):
            nc.sync.dma_start(out=tile.bitcast(I32), in_=words.rearrange("p t i -> p (t i)").bitcast(I32))

        def load_wc(tile, b, n0, n1):
            nc.sync.dma_start(
                out=tile, in_=wc[b * HALF : (b + 1) * HALF, n0:n1].rearrange("(p t) n -> p t n", t=PACK)
            )

        v_scales = [kept([P, S], U8, f"v_scales{a}") for a in range(2)]
        nc.vector.memset(shop_scales[:].bitcast(I32), 0)
        nc.vector.memset(prod_scales[32:64, :].bitcast(I32), 0)
        nc.vector.memset(prod_scales[64:P, :].bitcast(I32), 0)
        nc.vector.memset(v_scales[1][:].bitcast(I32), 0)

        warm = kept([P, 2], F32, "warm")
        nc.vector.memset(warm[:, 0:1], 1.0)
        nc.scalar.activation(out=warm[:, 1:2], in_=warm[:, 0:1], func=ACT.Abs_reciprocal_sqrt)

        def load_shop_scales():
            for q in range(4):
                nc.sync.dma_start(
                    out=shop_scales[32 * q + 8 : 32 * q + 16, :].bitcast(I32),
                    in_=tab2_scales[:, 4 * q : 4 * q + 4, :].bitcast(I32),
                )

        def load_prod_scales():
            nc.sync.dma_start(
                out=prod_scales[0:32, :].bitcast(I32), in_=tab_scales.rearrange("a q t -> (a q) t").bitcast(I32)
            )

        def move_prod_scales():
            for a in (FAT, AFF):
                for q in range(1 - a, 4):
                    row = 16 * a + 4 * q
                    nc.scalar.dma_start(
                        out=v_scales[a][32 * q : 32 * q + 4, :].bitcast(I32),
                        in_=v_scales[0][row : row + 4, :].bitcast(I32),
                    )

        def load_margins():
            nc.sync.dma_start(out=margins[:, :, 0:PACK], in_=margin.rearrange("(b p t) -> p b t", b=2, t=PACK))

        weights = {}

        def load_base_words():
            weights["words"] = kept([P, 2, 2 * N], U8, "base_words", tag="listed_scales")
            nc.scalar.dma_start(
                out=weights["words"][:].bitcast(I32), in_=w4_words.rearrange("b p x -> p b x").bitcast(I32)
            )

        def load_base_scales():
            weights["scales"] = placed([P, 2, N], U8, "base_scales", 42)
            for q in range(4):
                nc.sync.dma_start(
                    out=weights["scales"][32 * q : 32 * q + 4, :, :].bitcast(I32),
                    in_=w4_scales[:, 4 * q : 4 * q + 4, :].rearrange("b r n -> r b n").bitcast(I32),
                )

        def gather(picked, window, offsets):
            nc.vector.tensor_copy(out=picked, in_=window.indirect(offsets))

        v2_scales = kept([P, S2], U8, "v2_scales")
        listed_scales = kept([P, S], U8, "listed_scales")
        v_words = [kept([P, 2, HALF], U32, f"v_words{a}") for a in range(2)]
        v2_words = [kept([P, S2], U32, f"v2_words{a}") for a in range(2)]

        def pick_shop_words(a, j0, j1):
            gather(v2_words[a][:, j0:j1], shop_words[a], idx2[:, j0 // 16 : j1 // 16])

        def pick_shop_scales(j0, j1):
            gather(v2_scales[:, j0:j1], shop_scales[:], idx2[:, j0 // 16 : j1 // 16])

        def pick_prod_words(a, b):
            gather(
                v_words[a][:, b : b + 1, :].rearrange("p b (t s) -> p b s t", t=PACK),
                prod_words[a],
                idx[:, b * HALF // 16 : (b + 1) * HALF // 16],
            )

        def order_prod_scales(b):
            half = slice(b * HALF, (b + 1) * HALF)
            nc.vector.tensor_copy(
                out=v_scales[0][:, half].rearrange("p (t c i) -> p c t i", t=PACK, i=16),
                in_=listed_scales[:, half].rearrange("p (c i t) -> p c t i", t=PACK, i=16),
            )

        def table_product(dst, a, b, t, j0, width):
            nc.tensor.matmul_mx(
                out=dst,
                lhsT=v_words[a][:, b, t * P : (t + 1) * P].bitcast(FP8X4),
                lhsT_scale=v_scales[a][:, b * HALF + t * P : b * HALF + (t + 1) * P],
                rhs=v2_words[a][:, j0 : j0 + width].bitcast(FP8X4),
                rhs_scale=v2_scales[8 + 4 * a :, j0 : j0 + width],
                start=True,
                stop=True,
            )

        fatigue, roots, damp, squared, sums, h_bf = {}, {}, {}, {}, {}, {}

        def fatigue_sums(k):
            n, t0, slots = SLABS[k]
            j0, width, b = BLOCKS[n]
            fatigue[k] = bank(k % 2 if k < 8 else 6 if k == 8 else 3 - k % 2, [P, HALF], f"f{k}")
            for s in range(slots):
                table_product(fatigue[k][:, s * width : (s + 1) * width], FAT, b, t0 + s, j0, width)

        def square(k, onto=None):
            squared[k] = onto if onto is not None else ring.tile([P, HALF], F32, name="squared")
            nc.scalar.activation(out=squared[k][:], in_=fatigue[k][:], func=ACT.Square)
            if k + 2 < len(SLABS) and k + 2 not in (8, 9, 10):
                fatigue_sums(k + 2)

        def root(k, onto=None):
            roots[k] = onto if onto is not None else kept([P, HALF], F32, f"roots{k}")
            nc.scalar.activation(out=roots[k][:], in_=squared[k][:], func=ACT.Abs_reciprocal_sqrt, bias=1.0)

        def square_root(k, onto=None):
            plain = roots[k]
            if onto is not None:
                roots[k] = onto
            nc.scalar.activation(out=roots[k][:], in_=plain[:], func=ACT.Square)

        def weigh(k, only=None):
            n, t0, slots = SLABS[k]
            j0, width, b = BLOCKS[n]
            for s in range(slots) if only is None else (only,):
                t = t0 + s
                root_t, margin_t = roots[k][:, s * width : (s + 1) * width], margins[:, b, t : t + 1]
                if k in GPSIMD_MARGINS:
                    nc.gpsimd.tensor_scalar(
                        out=damp[n][:, t, :], in0=root_t, scalar1=margin_t, scalar2=0.0, op0=MULT, op1=ADD
                    )
                elif k in SCALAR_SQUARES:
                    nc.vector.tensor_scalar_mul(out=damp[n][:, t, :], in0=root_t, scalar1=margin_t)
                else:
                    nc.vector.scalar_tensor_tensor(
                        out=damp[n][:, t, :], in0=root_t, scalar=margin_t, in1=root_t, op0=MULT, op1=MULT
                    )

        def affinity_sums(n, c, where):
            j0, width, b = BLOCKS[n]
            sums[n, c] = bank(where, [P, PACK, P], f"a{n}{c}")
            for t in range(PACK):
                table_product(sums[n, c][:, t, :], AFF, b, t, j0 + c * P, P)

        def affinity(n, c):
            nc.vector.tensor_tensor(
                out=h_bf[n][:, c * HALF : (c + 1) * HALF].rearrange("p (k i t) -> p k t i", i=2, t=PACK),
                in0=sums[n, c][:].rearrange("p t (k i) -> p k t i", i=2),
                in1=damp[n][:, :, c * P : (c + 1) * P].rearrange("p t (k i) -> p k t i", i=2),
                op=MULT,
            )

        h_words = [kept([P, S2], U32, f"h_words{b}") for b in range(2)]
        h_scales = [kept([P, S2], U8, f"h_scales{b}") for b in range(2)]
        wc_words = [kept([P, N], U32, f"wc_words{b}") for b in range(2)]
        wc_scales = [kept([P, N], U8, f"wc_scales{b}") for b in range(2)]

        def quantise_h(b, j0, rounded):
            cols = slice(j0, j0 + rounded.shape[1] // PACK)
            nc.vector.quantize_mx(out=h_words[b][:, cols].bitcast(FP8X4), scales=h_scales[b][:, cols], in_=rounded)

        def quantise_wc(b, n0, rounded):
            cols = slice(n0, n0 + rounded.shape[1] // PACK)
            nc.vector.quantize_mx(out=wc_words[b][:, cols].bitcast(FP8X4), scales=wc_scales[b][:, cols], in_=rounded)

        def round_wc_scalar(rounded, raw):
            nc.scalar.copy(
                out=rounded.rearrange("p (k i t) -> p k t i", i=4, t=PACK),
                in_=raw.rearrange("p t (k i) -> p k t i", i=4),
            )

        def round_wc_gpsimd(rounded, raw):
            nc.gpsimd.tensor_scalar(
                out=rounded.rearrange("p (n t) -> p n t", t=PACK),
                in0=raw.rearrange("p t n -> p n t"),
                scalar1=1.0, scalar2=0.0, op0=MULT, op1=ADD,
            )

        acc = {}

        def open_part(part, where):
            j0, width, lo, hi = part
            acc[part] = bank(where, [P, hi - lo, width], f"acc{j0}_{lo}")

        def brands(part, terms, opens=False, closes=False):
            j0, width, lo, hi = part
            cols = slice(j0, j0 + width)
            steps = [(nt, kind, b) for nt in range(lo, hi) for kind, b in terms]
            for m, (nt, kind, b) in enumerate(steps):
                tile = slice(nt * P, (nt + 1) * P)
                if kind == BASE:
                    codes = weights["words"][:, b, 2 * nt * P : 2 * (nt + 1) * P].bitcast(FP4X4)
                    scales = weights["scales"][:, b, tile]
                else:
                    codes = wc_words[b][:, tile].bitcast(FP8X4)
                    scales = wc_scales[b][:, tile]
                nc.tensor.matmul_mx(
                    out=acc[part][:, nt - lo, :],
                    lhsT=codes,
                    lhsT_scale=scales,
                    rhs=h_words[b][:, cols].bitcast(FP8X4),
                    rhs_scale=h_scales[b][:, cols],
                    start=opens and m == 0,
                    stop=closes and m == len(steps) - 1,
                )

        def store(part, copy, queue=nc.sync, tag=""):
            j0, width, lo, hi = part
            staged = kept([P, hi - lo, width], F32, f"staged{j0}_{lo}", tag=tag)
            copy(out=staged[:], in_=acc[part][:])
            queue.dma_start(
                out=out[lo * P : hi * P, j0 : j0 + width].rearrange("(nt p) j -> p nt j", p=P), in_=staged[:]
            )

        wide = [(0, HALF, nt, nt + 1) for nt in range(4)]
        middle = [(HALF, GROUP, 0, 2), (HALF, GROUP, 2, 4)]
        last = [(768, P, 0, 4), (896, P, 0, 3), (896, P, 3, 4)]
        both = [[(BASE, b), (CAMPAIGN, b)] for b in range(2)]

        nc.sync.dma_start(idx[:], offs)
        load_prod_scales()
        nc.sync.dma_start(idx2[:], offs2)
        load_words(shop_words[FAT], tab2_words[FAT])
        load_shop_scales()
        load_margins()
        load_words(prod_words[FAT], tab_words[FAT])
        gather(listed_scales[:], prod_scales[:], idx[:])
        order_prod_scales(0)
        order_prod_scales(1)
        move_prod_scales()
        load_base_words()
        pick_shop_words(FAT, 0, S2)
        shop_words[AFF] = placed([P, T2], U32, "shop_affinity", 36)[:]
        load_words(shop_words[AFF], tab2_words[AFF])
        pick_shop_scales(0, S2)
        prod_words[AFF] = placed([P, T], U32, "prod_affinity", 8)[:]
        load_words(prod_words[AFF], tab_words[AFF])
        pick_prod_words(FAT, 0)
        pick_prod_words(FAT, 1)
        for k in (0, 1, 8):
            fatigue_sums(k)
        for k in (0, 2):
            square(k)
            square(k + 1)
            root(k, placed([P, HALF], F32, f"roots{k}", 47 if k == 0 else 0))
            root(k + 1, placed([P, HALF], F32, f"roots{k + 1}", 68 if k == 0 else 54))
        pick_shop_words(AFF, 0, S2)
        wc_raw = [placed([P, PACK, FIRST], F32, "wc_first", 43)]
        load_wc(wc_raw[0][:], 0, 0, FIRST)
        load_base_scales()
        damp[0] = placed([P, PACK, HALF], F32, "damp0", 33)
        for k in range(4):
            weigh(k)
        wc_raw.append(placed([P, PACK, FIRST], F32, "wc_second", 46))
        wc_raw.append(placed([P, PACK, GROUP], F32, "wc_third", 48))
        wc_raw.append(placed([P, PACK, SHARE], F32, "wc_fourth", 69))
        wc_raw.append(placed([P, PACK, N - SHARE], F32, "wc_fifth", 0))
        load_wc(wc_raw[1][:], 0, FIRST, GROUP)
        load_wc(wc_raw[2][:], 0, GROUP, N)
        load_wc(wc_raw[3][:], 1, 0, SHARE)
        load_wc(wc_raw[4][:], 1, SHARE, N)
        square(4)
        square(5)
        root(4, placed([P, HALF], F32, "roots4", 62))
        pick_prod_words(AFF, 0)
        pick_prod_words(AFF, 1)
        for c in range(4):
            affinity_sums(0, c, 2 + c)
        square(6)
        rounded = placed([P, 10 * HALF], BF16, "rounded", 52)
        wc_bf = [rounded[:, 2 * HALF : 6 * HALF], rounded[:, 6 * HALF :]]
        round_wc_gpsimd(wc_bf[0][:, : FIRST * PACK], wc_raw[0][:])
        round_wc_gpsimd(wc_bf[0][:, FIRST * PACK : GROUP * PACK], wc_raw[1][:])
        round_wc_gpsimd(wc_bf[0][:, GROUP * PACK :], wc_raw[2][:])
        root(5, placed([P, HALF], F32, "roots5", 64))
        square(7)
        root(6, placed([P, HALF], F32, "roots6", 66))
        square(8)
        for c, where in enumerate((7, 0, 1)):
            affinity_sums(1, c, where)
        for n in (0, 3, 4, 5):
            h_bf[n] = kept([P, BLOCKS[n][1] * PACK], BF16, f"h_bf{n}")[:]
        square_root(6)
        root(7)
        for c in range(4):
            affinity(0, c)
            if c < 2:
                fatigue_sums(9 + c)
        square(9)
        square_root(7, rounded[:, 7 * HALF : 9 * HALF].bitcast(F32))
        root(8)
        late = placed([P, 10 * HALF + P], F32, "late", 20.5)
        damp[1] = late[:, 6 * HALF + P :].rearrange("p (t j) -> p t j", t=PACK)
        for n in range(2, 6):
            damp[n] = late[:, (10 - 2 * n) * HALF + P : (12 - 2 * n) * HALF + P].rearrange("p (t j) -> p t j", t=PACK)
        quantise_h(0, 0, h_bf[0][:, : GROUP * PACK])
        weigh(4)
        quantise_h(0, GROUP, h_bf[0][:, GROUP * PACK :])
        for nt in range(3):
            open_part(wide[nt], 4 + nt)
            brands(wide[nt], [(BASE, 0)], opens=True)
        square(10, placed([P, HALF], F32, "squared10", 62))
        root(9, late[:, 4 * HALF : 5 * HALF])
        for k in range(5, 8):
            weigh(k)
        quantise_wc(0, 0, wc_bf[0][:, : GROUP * PACK])
        for nt in range(2):
            brands(wide[nt], [(CAMPAIGN, 0)])
        square(11, placed([P, HALF], F32, "squared11", 64))
        root(10)
        round_wc_gpsimd(wc_bf[1][:, : SHARE * PACK], wc_raw[3][:])
        h_bf[1] = rounded[:, : HALF * PACK]
        affinity(1, 0)
        affinity_sums(1, 3, 7)
        affinity(1, 1)
        square(12, placed([P, HALF], F32, "squared12", 66))
        round_wc_scalar(wc_bf[1][:, SHARE * PACK :], wc_raw[4][:])
        square_root(10, placed([P, HALF], F32, "squared_roots10", 69))
        affinity_sums(2, 0, 0)
        affinity(1, 2)
        affinity_sums(2, 1, 1)
        affinity(1, 3)
        square(13, placed([P, HALF], F32, "squared13", 0))
        root(11, late[:, 2 * HALF : 3 * HALF])
        quantise_h(1, 0, h_bf[1][:, : GROUP * PACK])
        open_part(wide[3], 7)
        brands(wide[3], [(BASE, 0)], opens=True)
        weigh(8, 0)
        quantise_h(1, GROUP, h_bf[1][:, GROUP * PACK :])
        weigh(8, 1)
        for nt in range(4):
            brands(wide[nt], [(BASE, 1)])
        weigh(9)
        quantise_wc(0, GROUP, wc_bf[0][:, GROUP * PACK :])
        for nt in range(2, 4):
            brands(wide[nt], [(CAMPAIGN, 0)])
        h_bf[2] = rounded[:, 3 * HALF : 5 * HALF]
        root(12, placed([P, HALF], F32, "roots12", 2))
        square(14)
        square_root(12)
        root(13, late[:, :HALF])
        root(14)
        square(15)
        square_root(14)
        root(15)
        square_root(15)
        for n in (2, 3, 4):
            j0, width, half = BLOCKS[n]
            weigh(2 * n + 6)
            for c in range(2):
                affinity(n, c)
                affinity_sums(n + 1, c, c)
            if n == 2:
                quantise_wc(1, 0, wc_bf[1])
                for nt in range(4):
                    brands(wide[nt], [(CAMPAIGN, 1)], closes=True)
            if n == 4:
                weigh(15, 0)
                quantise_h(half, j0, h_bf[n][:, :HALF])
                weigh(15, 1)
                quantise_h(half, j0 + P, h_bf[n][:, HALF:])
            else:
                weigh(2 * n + 7)
                quantise_h(half, j0, h_bf[n])
                for c in range(2):
                    if n == 2:
                        open_part(middle[c], 3 - c)
                    brands(middle[c], both[half], opens=n == 2, closes=n == 3)
        for nt in range(4):
            store(wide[nt], nc.scalar.copy)
        for part, where in zip(last, (4, 5, 6)):
            open_part(part, where)
            brands(part, both[0], opens=True)
        for c in range(2):
            affinity(5, c)
        store(middle[0], nc.scalar.copy)
        quantise_h(1, 3 * GROUP, h_bf[5][:, :HALF])
        brands(last[0], both[1], closes=True)
        quantise_h(1, 3 * GROUP + P, h_bf[5][:, HALF:])
        store(middle[1], nc.vector.tensor_copy, tag="h_bf5")
        store(last[0], nc.vector.tensor_copy)
        brands(last[1], both[1], closes=True)
        brands(last[2], both[1], closes=True)
        store(last[1], nc.scalar.copy, nc.scalar)
        store(last[2], nc.vector.tensor_copy)
